import numpy as np, ml_dtypes
CORES = [40,42,43,45,46]
N = 5
BF = ml_dtypes.bfloat16
H, H0, L, CAP, S, JS, T = 4096, 3072, 1024, 64, 2, 5, 3
TB = 4 * 2 ** JS
def edges(rng, late=False):
    nt = H // TB; m = H0 // TB; half = (m // 2) * TB; w = np.arange(H) // TB
    t = rng.integers(0, nt, (N, 8, nt))
    if late: t[:, :, :m // 2] = rng.integers(0, m, (N, 8, m // 2))
    base = t[:, :, w] * TB
    x = base + rng.integers(0, TB, (N, 8, H)); y = base + rng.integers(0, TB, (N, 8, H))
    odd = rng.random((N, 8, H)) < 0.1
    if late: odd = odd & (np.arange(H) >= half)
    return x, np.where(odd, rng.integers(0, H, (N, 8, H)), y)
def packets(rng, alive, pb):
    on = rng.random((N, 8, L)) < alive; j = rng.integers(0, 16, (N, 8, 1, L))
    live = on[:, :, None] & ((rng.random((N, 8, 16, L)) < np.broadcast_to(pb, (N, 8, L))[:, :, None]) | (np.arange(16)[:, None] == j))
    a = (1 + 0.5 * rng.random((N, 8, 16, L))) * (1 - 2 * rng.integers(0, 2, (N, 8, 16, L)))
    q = rng.choice(np.array([0.0, 0.15, 0.5, 0.5, 0.85, 1.0]), (N, 8, 1, L))
    c = rng.random((N, 8, 16, L)) * np.where(rng.random((N, 8, 16, L)) < q, 1.0, -1.0)
    return live, a, c, rng.integers(0, H, (N, 8, L))
def pack(rng, live, a, c, h, x, y, kap=None, dam=None):
    if kap is None: kap = 0.5 + 0.5 * rng.random((N, 128, H), dtype=np.float32)
    if dam is None: dam = 1.5 + 2.5 * rng.random((N, 128, H), dtype=np.float32)
    c = np.where(np.abs(c) < 2.0 ** -20, 0.0 * c, c)
    return {"kap": kap.astype(BF), "dam": dam.astype(BF), "lf": x.astype(np.int32), "rt": y.astype(np.int32), "place": h.astype(np.int32),
            "cro": c.reshape(N, 128, L).astype(BF), "amp": np.where(live, np.abs(a), 0.0 * a).reshape(N, 128, L).astype(BF)}
def ends(rng, v, share):
    return np.where(rng.random(v.shape) < share, (H - 1) * rng.integers(0, 2, v.shape), v)
def setup_inputs(rng):
    x, y = edges(rng)
    alive = rng.permuted(np.tile(np.array([0.08, 0.12, 0.2, 0.25, 0.35, 0.45, 0.5, 0.6]), (N, 1)), axis=1)[:, :, None]
    live, a, c, h = packets(rng, alive, rng.choice(np.array([0.5, 0.8, 1.0]), (N, 8, L)))
    return pack(rng, live, a, c, h, x, y)
def setup_inputs_calm(rng):
    x, y = edges(rng); live, a, c, h = packets(rng, 0.6, 0.9); o = int(rng.integers(0, 8))
    for r in range(N):
        for k in range(5):
            g = (o + k) % 8
            x[r, g] = np.where(rng.random(H) < 0.002, rng.integers(H0, H, H), x[r, g] % H0); y[r, g] = np.where(rng.random(H) < 0.002, rng.integers(H0, H, H), y[r, g] % H0)
            live[r, g] = np.arange(16)[:, None] == rng.integers(0, 16, L)
            p = rng.permutation(L); h[r, g] = rng.integers(0, H0, L)
            two = p[:4]; live[r, g][:, two] = False
            for l in two:
                b = rng.permutation(16)[:2]; live[r, g, b, l] = True; c[r, g, b[0], l] = 0.5; c[r, g, b[1], l] = -0.5
            nd = (r + k) % 4; h[r, g, p[4:4 + nd]] = rng.integers(H0, H, nd)
            nf = (k + 2 * r + 1) % 4; live[r, g][:, p[8:8 + nf]] = False
    return pack(rng, live, a, c, h, x, y)
def setup_inputs_corners(rng):
    x, y = edges(rng, True); live, a, c, h = packets(rng, 1.0, 0.9); half = (H0 // TB // 2) * TB; n2 = (H - H0) // 2
    g0 = int(rng.integers(0, 8)); cell = {}
    for j in range(4):
        g = (g0 + (0, 4, 2, 6)[j]) % 8
        cell[0, g] = ((L - 2 * CAP, L - 2 * CAP + 1, (L - 2 * CAP) // 2, 0)[j], 0, 0)
        cell[N - 1, g] = (L // 2, (CAP + 1, L // 2, L // 2, 0)[j], 0)
        cell[N - S, (g - 1) % 8] = (L // 2, (CAP + 2, L // 2, L // 2, 0)[j], 1)
    for r in range(N):
        for g in range(8):
            n = (0, 1, L, L - 1, L - 2, L - 3, L // 2, L // 4)[(r + g) % 8]; v = (3 * r + g) % 8
            k = min(n, (CAP, CAP + 1, 1, 0, L, CAP - 1, 2, 3)[v]); odd = {0: 0, 1: 0, 5: 1}.get(v)
            if (r, g) in cell: n, k, odd = cell[r, g]
            p = rng.permutation(L)[:n] if n != 1 else np.array([L - 1])
            keep = np.zeros(L, bool); keep[p] = True; live[r, g] &= keep
            if (r, g) in cell and k == 0: live[r, g] = keep & (np.arange(16)[:, None] == rng.integers(0, 16, L))
            h[r, g] = rng.integers(0, half, L)
            par = rng.integers(0, 2, k) if odd is None else np.full(k, odd)
            h[r, g, p[:k]] = H0 + 2 * rng.integers(0, n2, k) + par
    g = (g0 + 2) % 8; o = rng.permutation(half); p, s, u = int(o[0]), int(o[1]), int(o[2])
    x[0, g, p] = s; x[0, g, s] = u; y[0, g, s] = (u + 2 ** JS) % half
    l = np.flatnonzero(np.any(live[0, g], axis=0)); b = rng.integers(0, 16, len(l)); b2 = (b + rng.integers(1, 16, len(l))) % 16
    live[0, g] = False; live[0, g, b, l] = True; live[0, g, b2, l] = True; h[0, g] = p
    c[0, g, b, l] = 1.0; c[0, g, b2, l] = 0.125 + 0.25 * rng.random(len(l))
    g = (g0 + 6) % 8
    for r, k, odd in ((N - 1, g, 0), (N - S, (g - 1) % 8, 1)):
        o = rng.permutation(half); p, s = int(o[0]), int(o[1]); door = H0 + 2 * int(rng.integers(0, n2)) + odd
        h[r, k] = p; x[r, k, p] = s; y[r, k, p] = s; x[r, k, s] = door; y[r, k, s] = door
    return pack(rng, live, a, c, h, x, y)
def setup_inputs_crowd(rng):
    x, y = edges(rng); live, a, c, h = packets(rng, 0.5, 1.0); i = (np.arange(16)[:, None] + np.arange(L)) % 16
    for r in range(N):
        for g in range(8):
            u = (r + g) % 8
            if u == 7: continue
            p = int(rng.integers(0, H0)); door = int(rng.integers(H0, H))
            h[r, g] = door if u in (3, 4) else p
            if u in (0, 1, 3, 4): live[r, g] = True
            if u in (1, 4): live[r, g][:, int(rng.integers(0, L))] = False
            if u == 4: h[r, g, int(rng.integers(0, L))] = p
            left = (16, 15, 8, 16, 1, 8, 7)[u]
            c[r, g] = np.abs(c[r, g]) * np.where(i < left, 1.0, -1.0)
            j = int(rng.integers(0, H0 // TB)) * TB
            if u in (0, 1, 2, 5, 6): x[r, g, p] = j; y[r, g, p] = j + (2 ** JS - 1 if u == 2 else 2 ** JS)
    g = int(rng.integers(0, 8)); e = 2 * int(rng.integers(0, (H - H0) // 2)); o = rng.permutation(H0); p = int(o[0]); s = int(o[1])
    live[N - 1, g] = True; h[N - 1, g] = H0 + e
    m = (e >> JS << JS) + rng.integers(0, 2 ** JS, 2)
    x[0, g, p] = s; y[0, g, p] = int(rng.integers(H0, H)); x[0, g, s] = m[0]; y[0, g, s] = m[1]
    l = rng.permutation(L)[:CAP]; b = rng.integers(0, 16, CAP); b2 = (b + rng.integers(1, 16, CAP)) % 16
    live[0, g] = False; live[0, g, b, l] = True; live[0, g, b2, l] = True; h[0, g] = p
    c[0, g, b, l] = 0.25 + 0.5 * rng.random(CAP); c[0, g, b2, l] = -0.25 - 0.5 * rng.random(CAP)
    return pack(rng, live, a, c, h, x, y)
def setup_inputs_ends(rng):
    x, y = edges(rng); x = ends(rng, x, 0.8); y = ends(rng, y, 0.8); k = (np.arange(N)[:, None] + np.arange(8)) % 4
    x[:, :, 0] = np.array([0, H - 1, 0, H0 - 1])[k]; y[:, :, 0] = np.array([H - 1, 0, 0, H - 1])[k]
    x[:, :, H - H0 - 1] = 0; y[:, :, H - H0 - 1] = H - 1; x[:, :, H - 1] = 0; y[:, :, H - 1] = H - 1
    live, a, c, h = packets(rng, 0.5, rng.integers(0, 2, (N, 8, L)).astype(np.float64)); h = ends(rng, h, 0.8)
    big = rng.random(a.shape) < rng.choice(np.array([0.0, 0.5, 1.0]), (N, 8, 1, L))
    a = np.where(a < 0, -1.0, 1.0) * np.where(big, 4.0, 0.25)
    e = rng.choice(np.array([-1.0, -2.0 ** -20, -0.0, 0.0, 2.0 ** -20, 1.0]), c.shape); c = np.where(rng.random(c.shape) < 0.7, e, c)
    h[:, :, 0] = 0; h[:, :, L - 1] = H - 1; h[N - 1, 7, L - 1] = 0; h[0, :4, L - 1] = 0
    tie = np.where(np.arange(16) < 8, 2.0 ** -20, -2.0 ** -20)
    for l in (0, L - 1): live[:, :, :, l] = True; c[:, :, :, l] = tie
    return pack(rng, live, a, c, h, x, y, np.where(rng.random((N, 128, H)) < 0.5, 0.5, 1.0), np.where(rng.random((N, 128, H)) < 0.25, 0.0, 4.0))
def setup_inputs_spread(rng):
    x, y = edges(rng); live, a, c, h = packets(rng, 0.5, 0.95)
    a = a * np.exp2(rng.integers(-1, 2, (N, 8, 1, L))); h = np.minimum((H * rng.random((N, 8, L)) ** 2).astype(np.int64), H - 1)
    low = rng.random((N, 1, H)) < 0.25
    dam = np.where(low, 1.4 * rng.random((N, 1, H)), 1.5 + 2 * rng.random((N, 1, H))) + 0.5 * rng.random((N, 128, H))
    kap = 0.5 + 0.5 * rng.random((N, 128, H), dtype=np.float32); i = np.arange(16) % 2
    for r in range(N):
        g = int(rng.integers(0, 8)); o = rng.permutation(H0); p, s, v = int(o[0]), int(o[1]), int(o[2]); l = rng.permutation(L)[:32]
        kap[r, 16 * g:16 * g + 16, p] = np.where(i == 0, 155, 205) * 2.0 ** -8; kap[r, 16 * g:16 * g + 16, s] = 132 * 2.0 ** -8
        x[r, g, p] = s; y[r, g, s] = v; h[r, g, l] = p
        live[r, g][:, l] = True; c[r, g][:, l] = (np.where(i == 0, 205, 155) * 2.0 ** -13)[:, None]
    return pack(rng, live, a, c, h, x, y, kap, dam)
def check_ranges(d):
    bad = []
    for k, lo, hi in (("lf", 0, H - 1), ("rt", 0, H - 1), ("place", 0, H - 1), ("kap", 0.5, 1.0), ("dam", 0.0, 4.0)):
        v = np.asarray(d[k], np.float64)
        if not (np.min(v) >= lo and np.max(v) <= hi): bad.append("range of " + k)
    for k, lo, hi in (("cro", 2.0 ** -20, 1.0), ("amp", 0.25, 4.0)):
        v = np.asarray(d[k], np.float64)
        if k == "cro": v = np.abs(v)
        if not np.all((v == 0) | ((v >= lo) & (v <= hi))): bad.append("range of " + k)
    return bad
def at(t, ix):
    return np.take_along_axis(t, ix, t.ndim - 1)
def reference(kap, dam, lf, rt, place, cro, amp):
    kf = kap.astype(np.float32).reshape(N, 8, 16, H)
    sg = np.reciprocal(1.0 + np.exp(-dam.astype(np.float64))).reshape(N, 8, 16, H)
    xt = lf.astype(np.int64); yt = rt.astype(np.int64); h = place.astype(np.int64)
    a = amp.astype(np.float64).reshape(N, 8, 16, L); one = np.float32(1); nil = np.float32(0)
    c = np.where(a != 0, cro.astype(np.float32).reshape(N, 8, 16, L), nil)
    own = np.arange(L); tw = np.tile(own, (N, 8, 1)); box = {}
    for step in range(T):
        live = a != 0; on = np.any(live, axis=2); go = on & (h < H0); moves = live & go[:, :, None]
        k = at(kf, h[:, :, None]) * c
        left = moves & (k >= 0); right = moves & (k < 0); k = np.float32(2) * k
        c = np.where(left, k - one, np.where(right, k + one, c))
        xl = at(xt, h); xr = at(yt, h)
        a = np.where(left, a * at(sg, xl[:, :, None]), np.where(right, a * at(sg, xr[:, :, None]), a))
        lw = np.sum(left, axis=2) >= np.sum(right, axis=2)
        out = np.where(lw[:, :, None], right, left); dis = np.any(out, axis=2)
        h = np.where(go, np.where(lw, xl, xr), h); other = np.where(lw, xr, xl)
        da = np.where(out, a, 0.0); dc = np.where(out, c, nil)
        a = np.where(out, 0.0, a); c = np.where(out, nil, c)
        for r in range(N):
            for g in range(8):
                w = np.flatnonzero(~on[r, g]); d = np.flatnonzero(dis[r, g])
                nh = [other[r, g, d]]; na = [da[r, g][:, d]]; nc = [dc[r, g][:, d]]; m = 0
                if step > 0:
                    e0, a0, c0 = box[(r - 1) % N, g]; e1, a1, c1 = box[(r - S) % N, (g - 1) % 8]
                    i0 = e0 % 2 == 0; i1 = e1 % 2 == 1
                    nh = [e0[i0], e1[i1]] + nh; na = [a0[:, i0], a1[:, i1]] + na; nc = [c0[:, i0], c1[:, i1]] + nc
                    m = len(nh[0]) + len(nh[1])
                nh = np.concatenate(nh); na = np.concatenate(na, axis=1); nc = np.concatenate(nc, axis=1)
                n = min(len(w), len(nh)); w = w[:n]
                h[r, g, w] = nh[:n]; a[r, g][:, w] = na[:, :n]; c[r, g][:, w] = nc[:, :n]
                tw[r, g, w[:m]] = w[:m]; born = w[m:]; par = d[:len(born)]
                tw[r, g, born] = par; tw[r, g, par] = born
        on = np.any(a != 0, axis=2)
        f = on & at(on, tw) & (at(tw, tw) == own) & (tw != own) & ((h >> JS) == (at(h, tw) >> JS))
        lo = (f & (own < tw))[:, :, None]; up = (f & (own > tw))[:, :, None]; ix = tw[:, :, None]
        a = np.where(lo, a + at(a, ix), np.where(up, 0.0, a)); c = np.where(lo, c + at(c, ix), np.where(up, nil, c))
        if step < T - 1:
            on = np.any(a != 0, axis=2)
            for r in range(N):
                for g in range(8):
                    e = np.flatnonzero(on[r, g] & (h[r, g] >= H0))[:CAP]
                    box[r, g] = (h[r, g, e] - H0, a[r, g][:, e], c[r, g][:, e])
                    a[r, g][:, e] = 0.0; c[r, g][:, e] = nil
    y = a * at(kf, h[:, :, None])
    return {"ya": y.reshape(N, 128, L).astype(np.float32), "yc": c.reshape(N, 128, L).astype(np.float32)}

def check_inputs(d):
    bad = list(check_ranges(d))
    if not bad:
        for name, y in reference(**d).items():
            for q in range(N):
                v = np.abs(np.asarray(y[q], np.float64)); s = np.sqrt(np.mean(v * v))
                if v.max() > 7 * s or s < 2.0 ** -4: bad.append('%s of rank %d is uneven or too small' % (name, q))
    return bad

@@ -1,0 +1,636 @@
+from concourse.bass import DstId, RemoteDMATransfer
+from concourse.mybir import AluOpType as OP, ActivationFunctionType as AF
+
+H, H0, L, CAP, STEPS = 4096, 3072, 1024, 64, 3
+ZC = 3072
+A0 = ZC + 8
+WW = A0 + 256
+F, B, I, U, HF = "float32", "bfloat16", "int32", "uint16", "float16"
+CI = I
+SIZE = {F: 4, B: 2, I: 4, U: 2, HF: 2}
+POOL = {F: ("pf", 11200), B: ("pb", 5800), I: ("pi", 2200), U: ("pu", 1024), HF: ("ph", 1000)}
+SCRATCH = {
+    "kp": ("sbuf", [128, H], B), "dm": ("sbuf", [128, H], B), "sg": ("sbuf", [128, H], F), "ex": ("sbuf", [128, H], B),
+    "wc0": ("sbuf", [128, WW], F), "wc1": ("sbuf", [128, WW], F), "wa0": ("sbuf", [128, WW], F), "wa1": ("sbuf", [128, WW], F),
+    "zz": ("sbuf", [128, L + WW], F), "mm": ("sbuf", [128, L], B),
+    "kk": ("sbuf", [128, L], F), "c1": ("sbuf", [128, L], F), "a1": ("sbuf", [128, L], F), "ss": ("sbuf", [128, L], F),
+    "ns": ("sbuf", [128, L], F), "mr": ("sbuf", [128, L], B), "nl": ("sbuf", [128, L], B), "eg": ("sbuf", [128, L], B),
+    "g2": ("sbuf", [128, L], HF), "cb": ("sbuf", [128, L], B), "ab": ("sbuf", [128, L], B),
+    "sn": ("sbuf", [128, L], B), "p8": ("sbuf", [128, L], I), "p8h": ("sbuf", [128, L], HF),
+}
+for _d, (_n, _w) in POOL.items():
+    SCRATCH[_n] = ("sbuf", [128, _w], _d)
+for _n in ("qs0", "qs1", "qr0", "qr1", "qa", "qb", "qc", "qd"):
+    SCRATCH[_n] = ("psum", [128, 512], F)
+SEMAPHORES = ["eV", "eA", "eP", "eG"] + ["d%d" % k for k in range(60)] + ["rv0", "rv1", "rd0", "rd1", "rc0", "rc1"]
+
+CY, FAC, GA, SC, PEC, HOP, BIAS = 0.00083, 1.25, 1.55, 3.8, 0.00042, 0.08, 0.3
+PIECES, LAST, TRIES = 2, 2, 100
+SILU = True
+EPS = 2.0 ** -40
+OFF = 6144.0
+
+
+def build(T, topo, core):
+    ops, hist, lay, top, nsem = [], {}, {}, {}, [0]
+
+    def V(name, a=0, n=None, p=None, step=1):
+        t = T[name]
+        n = t.shape[1] - a if n is None else n
+        cs = slice(a, a + n) if step == 1 else slice(a, a + n, step)
+        pm = sum(1 << j for j in range(128)[slice(None) if p is None else p])
+        return (name, a, n, t[(slice(None) if p is None else p), cs], pm, step, (n + step - 1) // step)
+
+    def sub(v, a, n, p=None):
+        return V(v[0], v[1] + a * v[5], (n - 1) * v[5] + 1, p, v[5])
+
+    def every(v, a, step, n):
+        return V(v[0], v[1] + a, (n - 1) * step + 1, None, step)
+
+    def S(name, dt=F, n=64):
+        if name not in lay:
+            w = (n + 15) // 16 * 16 if n > 1 else 8
+            o = top.get(dt, 0)
+            o = (o + 15) // 16 * 16 if n > 1 else o
+            top[dt] = o + w
+            assert top[dt] <= POOL[dt][1], (dt, top[dt])
+            lay[name] = V(POOL[dt][0], o, n)
+        return lay[name]
+
+    def C(name):
+        return S(name, F, 1)
+
+    def psum(v):
+        return SCRATCH.get(v[0], ("dram",))[0] == "psum"
+
+    def meet(v, u):
+        if not (v[1] < u[1] + u[2] and u[1] < v[1] + v[2] and v[4] & u[4]):
+            return False
+        return not (v[5] == u[5] and (v[1] - u[1]) % v[5])
+
+    def add(alts, rd, wr, lat=0.0, sem=None, after=()):
+        k = len(ops)
+        deps = {}
+        use = [(x, False) for x in rd if x[0] in SCRATCH] + [(x, True) for x in wr if x[0] in SCRATCH]
+        for v, w in use:
+            ps = psum(v)
+            for u, w2, k2 in hist.get(v[0], ()):
+                if (w or w2) and (ps or meet(v, u)):
+                    deps[k2] = True
+                elif ps:
+                    deps.setdefault(k2, False)
+        for v, w in use:
+            hs = hist.setdefault(v[0], [])
+            if w and psum(v):
+                hs[:] = [e for e in hs if e[2] == k]
+            elif w:
+                hs[:] = [e for e in hs if not (v[1] <= e[0][1] and e[0][1] + e[0][2] <= v[1] + v[2] and e[0][4] & ~v[4] == 0
+                                               and (v[5] == 1 or (v[5] == e[0][5] and (v[1] - e[0][1]) % v[5] == 0)))]
+            hs.append((v, w, k))
+        ops.append({"alts": alts, "deps": deps, "lat": lat, "sem": sem, "after": list(after),
+                    "nm": ([n for n, x in lay.items() if wr and meet(x, wr[0]) and x[0] == wr[0][0]] + [x[0] for x in wr] + ["-"])[0]})
+        return k
+
+    def isv(x):
+        return isinstance(x, tuple)
+
+    def ap(x):
+        return x[3] if isv(x) else x
+
+    def tv(n, c=1.0):
+        return (0.04 + max(64.0, n * c) * CY) * FAC
+
+    def two(*vs):
+        return all(SIZE[SCRATCH[v[0]][2]] == 2 for v in vs)
+
+    def ts(o, x, s1, op0, s2=None, op1=None):
+        a = (o[3], x[3], ap(s1), ap(s2), op0) + (() if op1 is None else (op1,))
+        add({"V": (tv(o[6], 0.5 if two(o, x) else 1), lambda q: q.tensor_scalar(*a))}, [x] + [s for s in (s1, s2) if isv(s)], [o])
+        return o
+
+    def tt(o, x, y, op):
+        add({"V": (tv(o[6], 1 if psum(x) or psum(y) else 2), lambda q: q.tensor_tensor(o[3], x[3], y[3], op))}, [x, y], [o])
+        return o
+
+    def act(o, x, fn, scale=1.0, bias=0.0, acc=None, off=None, alt=None, extra=0.0):
+        xi = x[3] if off is None else x[3].indirect(off[3])
+        kw = {} if acc is None else {"accum_out": acc[3]}
+        if not (fn == AF.Copy or (not isv(bias) and bias == 0.0)):
+            kw["bias"] = ap(bias)
+        if isv(scale) or scale != 1.0:
+            kw["scale"] = ap(scale)
+        alts = {"A": (tv(o[6], GA if off else 1) + 0.03 + extra, lambda q: q.activation(o[3], xi, fn, **kw))}
+        if alt:
+            alts["V"] = alt
+        add(alts, [x] + [s for s in (scale, bias, off) if isv(s)], [o] + ([acc] if acc else []))
+        return o
+
+    def aff(o, x, mul, plus):
+        return act(o, x, AF.Identity, mul, plus,
+                   alt=(tv(o[6]), lambda q: q.tensor_scalar(o[3], x[3], ap(mul), ap(plus), OP.mult, OP.add)))
+
+    def cp(o, x, both=False):
+        v = (tv(o[6], 0.5 if two(o, x) else 1), lambda q: q.tensor_copy(o[3], x[3]))
+        if both:
+            return act(o, x, AF.Copy, alt=v)
+        add({"V": v}, [x], [o])
+        return o
+
+    def gat(o, win, off):
+        return act(o, win, AF.Copy, off=off, alt=(tv(o[6], GA), lambda q: q.tensor_copy(o[3], win[3].indirect(off[3]))))
+
+    def gtt(o, win, off, y, op):
+        add({"V": (tv(o[6], GA), lambda q: q.tensor_tensor(o[3], win[3].indirect(off[3]), y[3], op))}, [win, off, y], [o])
+
+    def scat(win, off, x, silu=False, extra=0.0):
+        if silu:
+            add({"A": (tv(x[6], SC) + extra, lambda q: q.activation(win[3].indirect(off[3]), x[3], AF.Silu))}, [off, x, sg], [win])
+        else:
+            add({"V": (tv(x[6], SC), lambda q: q.tensor_copy(win[3].indirect(off[3]), x[3]))}, [off, x], [win])
+
+    def mset(o, c):
+        add({"V": (tv(o[6], 0.5 if two(o) else 1), lambda q: q.memset(o[3], c))}, [], [o])
+        return o
+
+    def scan(o, d0, d1):
+        add({"V": (tv(o[6], 0.5 if two(o, d0, d1) else 1), lambda q: q.tensor_tensor_scan(o[3], d0[3], d1[3], 0.0, OP.mult, OP.add))}, [d0, d1], [o])
+
+    def chain(name, n, t0=F, t1=F, t2=F, w=64):
+        name = "chain" + name
+        new = name + "0" not in lay
+        d0, d1, o = S(name + "0", t0, n * w), S(name + "1", t1, n * w), S(name + "2", t2, n * w)
+        if new:
+            mset(d0, 0 if t0 == I else 0.0)
+        return [[every(x, j, n, w) for j in range(n)] for x in (d0, d1, o)] + [lambda: scan(o, d0, d1), new]
+
+    def iota(o, pat, base=0, cm=0):
+        kw = {} if SCRATCH[o[0]][2] == I else {"allow_small_or_imprecise_dtypes": True}
+        add({"G": (0.13 + 2 * o[6] * CY * FAC, lambda q: q.iota(o[3], pat, base, cm, **kw))}, [], [o])
+        return o
+
+    def mms(lst):
+        def emit(q):
+            r = None
+            for o, l, x, s0, s1 in lst:
+                r = q.matmul(o[3], l[3], x[3], s0, s1)
+            return r
+        add({"P": (0.05 + sum(max(64, m[0][6]) * PEC * FAC * (SIZE[SCRATCH[m[1][0]][2]] // 2) ** 2 + 0.01 for m in lst), emit)}, [v for m in lst for v in m[1:3]], [m[0] for m in lst])
+
+    def acc(o, terms):
+        return [(o, l, x, j == 0, j == len(terms) - 1) for j, (l, x) in enumerate(terms)]
+
+    def wrap(o, bm, x, n, first=True, last=True, p=None):
+        mms([(o, sub(bm, 15 - i, 128, p), V(x[0], x[1] + i, 16 * n - i, p, 16), first and i == 0, last and i == 15) for i in range(16)])
+        return o
+
+    def dma(eng, o, x, kb, acc=False):
+        s = "d%d" % nsem[0]
+        nsem[0] += 1
+        kw = {"accum_op": OP.add} if acc else {}
+        add({eng: (1.0 if eng == "G" else 0.1, lambda q: q.dma_start(ap(o), ap(x), **kw))},
+            [v for v in (x, o if acc else None) if isv(v)], [o] if isv(o) else [], lat=1.6 + kb / 600.0, sem=(s, 16))
+        ops[-1]["pipe"] = kb / 600.0
+
+    def send(items, rsem, land):
+        s = "d%d" % nsem[0]
+        nsem[0] += 1
+        trs, tot = [], 0
+        for j, (src, dst, to) in enumerate(items):
+            en = topo.engines(core, to)
+            w = len(en) // len(items)
+            m = sum(1 << e for e in en[j * w:(j + 1) * w])
+            rid, pid, _ = topo.addr(to)
+            trs.append(RemoteDMATransfer(dst_ids=[DstId(rid=rid, pnc=pid)], dma_engine_mask=m, remote_sem=T.sem[rsem], src=src[3], dst=dst[3]))
+            tot += w
+        k = add({"G": (1.0, lambda q: q.remote_dma_fused(trs, local_sem=T.sem[s]))}, [i[0] for i in items], [], lat=1.5, sem=(s, tot))
+        ops[k]["remote"] = True
+        add({}, [], land, lat=0.3, sem=(rsem, tot), after=[k])
+
+    rank, n = T.rank_of(core), len(T.cores)
+    to1, to2 = T.cores[(rank + 1) % n], T.cores[(rank + 2) % n]
+    kp, dm, sg, ex, zz, mm = V("kp"), V("dm"), V("sg"), V("ex"), V("zz"), V("mm")
+    kk, c1, a1, ss, ns, mr, nl, eg, g2, cb, ab = [V(x) for x in ("kk", "c1", "a1", "ss", "ns", "mr", "nl", "eg", "g2", "cb", "ab")]
+    wc, wa = [V("wc0"), V("wc1")], [V("wa0"), V("wa1")]
+    qs, qr = [V("qs0"), V("qs1")], [V("qr0"), V("qr1")]
+    P8 = slice(0, 8)
+    HV = [(0, 512), (512, 512)]
+    PV = [(j * L // PIECES, L // PIECES) for j in range(PIECES)]
+    mul, plus, minus = OP.mult, OP.add, OP.subtract
+
+    nat = S("nat", I, 512)
+    dma("A", sub(nat, 0, 256), T.lf[:], 128)
+    dma("S", sub(nat, 256, 256), T.rt[:], 128)
+    dma("S", ab, T.amp[:], 256)
+    dma("A", cb, T.cro[:], 256)
+    dma("S", V("p8", p=P8), T.place[:], 200)
+    dma("S", ex, T.kap[:], 1000)
+    dma("A", dm, T.dam[:], 1000)
+    dma("S", kp, T.kap[:], 1000)
+    for j, o in enumerate(ops):
+        o["first"] = 1000.0 - j
+
+    pi = iota(S("pi", I, 1), [[0, 1]], 0, 1)
+    io = iota(S("io", F, 256), [[1, 256]])
+    qg = iota(S("qg", F, 128), [[16, 8], [0, 16]])
+    l16 = iota(S("l16"), [[16, 64]])
+    dma("G", sub(wa[0], 2 * L, L), T.amp[:], 512)
+    dma("G", sub(zz, L, 2 * L), sub(dm, 0, 2 * L), 1000)
+    mset(mm, 0.0)
+    ic = cp(C("ic"), ts(S("ici", I, 1), pi, 15, OP.bitwise_and))
+    pc = cp(C("pc"), pi)
+    g16 = tt(C("g16"), pc, ic, minus)
+    g15 = aff(C("g15"), g16, 1.0, 15.0)
+    lid = aff(S("lid"), l16, 1.0, ic)
+    lid1 = aff(S("lid1"), lid, 1.0, 1024.0)
+    lidm = aff(S("lidm"), lid, 1.0, -1024.0)
+    lidx = aff(S("lidx"), lid, 1.0, 512.0 - ZC)
+    lc = aff(S("lc"), lid, -1.0, 4096.0)
+    jh = aff(S("jh", F, 4), sub(lid, 0, 4), 1.0, 0.5)
+    i144, i128, i16 = sub(io, 0, 144), sub(io, 0, 128), sub(io, 0, 16)
+    hi8 = ts(C("hi8"), ic, 8.0, OP.is_ge)
+    lo8 = aff(C("lo8"), hi8, -1.0, 1.0)
+    b1m = ts(S("b1m", B, 144), i144, g15, OP.is_equal)
+
+    def sel(name, w):
+        return aff(S(name, B, 144), b1m, w, 0.0)
+    bhm, bnm, bim = sel("bhm", 0.5), sel("bnm", -0.5), sel("bim", ic)
+    w4 = ts(C("w4"), ts(S("w4i", I, 1), pi, 3, OP.bitwise_and), 0.0, OP.is_equal)
+    wl, wr_ = aff(C("wl"), w4, lo8, 0.0), aff(C("wr"), w4, hi8, 0.0)
+    bxl, bxr = sel("bxl", wl), sel("bxr", wr_)
+    bdx = sel("bdx", aff(C("wdx"), wr_, 1.0, aff(C("wdx0"), w4, -0.5, 0.0)))
+    bsm = sel("bsm", aff(C("wsm"), w4, 0.5, 0.0))
+    bjq = sel("bjq", ts(C("wjq"), ic, 1.0, OP.is_equal))
+    bgm = sel("bgm", ts(C("wg0"), ic, 0.0, OP.is_equal))
+    bpm = ts(S("bpm", B, 144), i144, aff(C("p15"), pc, 16.0, 15.0), OP.is_equal)
+    ones = ts(S("ones", B, 128), qg, g16, OP.is_equal)
+    tri = tt(S("tri", B, 128), ts(S("tri0", B, 128), i128, pc, OP.is_le, -1.0, mul), ones, mul)
+    gn = tt(C("gn"), ts(C("gn0"), g16, 112.0, OP.is_ge, -128.0, mul), g16, plus)
+    osh = ts(S("osh", B, 128), qg, aff(C("gn2"), gn, 1.0, 16.0), OP.is_equal)
+    i8 = ts(S("i8", B, 144), i144, aff(C("p8c"), pc, 1.0, 8.0), OP.is_equal)
+    ilo, ihi = aff(S("ilo", B, 144), i8, lo8, 0.0), aff(S("ihi", B, 144), i8, hi8, 0.0)
+    idn = sub(i8, 8, 128)
+    id1, idk, i64 = [aff(S(x, B, 128), idn, w, 0.0) for x, w in (("id1", -1.0), ("idk", -2048.0), ("i65", 65.0))]
+    sn = V("sn")
+
+    def fid(w):
+        new = "fid%d" % w not in lay
+        o = S("fid%d" % w, F, 128)
+        return aff(o, idn, float(w), 0.0) if new else o
+    d16 = ts(S("d16", B, 16), i16, ic, OP.is_equal)
+    scat(mm, ts(S("mof", U, 1), aff(C("mo1"), hi8, -1023.0, aff(C("mo0"), ic, 128.0, g16)), 0.0, plus), d16)
+    rs = mset(S("rs", B, 195), 1.0)
+    mset(sub(rs, 65, 1), 0.0)
+    mset(sub(rs, 130, 1), 0.0)
+    seg = mset(S("seg", B, 195), 0.0)
+    w2 = mset(S("w2", F, 144), 0.0)
+    for w in (wc[1], wa[1]):
+        mset(sub(w, ZC, 8), 0.0)
+    for w in (wc[0], wa[0]):
+        mset(sub(w, ZC, 8 + 128), 0.0)
+    mset(sub(zz, L + ZC, 8), 0.0)
+
+    nd = ts(C("ndc"), ic, 12.0, OP.is_lt)
+    dc = aff(C("dcc"), nd, -1.0, 1.0)
+    did = aff(S("did", F, 256), io, dc, aff(C("i257"), aff(C("i256"), ic, 256.0, 0.0), dc, 0.0))
+    for j in range(2):
+        v = tt(S("nv%d" % j, F, 256), ts(S("nu", F, 256), sub(nat, 256 * j, 256), nd, mul, -2048.0, plus), did, plus)
+        hi = cp(S("nh%d" % j, B, 256), v, True)
+        lo = tt(S("nl%d" % j, B, 256), v, hi, minus)
+        dma("S", V("ex", p=slice(8 * j, 128, 16)), hi, 250)
+        dma("A", V("ex", p=slice(8 * j + 4, 128, 16)), lo, 250)
+    nj = ts(S("nj", I, 512), nat, 5, OP.arith_shift_right)
+    dma("S", V("ex", p=slice(1, 128, 16)), aff(S("njq", B, 256), tt(S("nje", B, 256), sub(nj, 0, 256), sub(nj, 256, 256), OP.is_equal), 1024.0, -512.0), 250)
+
+    p8h = ts(V("p8h", p=P8), V("p8", p=P8), -2048.0, plus)
+    pw = wrap(V("qd", 0, 64), bpm, p8h, 64, p=P8)
+    hoff = ts(S("hoff", U), pw, 2048.0, plus)
+    nd0 = ts(S("nd"), pw, 1024.0, OP.is_lt)
+    for j, (a, w) in enumerate(HV):
+        act(sub(nl, a, w), sub(ab, a, w), AF.Sign, -1.0,
+            alt=(tv(w, 0.5), lambda q, x=sub(nl, a, w), y=sub(ab, a, w): q.tensor_scalar(x[3], y[3], 0.0, -1.0, OP.is_gt, mul)))
+        mms(acc(qs[j], [(id1, sub(nl, a, w))]))
+        tt(sub(wc[0], 2 * L + a, w), sub(cb, a, w), qs[j], mul)
+        act(sub(sn, a, w), sub(wc[0], 2 * L + a, w), AF.Sign, 1.0, EPS)
+    for j in range(8):
+        act(sub(sg, 512 * j, 512), sub(dm, 512 * j, 512), AF.Sigmoid, extra=1.3 if j == 0 else 0.0)
+    tw, on, free, rf, go = lid, S("on"), S("free"), S("rf", F, 65), S("go")
+
+    for t in range(STEPS):
+        cw, aw, cn, an = wc[t % 2], wa[t % 2], wc[1 - t % 2], wa[1 - t % 2]
+        wn = A0 + 128 * t
+        arr = wn - 128
+        c, A = sub(cw, 2 * L, L), sub(aw, 2 * L, L)
+        hl = wrap(V("qb", 0, 64), bnm, nl, 64)
+        dh = V("qa", 0, 64)
+        wrap(dh, bnm, sn, 64, last=False)
+        wrap(dh, bhm, nl, 64, first=False)
+        if t == 0:
+            ts(on, hl, 0.0, OP.is_gt)
+            ts(sub(seg, 130, 64), hl, 0.0, OP.is_equal)
+            aff(free, on, -1.0, 1.0)
+            tt(go, nd0, on, mul)
+            scf = S("scs", B, 195)
+            scan(sub(scf, 130, 65), sub(rs, 130, 65), sub(seg, 130, 65))
+            pf = V("qd", 0, 65)
+            mms(acc(pf, [(tri, sub(seg, 130, 65)), (ones, sub(scf, 130, 65))]))
+            cp(rf, pf, True)
+        nf, rF = sub(rf, 64, 1), sub(rf, 0, 64)
+        hlg = tt(S("hlg"), hl, go, mul)
+        for a, w in PV:
+            gat(sub(eg, a, w), ex, sub(hoff, a // 16, w // 16))
+        xl, xr, dxh, sm, jq = [wrap(V("qc", 64 * j, 64), b, eg, 64) for j, b in enumerate((bxl, bxr, bdx, bsm, bjq))]
+        xlo, xro = ts(S("xlo", U), xl, 2048.0, plus), ts(S("xro", U), xr, 2048.0, plus)
+        for j, (a, w) in enumerate(HV):
+            mms(acc(qs[j], [(idn, sub(sn, a, w))]))
+            tt(sub(ss, a, w), sub(A, a, w), qs[j], mul)
+            act(sub(mr, a, w), sub(sn, a, w), AF.Relu, -1.0,
+                alt=(tv(w, 0.5), lambda q, x=sub(mr, a, w), y=sub(sn, a, w): q.tensor_scalar(x[3], y[3], 0.0, None, OP.is_lt)))
+        for a, w in PV:
+            o = (a // 16, w // 16)
+            act(sub(ns, a, w), sub(ss, a, w), AF.Copy, -1.0)
+            gtt(sub(kk, a, w), kp, sub(hoff, *o), sub(c, a, w), mul)
+            act(sub(cw, a, w), sub(kk, a, w), AF.Relu, 2.0)
+            ts(sub(cw, L + a, w), sub(kk, a, w), 2.0, mul, 0.0, OP.min)
+            gtt(sub(aw, a, w), sg, sub(xlo, *o), sub(ss, a, w), mul)
+            gtt(sub(aw, L + a, w), sg, sub(xro, *o), sub(ns, a, w), mul)
+        dma("G", nl, mr, 500, True)
+        dma("G", sub(cw, L, L), mr, 1000, True)
+        dma("G", sub(cw, 0, L), nl, 1000, True)
+        b0, b1, b2, brun, new = chain("kb", 2, B, F, F, 65)
+        if new:
+            mset(sub(b1[0], 64, 1), 0.0)
+            mset(sub(b1[1], 64, 1), 0.0)
+        v0, v1, v2, vrun, new = chain("kv", 4, F, F, HF)
+        x0, x1, x2, xrun, new = chain("kx", 2)
+        y0, y1, y2, yrun, new = chain("ky", 4, F, CI, F)
+        if new:
+            mset(y0[2], -1.0)
+        z0, z1, z2, zrun, new = chain("kz", 4, F, CI, I)
+        p0 = tt(sub(b1[1], 0, 64), tt(S("p01"), aff(S("p00"), rF, -1.0, 2047.0), free, mul), lid, OP.max)
+        gokh = aff(S("gokh"), go, 512.0, 0.0)
+        sp = [(fid(1), tt(S("sp0"), on, lidm, mul)), (fid(-1536), go)]
+        v2p = V("qc", 320, 64)
+        mms(acc(v2p, [(fid(1), lid1), (fid(-2048), on), (fid(1536), go)] + ([(fid(1), twl)] if t else [])))
+        if t == 0:
+            ts(v1[2], jq, -512.0, plus)
+            pre, nfm, twb, cm = aff(S("d0"), lid, 1.0, 2048.0), aff(C("nfm"), nf, 1.0, -2048.0), lid, 3071.0
+        else:
+            tt(v1[2], jq, aff(S("ta"), twl, 0.5, 512.0), minus)
+            twb = tt(S("twb"), twl, lid, plus)
+            n0, n1 = sub(S("cnt", F, 16), 8 * (t - 1), 1), sub(S("cnt", F, 16), 8 * (t - 1) + 4, 1)
+            cm = aff(C("cm"), n1, -1.0, aff(C("cm0"), n0, -1.0, 3071.0))
+            nfm = aff(C("nfm"), cm, 1.0, aff(C("nf5"), nf, 1.0, -5119.0))
+            thi = aff(C("thi"), cm, 1.0, -1024.0)
+            isa = ts(S("isa"), p0, thi, OP.is_gt)
+            aj = tt(S("aj"), ts(S("aj0"), rF, n0, OP.is_ge, aff(C("c64"), n0, -1.0, 64.0), mul), aff(S("rfa"), rF, 1.0, float(arr)), plus)
+            a3 = tt(S("a3"), aj, isa, mul)
+            pre = tt(S("pre"), aff(S("d0"), twb, 1.0, 2048.0), a3, OP.max)
+            sp.append((fid(1), a3))
+        adh = act(S("adh"), dh, AF.Abs, 1.0, 8.0)
+        lws = act(S("lws"), dh, AF.Sign, -1.0, -7.75)
+        dis = b0[1]
+        tt(sub(dis, 0, 64), adh, hlg, OP.is_lt)
+        scd = S("scd", B, 65)
+        scan(scd, sub(rs, 0, 65), dis)
+        pd = V("qb", 0, 65)
+        mms(acc(pd, [(tri, dis), (idk, dis), (ones, scd)]))
+        rD = V("qb", 0, 64)
+        ts(v0[1], rD, nfm, OP.is_lt, 2.0, mul)
+        par2 = ts(v0[3], rD, nfm, OP.is_lt, 2.0, mul)
+        hd = tt(v1[0], lws, dxh, mul)
+        winm = tt(v1[1], sm, hd, minus)
+        gq = tt(S("gq"), lws, gokh, mul)
+        tt(v1[3], v2p, gq, plus)
+        vrun()
+        qw = V("qd", 0, 128)
+        mms(acc(every(qw, 0, 2, 64), [(sub(ilo, 8, 128), v2[1]), (sub(ilo, 0, 128), v2[3])])
+            + acc(every(qw, 1, 2, 64), [(sub(ihi, 16, 128), v2[1]), (sub(ihi, 8, 128), v2[3])]))
+        wsb = cp(S("wsb", HF, 128), qw, True)
+        for j in range(2):
+            mms([(every(qr[j], r, 8, 64), sub(mm, 128 * r, 128), sub(wsb, 64 * j, 64), True, True) for r in range(8)])
+            aff(sub(zz, 3 * L + 512 * j, 512), qr[j], 1.0, OFF)
+        tt(sub(b1[0], 0, 64), rD, lc, plus)
+        par = aff(S("par"), par2, 0.5, 0.0)
+        thj = 2047.0 if t == 0 else thi
+        mnd = ts(C("mnd"), aff(C("mnd0"), V("qb", 64, 1), -1.0, thj), 1023.0, OP.max)
+        brun()
+        posf = sub(b2[1], 0, 64)
+        scat(sub(zz, 0, 3 * L), cp(S("pos", U), posf), sub(zz, 3 * L, L), SILU, 1.5 if t == 0 else 0.0)
+        aff(x1[0], posf, -1.0, cm)
+        ba = ts(z0[3], p0, mnd, OP.is_gt)
+        born = cp(z0[1], ba, True) if t == 0 else tt(z0[1], ba, isa, minus)
+        mt = tt(x0[1], born, par, plus)
+        nmt = aff(S("nmt"), mt, -1.0, 1.0)
+        tt(x1[1], nmt, pre, mul)
+        xrun()
+        idx = cp(S("idx", U), x2[1])
+        for a, w in PV:
+            o, zw, io_ = sub(g2, a, w), sub(zz, L, wn), sub(idx, a // 16, w // 16)
+            act(o, zw, AF.Identity, 1.0, -OFF, off=io_,
+                alt=(tv(w, GA), lambda q, o=o, zw=zw, io_=io_: q.tensor_scalar(o[3], zw[3].indirect(io_[3]), -OFF, None, plus)))
+        pg2 = wrap(V("qa", 0, 64), bjq, g2, 64)
+        pg1 = wrap(V("qd", 0, 64), bgm, g2, 64)
+        thr = tt(S("thr"), aff(S("th0"), born, -2048.0, 4096.0), tt(S("pj"), jq, par2, mul), minus)
+        win = ts(S("win", I), winm, 2048.0, plus)
+        tt(z1[3], win, aff(S("nba"), ba, -1.0, 1.0), mul)
+        s1p = V("qc", 384, 64)
+        mms(acc(s1p, sp + [(fid(-ZC), ba)]))
+        tt(z1[1], s1p, gq, minus)
+        cp(y0[1], mt, True)
+        tt(y1[1], twb, nmt, mul)
+        aff(y0[3], par, 1.0, -1.0)
+        tt(y1[3], tt(S("ox"), lidx, gq, plus), par, mul)
+        pq = ts(S("pq", I), pg2, 2048.0, plus)
+        low = ts(y1[0], pq, 1023, OP.bitwise_and)
+        hk = ts(y1[2], pq, 3072, OP.bitwise_and)
+        yrun()
+        ts(z1[0], pq, 2047, OP.bitwise_and)
+        pv = ts(z1[2], pg1, 2048.0, plus)
+        zrun()
+        f = tt(S("ge"), hk, thr, OP.is_ge)
+        if t > 0:
+            ej = tt(S("ej"), ts(S("key", I), pv, 4064, OP.bitwise_and), ts(S("wj", I), win, 4064, OP.bitwise_and), OP.is_equal)
+            f = tt(S("f"), f, tt(S("eq"), tt(S("el"), low, kb, OP.is_equal), ej, mul), plus)
+        tw, h = y2[1], z2[3]
+        lo = tt(S("lo"), tt(S("lt"), lid, tw, OP.is_lt), f, mul)
+        nup = tt(S("nup"), lo, f, OP.is_equal)
+        s1 = ts(S("s1", U), tt(S("x3"), z2[1], nup, mul), float(ZC), plus)
+        s2 = ts(S("s2", U), tt(S("y4"), y2[3], lo, mul), float(ZC), plus)
+        hoff = cp(S("hoff", U), h)
+        c, A = sub(cn, 2 * L, L), sub(an, 2 * L, L)
+        cwin, awin = sub(cw, 0, wn), sub(aw, 0, wn)
+        for a, w in (PV if t < STEPS - 1 else [(j * L // LAST, L // LAST) for j in range(LAST)]):
+            o = (a // 16, w // 16)
+            gat(sub(c1, a, w), cwin, sub(s1, *o))
+            gtt(sub(c, a, w), cwin, sub(s2, *o), sub(c1, a, w), plus)
+            act(sub(a1, a, w), awin, AF.Relu, off=sub(s1, *o))
+            gtt(sub(A, a, w), awin, sub(s2, *o), sub(a1, a, w), OP.max)
+            if t < STEPS - 1:
+                act(sub(sn, a, w), sub(c, a, w), AF.Sign, 1.0, EPS)
+                act(sub(nl, a, w), sub(A, a, w), AF.Sign, -1.0,
+                    alt=(tv(w), lambda q, x=sub(nl, a, w), y=sub(A, a, w): q.tensor_scalar(x[3], y[3], 0.0, -1.0, OP.is_gt, mul)))
+            else:
+                dma("S", T.yc[:, a:a + w], sub(c, a, w), w // 2)
+                gtt(sub(kk, a, w), kp, sub(hoff, *o), sub(A, a, w), mul)
+                dma("S", T.ya[:, a:a + w], sub(kk, a, w), w // 2)
+        if t == STEPS - 1:
+            break
+        onn = tt(S("onn"), tt(S("onp"), on, ba, plus), nup, mul)
+        dr = tt(S("dr"), ts(S("dr0"), h, float(H0), OP.is_ge), onn, mul)
+        se, so, sf = [sub(seg, 65 * j, 65) for j in range(3)]
+        tt(sub(so, 0, 64), dr, ts(S("od", I), h, 1, OP.bitwise_and), mul)
+        tt(sub(se, 0, 64), dr, sub(so, 0, 64), minus)
+        aff(sub(sf, 0, 64), onn, -1.0, 1.0)
+        tt(go, onn, dr, minus)
+        scs = S("scs", B, 195)
+        scan(scs, rs, seg)
+        ce, co, cf = [sub(scs, 65 * j, 65) for j in range(3)]
+        be = V("qd", 0, 130)
+        mms(acc(be, [(ones, sub(scs, 0, 130))]))
+        rk, pf, pe, po = [V("qr0", 65 * j, 65) for j in range(4)]
+        mms(acc(rk, [(tri, se), (tri, so), (ones, ce), (ones, co)]) + acc(pf, [(tri, sf), (ones, cf)])
+            + acc(pe, [(tri, se), (idn, se), (ones, ce)]) + acc(po, [(tri, so), (i64, so), (ones, co)]))
+        lt64 = ts(S("lt64"), sub(rk, 0, 64), float(CAP), OP.is_lt)
+        tt(rf, ts(S("rkm", F, 65), rk, float(CAP), OP.min), pf, plus)
+        le, lo_ = tt(S("le", B), lt64, sub(se, 0, 64), mul), tt(S("lod", B), lt64, sub(so, 0, 64), mul)
+        qn = V("qr1", 64, 128)
+        mms([(sub(qn, 0, 64), ones, le, True, True), (sub(qn, 64, 64), osh, lo_, True, True)])
+        sc_, cnt = S("sc%d" % t, F, 16), S("cnt", F, 16)
+        for j in range(2):
+            act(S("jk%d" % j), sub(qn, 64 * j, 64), AF.Identity, acc=sub(sc_, 4 * j, 1))
+        send([(sub(sc_, 0, 1), sub(cnt, 8 * t, 1), to1), (sub(sc_, 4, 1), sub(cnt, 8 * t + 4, 1), to2)], "rc%d" % t, [sub(cnt, 8 * t, 8)])
+        tt(on, onn, tt(S("lv"), le, lo_, plus), minus)
+        aff(free, on, -1.0, 1.0)
+        twl = tt(S("twl"), tt(S("twd"), tw, lid, minus), on, mul)
+        kb = tt(S("kb"), ts(S("kbe"), twl, 0.0, OP.is_equal, 2048.0, mul), lid, plus)
+        cd = tt(S("cd1", F, 130), V("qr0", 130, 130), sub(seg, 0, 130), mul)
+        tt(sub(w2, 0, 64), tt(S("cd2"), sub(cd, 0, 64), sub(cd, 65, 64), plus), lt64, mul)
+        ts(sub(w2, 72, 64), h, -float(H0 + 2048), plus)
+        kbs = S("kbs", F, 8)
+        for j in range(8):
+            act(S("jk%d" % (j % 2)), V("qd", 65 * (j // 4), 64), AF.Sign, -1.0, sub(jh, j % 4, 1), acc=sub(kbs, j, 1))
+        ko = S("ko", U, 16)
+        ts(sub(ko, 0, 8), kbs, 0.5, mul, 32.0, plus)
+        ts(sub(ko, 8, 8), kbs, 0.5, mul, 104.0, plus)
+        kb16 = aff(S("kb16", F, 8), kbs, 8.0, 512.0)
+        gg = gat(S("gg", F, 256), w2, ko)
+        msk = tt(S("msk", B, 128), sub(gg, 0, 128), sub(io, 1, 128), OP.is_equal)
+        hvm = tt(S("hvm", HF, 128), sub(gg, 128, 128), msk, mul)
+        vr = V("qd", 256, 128)
+        mms([(sub(vr, 0, 64), ones, sub(hvm, 0, 64), True, True), (sub(vr, 64, 64), osh, sub(hvm, 64, 64), True, True)])
+        sv = aff(S("sv%d" % t, F, 128), vr, 1.0, OFF)
+        send([(sub(sv, 0, 64), sub(zz, L + wn, 64), to1), (sub(sv, 64, 64), sub(zz, L + wn + 64, 64), to2)], "rv%d" % t, [sub(zz, L + wn, 128)])
+        ln = tt(S("ln", F, 8), wrap(V("qr1", 0, 8), bim, msk, 8), kb16, plus)
+        lno = S("lno", U, 12)
+        cp(sub(lno, 0, 8), ln)
+        cp(sub(lno, 8, 4), sub(ln, 0, 4))
+        sd, sh = S("sd%d" % t, F, 256), S("sh%d" % t, F, 128)
+        gat(sub(sd, 0, 128), sub(cn, 2 * L, L + 8), sub(lno, 0, 8))
+        gat(sub(sd, 128, 128), sub(an, 2 * L, L + 8), sub(lno, 4, 8))
+        dma("S", sub(sh, 0, 128, slice(16, 128)), sub(sd, 64, 128, slice(0, 112)), 64)
+        dma("S", sub(sh, 0, 128, slice(0, 16)), sub(sd, 64, 128, slice(112, 128)), 64)
+        send([(sub(sd, 0, 64), sub(cn, wn, 64), to1), (sub(sd, 192, 64), sub(an, wn, 64), to1),
+              (sub(sh, 0, 64), sub(cn, wn + 64, 64), to2), (sub(sh, 64, 64), sub(an, wn + 64, 64), to2)],
+             "rd%d" % t, [sub(cn, wn, 128), sub(an, wn, 128)])
+    return ops
+
+
+BEST = []
+
+
+def schedule(ops):
+    if not BEST:
+        BEST.append(min(range(TRIES), key=lambda s: schedule1(ops, s)[1]))
+    return schedule1(ops, BEST[0])
+
+
+def schedule1(ops, seed):
+    n = len(ops)
+    x = [seed * 7919 + 1]
+
+    def rnd():
+        x[0] = (x[0] * 1103515245 + 12345) % 2 ** 31
+        return x[0] / 2.0 ** 31
+    bias = BIAS * (0.5 + 2 * rnd())
+    noise = 0.6 * rnd()
+    succ = [[] for _ in range(n)]
+    for k, o in enumerate(ops):
+        for d in list(o["deps"]) + o["after"]:
+            succ[d].append(k)
+    pr = [0.0] * n
+    for k in range(n - 1, -1, -1):
+        o = ops[k]
+        pr[k] = min([a[0] for a in o["alts"].values()] or [0.0]) * (1 + noise * (rnd() - 0.5)) + o["lat"] + HOP + max([pr[s] for s in succ[k]] or [0.0])
+    pr = [o.get("first", p) for o, p in zip(ops, pr)]
+    left = [len(o["deps"]) + len(o["after"]) for o in ops]
+    ready, fin = [0.0] * n, [0.0] * n
+    free = {e: 0.0 for e in list("VAPGS") + ["pipe"]}
+    order = {e: [] for e in "VAPGS"}
+    cand = [k for k in range(n) if left[k] == 0]
+
+    def done(k, t):
+        fin[k] = t
+        cand.remove(k)
+        for s in succ[k]:
+            ready[s] = max(ready[s], t + HOP)
+            left[s] -= 1
+            if left[s] == 0:
+                cand.append(s)
+    while cand:
+        z = [k for k in cand if not ops[k]["alts"]]
+        if z:
+            done(z[0], ready[z[0]] + ops[z[0]]["lat"])
+            continue
+        t, e = min((max(free[e], ready[k]), e) for k in cand for e in ops[k]["alts"])
+        mine = [k for k in cand if e in ops[k]["alts"] and ready[k] <= t]
+        k = max(mine, key=lambda j: pr[j])
+        e = min(ops[k]["alts"], key=lambda x: max(free[x], ready[k]) + ops[k]["alts"][x][0] * (1 + bias if x == "V" else 1) + (bias if x == "V" else 0.0))
+        t = max(free[e], ready[k])
+        free[e] = t + ops[k]["alts"][e][0]
+        ops[k]["eng"], ops[k]["t0"] = e, t
+        order[e].append(k)
+        t = free[e]
+        if "pipe" in ops[k]:
+            t = max(t, free["pipe"])
+            free["pipe"] = t + ops[k]["pipe"]
+        done(k, t + ops[k]["lat"])
+    return order, max(fin)
+
+
+def rank_program(g, core, T, topo):
+    if T.rank_of(core) is None:
+        return
+    ops = build(T, topo, core)
+    order, _ = schedule(ops)
+    qs = {"V": g.vector, "A": g.scalar, "P": g.tensor, "G": g, "S": g.sync}
+    for o in ops:
+        o["wait"] = [d for d, hard in o["deps"].items() if hard or ops[d].get("eng") != o.get("eng")]
+    needed = set(d for o in ops for d in o["wait"])
+    cnt = {}
+    for e in order:
+        for k in order[e]:
+            if ops[k]["sem"] is None and k in needed:
+                cnt[e] = cnt.get(e, 0) + 1
+                ops[k]["sem"], ops[k]["one"] = ("e" + e, cnt[e]), True
+    top = {}
+    for e in order:
+        seen = {}
+        for k in order[e]:
+            o = ops[k]
+            want = {}
+            for d in o["wait"]:
+                s, v = ops[d]["sem"]
+                want[s] = max(want.get(s, 0), v)
+            for s, v in sorted(want.items()):
+                if seen.get(s, 0) < v:
+                    qs[e].wait_ge(T.sem[s], v)
+                    seen[s] = v
+                    top[s] = max(top.get(s, 0), v)
+            r = o["alts"][e][1](qs[e])
+            if o.get("one"):
+                r.then_inc(T.sem[o["sem"][0]], 1)
+            elif o["sem"] is not None and not o.get("remote"):
+                r.then_inc(T.sem[o["sem"][0]], o["sem"][1])
+    for o in ops:
+        if o["sem"] is not None and not o.get("one") and top.get(o["sem"][0], 0) < o["sem"][1]:
+            g.sync.wait_ge(T.sem[o["sem"][0]], o["sem"][1])

@@ -1,5 +1,5 @@
 from concourse.bass import DstId, RemoteDMATransfer
-from concourse.mybir import AluOpType as OP, ActivationFunctionType as AF
+from concourse.mybir import AluOpType as OP, ActivationFunctionType as AF, AxisListType as AX
 
 H, H0, L, CAP, STEPS = 4096, 3072, 1024, 64, 3
 ZC = 3072
@@ -8,11 +8,11 @@ WW = A0 + 256
 F, B, I, U, HF = "float32", "bfloat16", "int32", "uint16", "float16"
 CI = I
 SIZE = {F: 4, B: 2, I: 4, U: 2, HF: 2}
-POOL = {F: ("pf", 11200), B: ("pb", 5800), I: ("pi", 2200), U: ("pu", 1024), HF: ("ph", 1000)}
+POOL = {F: ("pf", 11200), B: ("pb", 7800), I: ("pi", 2200), U: ("pu", 1024), HF: ("ph", 1000)}
 SCRATCH = {
     "kp": ("sbuf", [128, H], B), "dm": ("sbuf", [128, H], B), "sg": ("sbuf", [128, H], F), "ex": ("sbuf", [128, H], B),
     "wc0": ("sbuf", [128, WW], F), "wc1": ("sbuf", [128, WW], F), "wa0": ("sbuf", [128, WW], F), "wa1": ("sbuf", [128, WW], F),
-    "zz": ("sbuf", [128, L + WW], F), "mm": ("sbuf", [128, L], B),
+    "zz": ("sbuf", [128, 4 * L + WW], F), "mm": ("sbuf", [128, L], B),
     "kk": ("sbuf", [128, L], F), "c1": ("sbuf", [128, L], F), "a1": ("sbuf", [128, L], F), "ss": ("sbuf", [128, L], F),
     "ns": ("sbuf", [128, L], F), "mr": ("sbuf", [128, L], B), "nl": ("sbuf", [128, L], B), "eg": ("sbuf", [128, L], B),
     "g2": ("sbuf", [128, L], HF), "cb": ("sbuf", [128, L], B), "ab": ("sbuf", [128, L], B),
@@ -24,14 +24,18 @@ for _n in ("qs0", "qs1", "qr0", "qr1", "qa", "qb", "qc", "qd"):
     SCRATCH[_n] = ("psum", [128, 512], F)
 SEMAPHORES = ["eV", "eA", "eP", "eG"] + ["d%d" % k for k in range(60)] + ["rv0", "rv1", "rd0", "rd1", "rc0", "rc1"]
 
-CY, FAC, GA, SC, PEC, HOP, BIAS = 0.00083, 1.25, 1.55, 3.8, 0.00042, 0.08, 0.3
-PIECES, LAST, TRIES = 2, 2, 100
+CY, FAC, GA, SC, PEC, HOP, BIAS = 0.00083, 1.1, 1.45, 3.5, 0.00042, 0.14, 0.3
+CASES = [(1.0, 1.3, 3.0, 0.15, 0.08, 1.0, 0.5, 0.8), (1.0, 1.55, 3.8, 0.1, 0.1, 2.0, 0.0, 0.8),
+         (1.25, 1.55, 3.8, 0.2, 0.1, 2.0, 1.0, 1.0), (1.45, 1.9, 5.5, 0.15, 0.05, 0.5, 0.3, 1.2)]
+PIECES, LAST, TRIES, CLIMB, PIN = 2, 2, 150, 4800, 0.5
+NEG = [0, 0, 0]
+KS = 40
 SILU = True
 EPS = 2.0 ** -40
 OFF = 6144.0
 
 
-def build(T, topo, core):
+def build(T, topo, core, FAC, GA, SC):
     ops, hist, lay, top, nsem = [], {}, {}, {}, [0]
 
     def V(name, a=0, n=None, p=None, step=1):
@@ -158,9 +162,12 @@ def build(T, topo, core):
     def chain(name, n, t0=F, t1=F, t2=F, w=64):
         name = "chain" + name
         new = name + "0" not in lay
-        d0, d1, o = S(name + "0", t0, n * w), S(name + "1", t1, n * w), S(name + "2", t2, n * w)
         if new:
-            mset(d0, 0 if t0 == I else 0.0)
+            if "chains" not in lay:
+                mset(S("chains", B, 1104), 0.0)
+            lay[name + "0"] = sub(lay["chains"], top.get("c", 0), n * w)
+            top["c"] = top.get("c", 0) + (n * w + 15) // 16 * 16
+        d0, d1, o = lay[name + "0"], S(name + "1", t1, n * w), S(name + "2", t2, n * w)
         return [[every(x, j, n, w) for j in range(n)] for x in (d0, d1, o)] + [lambda: scan(o, d0, d1), new]
 
     def iota(o, pat, base=0, cm=0):
@@ -208,7 +215,8 @@ def build(T, topo, core):
 
     rank, n = T.rank_of(core), len(T.cores)
     to1, to2 = T.cores[(rank + 1) % n], T.cores[(rank + 2) % n]
-    kp, dm, sg, ex, zz, mm = V("kp"), V("dm"), V("sg"), V("ex"), V("zz"), V("mm")
+    kp, dm, sg, ex, zz, mm = V("kp"), V("dm"), V("sg"), V("ex"), V("zz", 3 * L), V("mm")
+    zb = V("zz")
     kk, c1, a1, ss, ns, mr, nl, eg, g2, cb, ab = [V(x) for x in ("kk", "c1", "a1", "ss", "ns", "mr", "nl", "eg", "g2", "cb", "ab")]
     wc, wa = [V("wc0"), V("wc1")], [V("wa0"), V("wa1")]
     qs, qr = [V("qs0"), V("qs1")], [V("qr0"), V("qr1")]
@@ -223,7 +231,7 @@ def build(T, topo, core):
     dma("S", ab, T.amp[:], 256)
     dma("A", cb, T.cro[:], 256)
     dma("S", V("p8", p=P8), T.place[:], 200)
-    dma("S", ex, T.kap[:], 1000)
+    mset(ex, 0.0)
     dma("A", dm, T.dam[:], 1000)
     dma("S", kp, T.kap[:], 1000)
     for j, o in enumerate(ops):
@@ -234,7 +242,6 @@ def build(T, topo, core):
     qg = iota(S("qg", F, 128), [[16, 8], [0, 16]])
     l16 = iota(S("l16"), [[16, 64]])
     dma("G", sub(wa[0], 2 * L, L), T.amp[:], 512)
-    dma("G", sub(zz, L, 2 * L), sub(dm, 0, 2 * L), 1000)
     mset(mm, 0.0)
     ic = cp(C("ic"), ts(S("ici", I, 1), pi, 15, OP.bitwise_and))
     pc = cp(C("pc"), pi)
@@ -253,7 +260,7 @@ def build(T, topo, core):
 
     def sel(name, w):
         return aff(S(name, B, 144), b1m, w, 0.0)
-    bhm, bnm, bim = sel("bhm", 0.5), sel("bnm", -0.5), sel("bim", ic)
+    bhm, bnm, bim = sel("bhm", -1.0), sel("bnm", -0.5), sel("bim", ic)
     w4 = ts(C("w4"), ts(S("w4i", I, 1), pi, 3, OP.bitwise_and), 0.0, OP.is_equal)
     wl, wr_ = aff(C("wl"), w4, lo8, 0.0), aff(C("wr"), w4, hi8, 0.0)
     bxl, bxr = sel("bxl", wl), sel("bxr", wr_)
@@ -269,7 +276,7 @@ def build(T, topo, core):
     i8 = ts(S("i8", B, 144), i144, aff(C("p8c"), pc, 1.0, 8.0), OP.is_equal)
     ilo, ihi = aff(S("ilo", B, 144), i8, lo8, 0.0), aff(S("ihi", B, 144), i8, hi8, 0.0)
     idn = sub(i8, 8, 128)
-    id1, idk, i64 = [aff(S(x, B, 128), idn, w, 0.0) for x, w in (("id1", -1.0), ("idk", -2048.0), ("i65", 65.0))]
+    id1, idk, i64, i3k = [aff(S(x, B, 128), idn, w, 0.0) for x, w in (("id1", -1.0), ("idk", -2048.0), ("i65", 65.0), ("i3k", -float(ZC)))]
     sn = V("sn")
 
     def fid(w):
@@ -301,6 +308,9 @@ def build(T, topo, core):
     nj = ts(S("nj", I, 512), nat, 5, OP.arith_shift_right)
     dma("S", V("ex", p=slice(1, 128, 16)), aff(S("njq", B, 256), tt(S("nje", B, 256), sub(nj, 0, 256), sub(nj, 256, 256), OP.is_equal), 1024.0, -512.0), 250)
 
+    dma("G", sub(zz, 0, 3 * L), sub(ex, 0, 3 * L), 1500)
+    dma("G", sub(zb, L, 2 * L), sub(ex, 0, 2 * L), 1000)
+
     p8h = ts(V("p8h", p=P8), V("p8", p=P8), -2048.0, plus)
     pw = wrap(V("qd", 0, 64), bpm, p8h, 64, p=P8)
     hoff = ts(S("hoff", U), pw, 2048.0, plus)
@@ -313,21 +323,28 @@ def build(T, topo, core):
         act(sub(sn, a, w), sub(wc[0], 2 * L + a, w), AF.Sign, 1.0, EPS)
     for j in range(8):
         act(sub(sg, 512 * j, 512), sub(dm, 512 * j, 512), AF.Sigmoid, extra=1.3 if j == 0 else 0.0)
-    tw, on, free, rf, go = lid, S("on"), S("free"), S("rf", F, 65), S("go")
+    tw, on, ngo, rf, go = lid, S("on"), S("ngo", B), S("rf", F, 65), S("go")
+    lq = mset(S("lq", B, 130), 0.0)
+    eight = mset(S("eight", B), 8.0)
+    row0 = aff(S("row0", F, 128), ones, C("wg0"), 0.0)
 
     for t in range(STEPS):
         cw, aw, cn, an = wc[t % 2], wa[t % 2], wc[1 - t % 2], wa[1 - t % 2]
         wn = A0 + 128 * t
         arr = wn - 128
         c, A = sub(cw, 2 * L, L), sub(aw, 2 * L, L)
-        hl = wrap(V("qb", 0, 64), bnm, nl, 64)
+        hl = V("qb", 128, 64)
+        if t:
+            mms([(hl, idk, ngo, True, False)])
+        wrap(hl, bhm, nl, 64, first=t == 0)
         dh = V("qa", 0, 64)
-        wrap(dh, bnm, sn, 64, last=False)
-        wrap(dh, bhm, nl, 64, first=False)
+        mms([(dh, idn, eight, True, False)])
+        wrap(dh, bnm, sn, 64, first=False)
+        nrb = tt(S("nrb"), ts(S("nrz"), dh, 0.0, OP.is_equal, 64.0, mul), dh, plus)
+        nr2 = aff(S("nr2"), dh, 2.0, 0.0)
         if t == 0:
             ts(on, hl, 0.0, OP.is_gt)
             ts(sub(seg, 130, 64), hl, 0.0, OP.is_equal)
-            aff(free, on, -1.0, 1.0)
             tt(go, nd0, on, mul)
             scf = S("scs", B, 195)
             scan(sub(scf, 130, 65), sub(rs, 130, 65), sub(seg, 130, 65))
@@ -335,11 +352,14 @@ def build(T, topo, core):
             mms(acc(pf, [(tri, sub(seg, 130, 65)), (ones, sub(scf, 130, 65))]))
             cp(rf, pf, True)
         nf, rF = sub(rf, 64, 1), sub(rf, 0, 64)
-        hlg = tt(S("hlg"), hl, go, mul)
+        hlg = hl if t else tt(S("hlg"), hl, go, mul)
         for a, w in PV:
             gat(sub(eg, a, w), ex, sub(hoff, a // 16, w // 16))
-        xl, xr, dxh, sm, jq = [wrap(V("qc", 64 * j, 64), b, eg, 64) for j, b in enumerate((bxl, bxr, bdx, bsm, bjq))]
-        xlo, xro = ts(S("xlo", U), xl, 2048.0, plus), ts(S("xro", U), xr, 2048.0, plus)
+        dxh, sm, jq = [wrap(V("qc", 64 * j, 64), b, eg, 64) for j, b in enumerate((bdx, bsm, bjq))]
+        for j, b in enumerate((bxl, bxr)):
+            wrap(V("qs1", 64 * j, 64), b, eg, 64)
+        xo = ts(S("xo", U, 128), V("qs1", 0, 128), 2048.0, plus)
+        xlo, xro = sub(xo, 0, 64), sub(xo, 64, 64)
         for j, (a, w) in enumerate(HV):
             mms(acc(qs[j], [(idn, sub(sn, a, w))]))
             tt(sub(ss, a, w), sub(A, a, w), qs[j], mul)
@@ -350,23 +370,30 @@ def build(T, topo, core):
             act(sub(ns, a, w), sub(ss, a, w), AF.Copy, -1.0)
             gtt(sub(kk, a, w), kp, sub(hoff, *o), sub(c, a, w), mul)
             act(sub(cw, a, w), sub(kk, a, w), AF.Relu, 2.0)
-            ts(sub(cw, L + a, w), sub(kk, a, w), 2.0, mul, 0.0, OP.min)
+            if NEG[t] > a // w:
+                act(sub(cw, L + a, w), act(sub(c1, a, w), sub(kk, a, w), AF.Relu, -2.0), AF.Copy, -1.0)
+            else:
+                ts(sub(cw, L + a, w), sub(kk, a, w), 2.0, mul, 0.0, OP.min)
             gtt(sub(aw, a, w), sg, sub(xlo, *o), sub(ss, a, w), mul)
             gtt(sub(aw, L + a, w), sg, sub(xro, *o), sub(ns, a, w), mul)
         dma("G", nl, mr, 500, True)
-        dma("G", sub(cw, L, L), mr, 1000, True)
-        dma("G", sub(cw, 0, L), nl, 1000, True)
+        dma("G", sub(cw, L, L), mr, 700, True)
+        dma("G", sub(cw, 0, L), nl, 700, True)
         b0, b1, b2, brun, new = chain("kb", 2, B, F, F, 65)
         if new:
             mset(sub(b1[0], 64, 1), 0.0)
             mset(sub(b1[1], 64, 1), 0.0)
         v0, v1, v2, vrun, new = chain("kv", 4, F, F, HF)
-        x0, x1, x2, xrun, new = chain("kx", 2)
+        x0, x1, x2, xrun, new = chain("kx", 3)
+        if new:
+            mset(x0[1], 1.0)
         y0, y1, y2, yrun, new = chain("ky", 4, F, CI, F)
         if new:
             mset(y0[2], -1.0)
         z0, z1, z2, zrun, new = chain("kz", 4, F, CI, I)
-        p0 = tt(sub(b1[1], 0, 64), tt(S("p01"), aff(S("p00"), rF, -1.0, 2047.0), free, mul), lid, OP.max)
+        qp = V("qc", 192, 64)
+        mms(acc(qp, [(fid(1), aff(S("p00"), rF, -1.0, 2047.0)), (fid(-2048), on)]))
+        p0 = tt(sub(b1[1], 0, 64), qp, lid, OP.max)
         gokh = aff(S("gokh"), go, 512.0, 0.0)
         sp = [(fid(1), tt(S("sp0"), on, lidm, mul)), (fid(-1536), go)]
         v2p = V("qc", 320, 64)
@@ -376,7 +403,8 @@ def build(T, topo, core):
             pre, nfm, twb, cm = aff(S("d0"), lid, 1.0, 2048.0), aff(C("nfm"), nf, 1.0, -2048.0), lid, 3071.0
         else:
             tt(v1[2], jq, aff(S("ta"), twl, 0.5, 512.0), minus)
-            twb = tt(S("twb"), twl, lid, plus)
+            twb = V("qc", 256, 64)
+            mms(acc(twb, [(fid(1), twl), (fid(1), lid)]))
             n0, n1 = sub(S("cnt", F, 16), 8 * (t - 1), 1), sub(S("cnt", F, 16), 8 * (t - 1) + 4, 1)
             cm = aff(C("cm"), n1, -1.0, aff(C("cm0"), n0, -1.0, 3071.0))
             nfm = aff(C("nfm"), cm, 1.0, aff(C("nf5"), nf, 1.0, -5119.0))
@@ -386,14 +414,14 @@ def build(T, topo, core):
             a3 = tt(S("a3"), aj, isa, mul)
             pre = tt(S("pre"), aff(S("d0"), twb, 1.0, 2048.0), a3, OP.max)
             sp.append((fid(1), a3))
-        adh = act(S("adh"), dh, AF.Abs, 1.0, 8.0)
-        lws = act(S("lws"), dh, AF.Sign, -1.0, -7.75)
         dis = b0[1]
-        tt(sub(dis, 0, 64), adh, hlg, OP.is_lt)
+        tt(sub(dis, 0, 64), nrb, hlg, OP.is_lt)
+        lws = aff(S("lws"), tt(S("lw"), hlg, nr2, OP.is_ge), 2.0, -1.0)
         scd = S("scd", B, 65)
         scan(scd, sub(rs, 0, 65), dis)
         pd = V("qb", 0, 65)
-        mms(acc(pd, [(tri, dis), (idk, dis), (ones, scd)]))
+        ndh, nfh = V("qb", 72, 1), V("qb", 80, 1)
+        mms(acc(pd, [(tri, dis), (idk, dis), (ones, scd)]) + acc(ndh, [(ones, sub(scd, KS - 1, 1))]) + acc(nfh, [(row0, sub(rf, KS, 1))]))
         rD = V("qb", 0, 64)
         ts(v0[1], rD, nfm, OP.is_lt, 2.0, mul)
         par2 = ts(v0[3], rD, nfm, OP.is_lt, 2.0, mul)
@@ -415,31 +443,38 @@ def build(T, topo, core):
         mnd = ts(C("mnd"), aff(C("mnd0"), V("qb", 64, 1), -1.0, thj), 1023.0, OP.max)
         brun()
         posf = sub(b2[1], 0, 64)
-        scat(sub(zz, 0, 3 * L), cp(S("pos", U), posf), sub(zz, 3 * L, L), SILU, 1.5 if t == 0 else 0.0)
+        pos = cp(S("pos", U), posf)
         aff(x1[0], posf, -1.0, cm)
+        scat(sub(zz, 0, 3 * L), sub(pos, 0, KS), sub(zz, 3 * L, 16 * KS), SILU, 1.5 if t == 0 else 0.0)
+        scat(sub(zb, 0, 3 * L), sub(pos, KS, 64 - KS), sub(zz, 3 * L + 16 * KS, L - 16 * KS))
+        hlo, hhi = aff(C("hlo"), nfh, -0.5, 511.5), aff(C("hhi"), ndh, 0.5, 512.0)
+        ts(x1[1], act(S("xab"), x1[0], AF.Abs, -1.0, aff(C("mid"), hlo, 1.0, hhi)), aff(C("rad"), hlo, -1.0, hhi), OP.is_ge, -3072.0, mul)
         ba = ts(z0[3], p0, mnd, OP.is_gt)
         born = cp(z0[1], ba, True) if t == 0 else tt(z0[1], ba, isa, minus)
-        mt = tt(x0[1], born, par, plus)
+        mt = tt(x0[2], born, par, plus)
         nmt = aff(S("nmt"), mt, -1.0, 1.0)
-        tt(x1[1], nmt, pre, mul)
+        tt(x1[2], nmt, pre, mul)
         xrun()
-        idx = cp(S("idx", U), x2[1])
+        idx = ts(S("idx", U), x2[2], 3072.0, plus)
         for a, w in PV:
-            o, zw, io_ = sub(g2, a, w), sub(zz, L, wn), sub(idx, a // 16, w // 16)
+            o, zw, io_ = sub(g2, a, w), sub(zb, L, 3 * L + wn), sub(idx, a // 16, w // 16)
             act(o, zw, AF.Identity, 1.0, -OFF, off=io_,
                 alt=(tv(w, GA), lambda q, o=o, zw=zw, io_=io_: q.tensor_scalar(o[3], zw[3].indirect(io_[3]), -OFF, None, plus)))
         pg2 = wrap(V("qa", 0, 64), bjq, g2, 64)
         pg1 = wrap(V("qd", 0, 64), bgm, g2, 64)
-        thr = tt(S("thr"), aff(S("th0"), born, -2048.0, 4096.0), tt(S("pj"), jq, par2, mul), minus)
+        thr, ox, onp, kb = [V("qs0", 64 * j, 64) for j in range(4)]
+        mms(acc(ox, [(fid(1), lidx), (fid(1), gq)]) + (acc(onp, [(fid(1), on), (idn, ba)]) if t < STEPS - 1 else [])
+            + (acc(kb, [(fid(1), lid), (fid(1), kbe)]) if t else []))
+        tt(y1[3], ox, par, mul)
+        mms(acc(thr, [(fid(1), aff(S("th0"), born, -2048.0, 4096.0)), (fid(-1), tt(S("pj"), jq, par2, mul))]))
         win = ts(S("win", I), winm, 2048.0, plus)
         tt(z1[3], win, aff(S("nba"), ba, -1.0, 1.0), mul)
         s1p = V("qc", 384, 64)
-        mms(acc(s1p, sp + [(fid(-ZC), ba)]))
+        mms(acc(s1p, sp + [(i3k, ba)]))
         tt(z1[1], s1p, gq, minus)
         cp(y0[1], mt, True)
         tt(y1[1], twb, nmt, mul)
         aff(y0[3], par, 1.0, -1.0)
-        tt(y1[3], tt(S("ox"), lidx, gq, plus), par, mul)
         pq = ts(S("pq", I), pg2, 2048.0, plus)
         low = ts(y1[0], pq, 1023, OP.bitwise_and)
         hk = ts(y1[2], pq, 3072, OP.bitwise_and)
@@ -454,8 +489,11 @@ def build(T, topo, core):
         tw, h = y2[1], z2[3]
         lo = tt(S("lo"), tt(S("lt"), lid, tw, OP.is_lt), f, mul)
         nup = tt(S("nup"), lo, f, OP.is_equal)
-        s1 = ts(S("s1", U), tt(S("x3"), z2[1], nup, mul), float(ZC), plus)
-        s2 = ts(S("s2", U), tt(S("y4"), y2[3], lo, mul), float(ZC), plus)
+        x34 = S("x34", F, 128)
+        tt(sub(x34, 0, 64), z2[1], nup, mul)
+        tt(sub(x34, 64, 64), y2[3], lo, mul)
+        s12 = ts(S("s12", U, 128), x34, float(ZC), plus)
+        s1, s2 = sub(s12, 0, 64), sub(s12, 64, 64)
         hoff = cp(S("hoff", U), h)
         c, A = sub(cn, 2 * L, L), sub(an, 2 * L, L)
         cwin, awin = sub(cw, 0, wn), sub(aw, 0, wn)
@@ -475,43 +513,48 @@ def build(T, topo, core):
                 dma("S", T.ya[:, a:a + w], sub(kk, a, w), w // 2)
         if t == STEPS - 1:
             break
-        onn = tt(S("onn"), tt(S("onp"), on, ba, plus), nup, mul)
+        onn = tt(S("onn"), onp, nup, mul)
         dr = tt(S("dr"), ts(S("dr0"), h, float(H0), OP.is_ge), onn, mul)
         se, so, sf = [sub(seg, 65 * j, 65) for j in range(3)]
         tt(sub(so, 0, 64), dr, ts(S("od", I), h, 1, OP.bitwise_and), mul)
         tt(sub(se, 0, 64), dr, sub(so, 0, 64), minus)
         aff(sub(sf, 0, 64), onn, -1.0, 1.0)
-        tt(go, onn, dr, minus)
         scs = S("scs", B, 195)
         scan(scs, rs, seg)
         ce, co, cf = [sub(scs, 65 * j, 65) for j in range(3)]
         be = V("qd", 0, 130)
         mms(acc(be, [(ones, sub(scs, 0, 130))]))
-        rk, pf, pe, po = [V("qr0", 65 * j, 65) for j in range(4)]
-        mms(acc(rk, [(tri, se), (tri, so), (ones, ce), (ones, co)]) + acc(pf, [(tri, sf), (ones, cf)])
+        rk, pe, po = [V("qr0", 65 * j, 65) for j in range(3)]
+        mms(acc(rk, [(tri, se), (tri, so), (ones, ce), (ones, co)])
             + acc(pe, [(tri, se), (idn, se), (ones, ce)]) + acc(po, [(tri, so), (i64, so), (ones, co)]))
         lt64 = ts(S("lt64"), sub(rk, 0, 64), float(CAP), OP.is_lt)
-        tt(rf, ts(S("rkm", F, 65), rk, float(CAP), OP.min), pf, plus)
-        le, lo_ = tt(S("le", B), lt64, sub(se, 0, 64), mul), tt(S("lod", B), lt64, sub(so, 0, 64), mul)
-        qn = V("qr1", 64, 128)
+        r64 = act(S("r64", F, 65), rk, AF.Relu, -1.0, float(CAP))
+        le, lo_ = tt(sub(lq, 0, 64), lt64, sub(se, 0, 64), mul), tt(sub(lq, 65, 64), lt64, sub(so, 0, 64), mul)
+        qn = V("qa", 64, 128)
         mms([(sub(qn, 0, 64), ones, le, True, True), (sub(qn, 64, 64), osh, lo_, True, True)])
         sc_, cnt = S("sc%d" % t, F, 16), S("cnt", F, 16)
         for j in range(2):
-            act(S("jk%d" % j), sub(qn, 64 * j, 64), AF.Identity, acc=sub(sc_, 4 * j, 1))
+            add({"V": (tv(64), lambda q, o=sub(sc_, 4 * j, 1), x=sub(qn, 64 * j, 64): q.tensor_reduce(o[3], x[3], AX.X, plus))},
+                [sub(qn, 64 * j, 64)], [sub(sc_, 4 * j, 1)])
         send([(sub(sc_, 0, 1), sub(cnt, 8 * t, 1), to1), (sub(sc_, 4, 1), sub(cnt, 8 * t + 4, 1), to2)], "rc%d" % t, [sub(cnt, 8 * t, 8)])
-        tt(on, onn, tt(S("lv"), le, lo_, plus), minus)
-        aff(free, on, -1.0, 1.0)
+        cd = tt(S("cd1", F, 130), V("qr0", 65, 130), lq, mul)
+        tt(sub(w2, 0, 64), sub(cd, 0, 64), sub(cd, 65, 64), plus)
+        qo, qg_, qf = V("qr0", 256, 64), V("qr0", 320, 64), V("qr0", 384, 65)
+        mms(acc(qo, [(fid(1), onn), (id1, le), (id1, lo_)]) + acc(qg_, [(fid(1), onn), (fid(-1), dr)])
+            + acc(qf, [(tri, sf), (ones, cf), (fid(-1), r64)]))
+        cp(on, qo, True)
+        cp(go, qg_, True)
+        aff(ngo, qg_, -1.0, 1.0)
+        aff(rf, qf, 1.0, float(CAP))
         twl = tt(S("twl"), tt(S("twd"), tw, lid, minus), on, mul)
-        kb = tt(S("kb"), ts(S("kbe"), twl, 0.0, OP.is_equal, 2048.0, mul), lid, plus)
-        cd = tt(S("cd1", F, 130), V("qr0", 130, 130), sub(seg, 0, 130), mul)
-        tt(sub(w2, 0, 64), tt(S("cd2"), sub(cd, 0, 64), sub(cd, 65, 64), plus), lt64, mul)
+        kbe = act(S("kbe"), act(S("kba"), twl, AF.Abs), AF.Relu, -2048.0, 2048.0)
         ts(sub(w2, 72, 64), h, -float(H0 + 2048), plus)
-        kbs = S("kbs", F, 8)
+        kb2 = S("kbs", F, 16)
+        kbs = sub(kb2, 0, 8)
         for j in range(8):
-            act(S("jk%d" % (j % 2)), V("qd", 65 * (j // 4), 64), AF.Sign, -1.0, sub(jh, j % 4, 1), acc=sub(kbs, j, 1))
-        ko = S("ko", U, 16)
-        ts(sub(ko, 0, 8), kbs, 0.5, mul, 32.0, plus)
-        ts(sub(ko, 8, 8), kbs, 0.5, mul, 104.0, plus)
+            act(S("jk%d" % (j + 2), B), V("qd", 65 * (j // 4), 64), AF.Sign, -1.0, sub(jh, j % 4, 1), acc=sub(kbs, j, 1))
+        aff(sub(kb2, 8, 8), kbs, 1.0, 144.0)
+        ko = ts(S("ko", U, 16), kb2, 0.5, mul, 32.0, plus)
         kb16 = aff(S("kb16", F, 8), kbs, 8.0, 512.0)
         gg = gat(S("gg", F, 256), w2, ko)
         msk = tt(S("msk", B, 128), sub(gg, 0, 128), sub(io, 1, 128), OP.is_equal)
@@ -520,31 +563,101 @@ def build(T, topo, core):
         mms([(sub(vr, 0, 64), ones, sub(hvm, 0, 64), True, True), (sub(vr, 64, 64), osh, sub(hvm, 64, 64), True, True)])
         sv = aff(S("sv%d" % t, F, 128), vr, 1.0, OFF)
         send([(sub(sv, 0, 64), sub(zz, L + wn, 64), to1), (sub(sv, 64, 64), sub(zz, L + wn + 64, 64), to2)], "rv%d" % t, [sub(zz, L + wn, 128)])
-        ln = tt(S("ln", F, 8), wrap(V("qr1", 0, 8), bim, msk, 8), kb16, plus)
-        lno = S("lno", U, 12)
-        cp(sub(lno, 0, 8), ln)
-        cp(sub(lno, 8, 4), sub(ln, 0, 4))
+        ql = V("qr1", 256, 8)
+        wrap(ql, bim, msk, 8, last=False)
+        mms([(ql, fid(1), kb16, False, True)])
+        lno = cp(S("lno", U, 8), ql)
         sd, sh = S("sd%d" % t, F, 256), S("sh%d" % t, F, 128)
-        gat(sub(sd, 0, 128), sub(cn, 2 * L, L + 8), sub(lno, 0, 8))
-        gat(sub(sd, 128, 128), sub(an, 2 * L, L + 8), sub(lno, 4, 8))
+        gat(sub(sd, 0, 128), sub(cn, 2 * L, L + 8), lno)
+        gat(sub(sd, 128, 64), sub(an, 2 * L, L + 8), sub(lno, 4, 4))
+        gat(sub(sd, 192, 64), sub(an, 2 * L, L + 8), sub(lno, 0, 4))
         dma("S", sub(sh, 0, 128, slice(16, 128)), sub(sd, 64, 128, slice(0, 112)), 64)
         dma("S", sub(sh, 0, 128, slice(0, 16)), sub(sd, 64, 128, slice(112, 128)), 64)
         send([(sub(sd, 0, 64), sub(cn, wn, 64), to1), (sub(sd, 192, 64), sub(an, wn, 64), to1),
               (sub(sh, 0, 64), sub(cn, wn + 64, 64), to2), (sub(sh, 64, 64), sub(an, wn + 64, 64), to2)],
              "rd%d" % t, [sub(cn, wn, 128), sub(an, wn, 128)])
+    for o in ops:
+        o["all"] = list(o["deps"]) + o["after"]
     return ops
 
 
 BEST = []
 
 
-def schedule(ops):
+def replay(ops, seq, eng, hop, own, rem, dma):
+    fin, free, last, why = [0.0] * len(ops), {}, {}, [None] * len(ops)
+    for k in seq:
+        o, e = ops[k], eng[k]
+        t = free.get(e, 0.0)
+        why[k] = last.get(e)
+        for d in o["all"]:
+            u = fin[d] + (own if eng[d] == e else hop)
+            if u > t:
+                t = u
+                why[k] = d
+        if e:
+            t += o["alts"][e][0]
+            free[e] = t
+            last[e] = k
+        if "pipe" in o:
+            t = max(t, free.get("pipe", 0.0))
+            free["pipe"] = t + o["pipe"]
+            t += dma
+        fin[k] = t + o["lat"] + (rem if o.get("remote") else 0.0)
+    k = fin.index(max(fin))
+    while why[k] is not None:
+        if why[k] not in ops[k]["deps"] and why[k] not in ops[k]["after"]:
+            WAY.append((why[k], k))
+        k = why[k]
+    return max(fin)
+
+
+WAY = []
+
+
+def schedule(ops, others):
+    def schedule1(*a):
+        order, m, seq, eng = listing(*a)
+        return order, sum(replay(o, seq, eng, *w[3:7]) / w[7] for o, w in zip(others, CASES)) / len(CASES)
     if not BEST:
-        BEST.append(min(range(TRIES), key=lambda s: schedule1(ops, s)[1]))
-    return schedule1(ops, BEST[0])
+        flex = [k for k, o in enumerate(ops) if len(o["alts"]) > 1]
+        shift, pin = {}, {k: "A" for k in flex if ops[k]["alts"]["A"][0] < PIN}
+        seed = min(range(TRIES), key=lambda s: schedule1(ops, s, shift, pin)[1])
+        del WAY[:]
+        best = schedule1(ops, seed, shift, pin)[1]
+        way, now = list(WAY), [o.get("eng") for o in ops]
+        x = 12345
+        for _ in range(CLIMB):
+            s2, p2 = dict(shift), dict(pin)
+            for _ in range(1 + (x >> 9) % 2):
+                x = (x * 1103515245 + 12345) % 2 ** 31
+                a, b = way[(x >> 8) % len(way)]
+                d = (1 + (x >> 3) % 16) / 4.0
+                u = (x >> 20) % 8
+                if u < 2 and len(ops[a]["alts"]) > 1:
+                    p2[a] = "V" if now[a] == "A" else "A"
+                elif u < 3 and len(ops[b]["alts"]) > 1:
+                    p2[b] = "V" if now[b] == "A" else "A"
+                elif u < 5:
+                    s2[a] = s2.get(a, 0.0) - d
+                elif u < 7:
+                    up = [b]
+                    for _ in range(3):
+                        up = set(up) | set(j for i in up for j in ops[i]["all"])
+                    for i in up:
+                        s2[i] = s2.get(i, 0.0) + d
+                else:
+                    k = (x >> 8) % len(ops)
+                    s2[k] = s2.get(k, 0.0) + 2 * d - 4
+            del WAY[:]
+            m = schedule1(ops, seed, s2, p2)[1]
+            if m <= best:
+                best, shift, pin, way, now = m, s2, p2, list(WAY), [o.get("eng") for o in ops]
+        BEST.append((seed, shift, pin))
+    return schedule1(ops, *BEST[0])
 
 
-def schedule1(ops, seed):
+def listing(ops, seed, shift, pin):
     n = len(ops)
     x = [seed * 7919 + 1]
 
@@ -553,6 +666,7 @@ def schedule1(ops, seed):
         return x[0] / 2.0 ** 31
     bias = BIAS * (0.5 + 2 * rnd())
     noise = 0.6 * rnd()
+    look, gap = 0.6 * rnd(), 0.5 + 3 * rnd()
     succ = [[] for _ in range(n)]
     for k, o in enumerate(ops):
         for d in list(o["deps"]) + o["after"]:
@@ -561,15 +675,17 @@ def schedule1(ops, seed):
     for k in range(n - 1, -1, -1):
         o = ops[k]
         pr[k] = min([a[0] for a in o["alts"].values()] or [0.0]) * (1 + noise * (rnd() - 0.5)) + o["lat"] + HOP + max([pr[s] for s in succ[k]] or [0.0])
-    pr = [o.get("first", p) for o, p in zip(ops, pr)]
+    pr = [o.get("first", pr[k] + shift.get(k, 0.0)) for k, o in enumerate(ops)]
+    engs = [[pin[k]] if k in pin else list(o["alts"]) for k, o in enumerate(ops)]
     left = [len(o["deps"]) + len(o["after"]) for o in ops]
-    ready, fin = [0.0] * n, [0.0] * n
+    ready, fin, seq = [0.0] * n, [0.0] * n, []
     free = {e: 0.0 for e in list("VAPGS") + ["pipe"]}
     order = {e: [] for e in "VAPGS"}
     cand = [k for k in range(n) if left[k] == 0]
 
     def done(k, t):
         fin[k] = t
+        seq.append(k)
         cand.remove(k)
         for s in succ[k]:
             ready[s] = max(ready[s], t + HOP)
@@ -581,10 +697,13 @@ def schedule1(ops, seed):
         if z:
             done(z[0], ready[z[0]] + ops[z[0]]["lat"])
             continue
-        t, e = min((max(free[e], ready[k]), e) for k in cand for e in ops[k]["alts"])
-        mine = [k for k in cand if e in ops[k]["alts"] and ready[k] <= t]
+        t, e = min((max(free[e], ready[k]), e) for k in cand for e in engs[k])
+        mine = [k for k in cand if e in engs[k] and ready[k] <= t + 0.05]
         k = max(mine, key=lambda j: pr[j])
-        e = min(ops[k]["alts"], key=lambda x: max(free[x], ready[k]) + ops[k]["alts"][x][0] * (1 + bias if x == "V" else 1) + (bias if x == "V" else 0.0))
+        soon = [j for j in cand if e in engs[j] and ready[j] <= t + look * ops[k]["alts"][e][0] and pr[j] > pr[k] + gap]
+        if soon:
+            k = max(soon, key=lambda j: pr[j])
+        e = min(engs[k], key=lambda x: max(free[x], ready[k]) + ops[k]["alts"][x][0] * (1 + bias if x == "V" else 1) + (bias if x == "V" else 0.0))
         t = max(free[e], ready[k])
         free[e] = t + ops[k]["alts"][e][0]
         ops[k]["eng"], ops[k]["t0"] = e, t
@@ -594,14 +713,21 @@ def schedule1(ops, seed):
             t = max(t, free["pipe"])
             free["pipe"] = t + ops[k]["pipe"]
         done(k, t + ops[k]["lat"])
-    return order, max(fin)
+    return order, max(fin), seq, [o.get("eng") for o in ops]
+
+
+def plan(T, topo, core):
+    others = [] if BEST else [build(T, topo, core, *w[:3]) for w in CASES]
+    ops = build(T, topo, core, FAC, GA, SC)
+    for o in ops:
+        o["lat"] += 1.5 if o.get("remote") else 0.5 if "pipe" in o else 0.0
+    return ops, schedule(ops, others)
 
 
 def rank_program(g, core, T, topo):
     if T.rank_of(core) is None:
         return
-    ops = build(T, topo, core)
-    order, _ = schedule(ops)
+    ops, (order, _) = plan(T, topo, core)
     qs = {"V": g.vector, "A": g.scalar, "P": g.tensor, "G": g, "S": g.sync}
     for o in ops:
         o["wait"] = [d for d, hard in o["deps"].items() if hard or ops[d].get("eng") != o.get("eng")]

@@ -2,25 +2,25 @@ from concourse.bass import DstId, RemoteDMATransfer
 from concourse.mybir import AluOpType as OP, ActivationFunctionType as AF, AxisListType as AX
 
 H, H0, L, CAP, STEPS = 4096, 3072, 1024, 64, 3
-ZC = 3072
-A0 = ZC + 8
-WW = A0 + 256
+ARR, LB = 8, 640
+OLD = LB + 2 * L
+WW = OLD + L
+ZC, ZB, ZA = 256, 1280, 3328
+BIG = 8192.0
+SW = 72
 F, B, I, U, HF = "float32", "bfloat16", "int32", "uint16", "float16"
-CI = I
 SIZE = {F: 4, B: 2, I: 4, U: 2, HF: 2}
-POOL = {F: ("pf", 11200), B: ("pb", 7800), I: ("pi", 2200), U: ("pu", 1024), HF: ("ph", 1000)}
+POOL = {F: ("pf", 4000), B: ("pb", 5800), I: ("pi", 600), U: ("pu", 640), HF: ("ph", 4000)}
 SCRATCH = {
-    "kp": ("sbuf", [128, H], B), "dm": ("sbuf", [128, H], B), "sg": ("sbuf", [128, H], F), "ex": ("sbuf", [128, H], B),
-    "wc0": ("sbuf", [128, WW], F), "wc1": ("sbuf", [128, WW], F), "wa0": ("sbuf", [128, WW], F), "wa1": ("sbuf", [128, WW], F),
-    "zz": ("sbuf", [128, 4 * L + WW], F), "mm": ("sbuf", [128, L], B),
-    "kk": ("sbuf", [128, L], F), "c1": ("sbuf", [128, L], F), "a1": ("sbuf", [128, L], F), "ss": ("sbuf", [128, L], F),
-    "ns": ("sbuf", [128, L], F), "mr": ("sbuf", [128, L], B), "nl": ("sbuf", [128, L], B), "eg": ("sbuf", [128, L], B),
-    "g2": ("sbuf", [128, L], HF), "cb": ("sbuf", [128, L], B), "ab": ("sbuf", [128, L], B),
-    "sn": ("sbuf", [128, L], B), "p8": ("sbuf", [128, L], I), "p8h": ("sbuf", [128, L], HF),
+    "kp": ("sbuf", [128, H], B), "dm": ("sbuf", [128, H], B), "sg": ("sbuf", [128, H], F), "ex": ("sbuf", [128, H], I),
+    "wn": ("sbuf", [128, 6 * WW + 8], F), "zz": ("sbuf", [128, ZA + 2 * L + 8], F),
+    "kk": ("sbuf", [128, L], F), "c1": ("sbuf", [128, L], F), "a1": ("sbuf", [128, L], F),
+    "mc": ("sbuf", [128, 2 * L], B), "ma": ("sbuf", [128, 2 * L], B), "eg": ("sbuf", [128, L], HF),
+    "g2": ("sbuf", [128, L], HF), "cb": ("sbuf", [128, L], B), "ab": ("sbuf", [128, L], B), "c0": ("sbuf", [128, L], B),
 }
 for _d, (_n, _w) in POOL.items():
     SCRATCH[_n] = ("sbuf", [128, _w], _d)
-for _n in ("qs0", "qs1", "qr0", "qr1", "qa", "qb", "qc", "qd"):
+for _n in ("qr0", "qr1", "qa", "qb", "qc", "qd", "qe", "qm"):
     SCRATCH[_n] = ("psum", [128, 512], F)
 SEMAPHORES = ["eV", "eA", "eP", "eG"] + ["d%d" % k for k in range(60)] + ["rv0", "rv1", "rd0", "rd1", "rc0", "rc1"]
 
@@ -30,8 +30,6 @@ CASES = [(1.0, 1.3, 3.0, 0.15, 0.08, 1.0, 0.5, 0.8), (1.0, 1.55, 3.8, 0.1, 0.1, 
 PIECES, LAST, TRIES, CLIMB, PIN = 2, 2, 150, 4800, 0.5
 NEG = [0, 0, 0]
 KS = 40
-SILU = True
-EPS = 2.0 ** -40
 OFF = 6144.0
 
 
@@ -70,6 +68,9 @@ def build(T, topo, core, FAC, GA, SC):
     def meet(v, u):
         if not (v[1] < u[1] + u[2] and u[1] < v[1] + v[2] and v[4] & u[4]):
             return False
+        if v[5] > 64 or u[5] > 64:
+            a, b = (v, u) if v[5] > 64 else (u, v)
+            return any(b[1] <= c < b[1] + b[2] for c in range(a[1], a[1] + a[2], a[5]))
         return not (v[5] == u[5] and (v[1] - u[1]) % v[5])
 
     def add(alts, rd, wr, lat=0.0, sem=None, after=()):
@@ -107,9 +108,13 @@ def build(T, topo, core, FAC, GA, SC):
     def two(*vs):
         return all(SIZE[SCRATCH[v[0]][2]] == 2 for v in vs)
 
+    def tsv(o, x, s1, op0, s2=None, op1=None, off=None):
+        xi = x[3] if off is None else x[3].indirect(off[3])
+        a = (o[3], xi, ap(s1), ap(s2), op0) + (() if op1 is None else (op1,))
+        return (tv(o[6], GA if off else 0.5 if two(o, x) else 1), lambda q: q.tensor_scalar(*a))
+
     def ts(o, x, s1, op0, s2=None, op1=None):
-        a = (o[3], x[3], ap(s1), ap(s2), op0) + (() if op1 is None else (op1,))
-        add({"V": (tv(o[6], 0.5 if two(o, x) else 1), lambda q: q.tensor_scalar(*a))}, [x] + [s for s in (s1, s2) if isv(s)], [o])
+        add({"V": tsv(o, x, s1, op0, s2, op1)}, [x] + [s for s in (s1, s2) if isv(s)], [o])
         return o
 
     def tt(o, x, y, op):
@@ -129,9 +134,8 @@ def build(T, topo, core, FAC, GA, SC):
         add(alts, [x] + [s for s in (scale, bias, off) if isv(s)], [o] + ([acc] if acc else []))
         return o
 
-    def aff(o, x, mul, plus):
-        return act(o, x, AF.Identity, mul, plus,
-                   alt=(tv(o[6]), lambda q: q.tensor_scalar(o[3], x[3], ap(mul), ap(plus), OP.mult, OP.add)))
+    def aff(o, x, mul, plus, off=None):
+        return act(o, x, AF.Identity, mul, plus, off=off, alt=tsv(o, x, mul, OP.mult, plus, OP.add, off))
 
     def cp(o, x, both=False):
         v = (tv(o[6], 0.5 if two(o, x) else 1), lambda q: q.tensor_copy(o[3], x[3]))
@@ -145,6 +149,7 @@ def build(T, topo, core, FAC, GA, SC):
 
     def gtt(o, win, off, y, op):
         add({"V": (tv(o[6], GA), lambda q: q.tensor_tensor(o[3], win[3].indirect(off[3]), y[3], op))}, [win, off, y], [o])
+        return o
 
     def scat(win, off, x, silu=False, extra=0.0):
         if silu:
@@ -156,23 +161,17 @@ def build(T, topo, core, FAC, GA, SC):
         add({"V": (tv(o[6], 0.5 if two(o) else 1), lambda q: q.memset(o[3], c))}, [], [o])
         return o
 
-    def scan(o, d0, d1):
-        add({"V": (tv(o[6], 0.5 if two(o, d0, d1) else 1), lambda q: q.tensor_tensor_scan(o[3], d0[3], d1[3], 0.0, OP.mult, OP.add))}, [d0, d1], [o])
-
-    def chain(name, n, t0=F, t1=F, t2=F, w=64):
-        name = "chain" + name
-        new = name + "0" not in lay
-        if new:
-            if "chains" not in lay:
-                mset(S("chains", B, 1104), 0.0)
-            lay[name + "0"] = sub(lay["chains"], top.get("c", 0), n * w)
-            top["c"] = top.get("c", 0) + (n * w + 15) // 16 * 16
-        d0, d1, o = lay[name + "0"], S(name + "1", t1, n * w), S(name + "2", t2, n * w)
-        return [[every(x, j, n, w) for j in range(n)] for x in (d0, d1, o)] + [lambda: scan(o, d0, d1), new]
+    def scan(o, d0, d1, op1=OP.add):
+        add({"V": (tv(o[6], 0.5 if two(o, d0, d1) else 1), lambda q: q.tensor_tensor_scan(o[3], d0[3], d1[3], 0.0, OP.mult, op1))}, [d0, d1], [o])
+        return o
 
     def iota(o, pat, base=0, cm=0):
         kw = {} if SCRATCH[o[0]][2] == I else {"allow_small_or_imprecise_dtypes": True}
         add({"G": (0.13 + 2 * o[6] * CY * FAC, lambda q: q.iota(o[3], pat, base, cm, **kw))}, [], [o])
+        return o
+
+    def pick(o, x, pat, base):
+        add({"G": (0.17 + 2 * o[6] * CY * FAC, lambda q: q.affine_select(o[3], x[3], pat, OP.is_equal, 0.0, base, 1))}, [x], [o])
         return o
 
     def mms(lst):
@@ -183,17 +182,17 @@ def build(T, topo, core, FAC, GA, SC):
             return r
         add({"P": (0.05 + sum(max(64, m[0][6]) * PEC * FAC * (SIZE[SCRATCH[m[1][0]][2]] // 2) ** 2 + 0.01 for m in lst), emit)}, [v for m in lst for v in m[1:3]], [m[0] for m in lst])
 
-    def acc(o, terms):
-        return [(o, l, x, j == 0, j == len(terms) - 1) for j, (l, x) in enumerate(terms)]
+    def acc(o, terms, first=True, last=True):
+        return [(o, l, x, first and j == 0, last and j == len(terms) - 1) for j, (l, x) in enumerate(terms)]
 
-    def wrap(o, bm, x, n, first=True, last=True, p=None):
-        mms([(o, sub(bm, 15 - i, 128, p), V(x[0], x[1] + i, 16 * n - i, p, 16), first and i == 0, last and i == 15) for i in range(16)])
+    def wrap(o, bm, x, n, first=True, last=True):
+        mms([(o, sub(bm, 15 - i, 128), every(x, i, 16, n), first and i == 0, last and i == 15) for i in range(16)])
         return o
 
     def dma(eng, o, x, kb, acc=False):
         s = "d%d" % nsem[0]
         nsem[0] += 1
-        kw = {"accum_op": OP.add} if acc else {}
+        kw = {"accum_op": OP.add, "max_dma_last_dim": 8192} if acc else {}
         add({eng: (1.0 if eng == "G" else 0.1, lambda q: q.dma_start(ap(o), ap(x), **kw))},
             [v for v in (x, o if acc else None) if isv(v)], [o] if isv(o) else [], lat=1.6 + kb / 600.0, sem=(s, 16))
         ops[-1]["pipe"] = kb / 600.0
@@ -215,367 +214,312 @@ def build(T, topo, core, FAC, GA, SC):
 
     rank, n = T.rank_of(core), len(T.cores)
     to1, to2 = T.cores[(rank + 1) % n], T.cores[(rank + 2) % n]
-    kp, dm, sg, ex, zz, mm = V("kp"), V("dm"), V("sg"), V("ex"), V("zz", 3 * L), V("mm")
-    zb = V("zz")
-    kk, c1, a1, ss, ns, mr, nl, eg, g2, cb, ab = [V(x) for x in ("kk", "c1", "a1", "ss", "ns", "mr", "nl", "eg", "g2", "cb", "ab")]
-    wc, wa = [V("wc0"), V("wc1")], [V("wa0"), V("wa1")]
-    qs, qr = [V("qs0"), V("qs1")], [V("qr0"), V("qr1")]
-    P8 = slice(0, 8)
+    kp, dm, sg, ex, zz, mc, ma = [V(x) for x in ("kp", "dm", "sg", "ex", "zz", "mc", "ma")]
+    kk, c1, a1, eg, g2, cb, ab, c0 = [V(x) for x in ("kk", "c1", "a1", "eg", "g2", "cb", "ab", "c0")]
+    nl, mr = sub(mc, 0, L), sub(mc, L, L)
+    wc, wa = [V("wn", 2 * t * WW, WW + 8) for t in range(3)], [V("wn", (2 * t + 1) * WW, WW + 8) for t in range(3)]
+    qr = [V("qr0"), V("qr1")]
     HV = [(0, 512), (512, 512)]
     PV = [(j * L // PIECES, L // PIECES) for j in range(PIECES)]
     mul, plus, minus = OP.mult, OP.add, OP.subtract
 
-    nat = S("nat", I, 512)
-    dma("A", sub(nat, 0, 256), T.lf[:], 128)
-    dma("S", sub(nat, 256, 256), T.rt[:], 128)
+    mset(sub(ex, 0, 2 * L), 0)
+    iota(sub(ex, 2 * L, L), [[1, L]])
+    p4 = S("p4", I)
     dma("S", ab, T.amp[:], 256)
     dma("A", cb, T.cro[:], 256)
-    dma("S", V("p8", p=P8), T.place[:], 200)
-    mset(ex, 0.0)
-    dma("A", dm, T.dam[:], 1000)
+    for j in range(4):
+        dma("SA"[j % 2], sub(p4, 16 * j, 16), T.place[j % 2::2, 512 * (j // 2):512 * (j // 2) + 512], 30)
+    dma("S", V("ex", 0, H0, slice(0, 128, 16)), T.lf[:, 0:H0], 300)
+    dma("A", V("ex", 0, H0, slice(8, 128, 16)), T.rt[:, 0:H0], 300)
+    dma("S", dm, T.dam[:], 1000)
     dma("S", kp, T.kap[:], 1000)
     for j, o in enumerate(ops):
         o["first"] = 1000.0 - j
 
     pi = iota(S("pi", I, 1), [[0, 1]], 0, 1)
-    io = iota(S("io", F, 256), [[1, 256]])
+    io = iota(S("io", F, 272), [[1, 272]])
     qg = iota(S("qg", F, 128), [[16, 8], [0, 16]])
     l16 = iota(S("l16"), [[16, 64]])
-    dma("G", sub(wa[0], 2 * L, L), T.amp[:], 512)
-    mset(mm, 0.0)
-    ic = cp(C("ic"), ts(S("ici", I, 1), pi, 15, OP.bitwise_and))
+    iota(sub(ex, H0, L), [[1, L]], H0)
+    dma("G", sub(wa[0], OLD, L), T.amp[:], 512)
+    mset(V("wn", 0, 6 * WW + 1, None, WW), 0.0)
+    all1 = mset(S("all1", B, 512), 1.0)
+    one = mset(S("one", HF, SW), 1.0)
+    one64, one1 = sub(one, 0, 64), sub(one, 0, 1)
+    ici = ts(S("ici", I, 1), pi, 15, OP.bitwise_and)
+    ic = cp(C("ic"), ici)
     pc = cp(C("pc"), pi)
     g16 = tt(C("g16"), pc, ic, minus)
-    g15 = aff(C("g15"), g16, 1.0, 15.0)
     lid = aff(S("lid"), l16, 1.0, ic)
-    lid1 = aff(S("lid1"), lid, 1.0, 1024.0)
-    lidm = aff(S("lidm"), lid, 1.0, -1024.0)
-    lidx = aff(S("lidx"), lid, 1.0, 512.0 - ZC)
-    lc = aff(S("lc"), lid, -1.0, 4096.0)
+    nlid = aff(S("nlid"), lid, -1.0, 0.0)
+    lidh, lidb, lidk = [aff(S(x, HF), lid, 1.0, w) for x, w in (("lidh", 0.0), ("lidb", float(LB)), ("lidk", 1024.0))]
     jh = aff(S("jh", F, 4), sub(lid, 0, 4), 1.0, 0.5)
-    i144, i128, i16 = sub(io, 0, 144), sub(io, 0, 128), sub(io, 0, 16)
-    hi8 = ts(C("hi8"), ic, 8.0, OP.is_ge)
-    lo8 = aff(C("lo8"), hi8, -1.0, 1.0)
-    b1m = ts(S("b1m", B, 144), i144, g15, OP.is_equal)
+    i128, i64 = sub(io, 0, 128), sub(io, 0, 64)
+    b1 = ts(S("b1", B, 272), io, aff(C("g31"), g16, 1.0, 31.0), OP.is_equal)
 
     def sel(name, w):
-        return aff(S(name, B, 144), b1m, w, 0.0)
-    bhm, bnm, bim = sel("bhm", -1.0), sel("bnm", -0.5), sel("bim", ic)
-    w4 = ts(C("w4"), ts(S("w4i", I, 1), pi, 3, OP.bitwise_and), 0.0, OP.is_equal)
-    wl, wr_ = aff(C("wl"), w4, lo8, 0.0), aff(C("wr"), w4, hi8, 0.0)
-    bxl, bxr = sel("bxl", wl), sel("bxr", wr_)
-    bdx = sel("bdx", aff(C("wdx"), wr_, 1.0, aff(C("wdx0"), w4, -0.5, 0.0)))
-    bsm = sel("bsm", aff(C("wsm"), w4, 0.5, 0.0))
-    bjq = sel("bjq", ts(C("wjq"), ic, 1.0, OP.is_equal))
-    bgm = sel("bgm", ts(C("wg0"), ic, 0.0, OP.is_equal))
-    bpm = ts(S("bpm", B, 144), i144, aff(C("p15"), pc, 16.0, 15.0), OP.is_equal)
+        return aff(S(name, B, 144), sub(b1, 16, 144), w, 0.0)
+    e16 = ts(S("e16", F, 16), sub(io, 0, 16), ic, OP.is_equal)
+    bm1, bm2, bim, bx0, bx8 = sel("bm1", -1.0), sel("bm2", -2.0), sel("bim", ic), sel("bx0", sub(e16, 0, 1)), sel("bx8", sub(e16, 8, 1))
     ones = ts(S("ones", B, 128), qg, g16, OP.is_equal)
     tri = tt(S("tri", B, 128), ts(S("tri0", B, 128), i128, pc, OP.is_le, -1.0, mul), ones, mul)
     gn = tt(C("gn"), ts(C("gn0"), g16, 112.0, OP.is_ge, -128.0, mul), g16, plus)
-    osh = ts(S("osh", B, 128), qg, aff(C("gn2"), gn, 1.0, 16.0), OP.is_equal)
-    i8 = ts(S("i8", B, 144), i144, aff(C("p8c"), pc, 1.0, 8.0), OP.is_equal)
-    ilo, ihi = aff(S("ilo", B, 144), i8, lo8, 0.0), aff(S("ihi", B, 144), i8, hi8, 0.0)
-    idn = sub(i8, 8, 128)
-    id1, idk, i64, i3k = [aff(S(x, B, 128), idn, w, 0.0) for x, w in (("id1", -1.0), ("idk", -2048.0), ("i65", 65.0), ("i3k", -float(ZC)))]
-    sn = V("sn")
+    osh = ts(S("osh", F, 128), qg, aff(C("gn2"), gn, 1.0, 16.0), OP.is_equal, 0.5, mul)
+    onh = aff(S("onh", F, 128), ones, 0.5, 0.0)
+    row0 = ts(S("row0", B, 128), ones, sub(e16, 0, 1), mul, -1.0, mul)
+    i12 = pick(S("i12", B, 152), sub(all1, 0, 152), [[-1, 152]], 12)
+    ip = sub(i12, 12, 128)
+    im, kp1, km1, bp, bm, hp = [aff(S("wt%d" % j, B, 128), ip, w, 0.0) for j, w in enumerate((-1.0, 1024.0, -1024.0, BIG, -BIG, 0.5))]
+    f8i = aff(S("f8i", F, 128), ip, 8.0, 0.0)
+    e4 = ts(S("e4", F, 4), sub(io, 0, 4), cp(C("q4"), ts(S("q4i", I, 1), ici, 2, OP.arith_shift_right)), OP.is_equal)
+    mu = [aff(S("mu%d" % u, B, 152), i12, sub(e4, u, 1), 0.0) for u in range(4)]
+    mu1d, mu2n = aff(S("mu1d", B, 152), mu[1], 2.0, 0.0), aff(S("mu2n", B, 152), mu[2], -1.0, 0.0)
+    mmq = pick(S("mmq", B, 512), all1, [[-1, 4], [-16, 8], [-4, 16]], 0)
+    qb_ = S("qbm", B, 144)
+    mset(sub(qb_, 0, 3), 0.0)
+    pick(sub(qb_, 3, 128), sub(all1, 0, 128), [[-16, 8], [-1, 4], [1000, 4]], 0)
+    rs = mset(S("rs", B, 3 * SW), 1.0)
+    mset(every(rs, SW, SW, 2), 0.0)
+    seg = mset(S("seg", B, 3 * SW), 0.0)
+    dis = mset(S("dis", B, 65), 0.0)
+    zeros = mset(S("zeros", HF, 384), 0.0)
+    kd0, kq0, kt0 = [sub(zeros, 128 * j, 128) for j in range(3)]
+    rt_ = S("rt", I, 128 + 8)
+    mset(sub(rt_, 128, 8), 0)
+    cdc, c84 = mset(S("cdc", HF), -3840.0), mset(S("c84", HF, 65), -1984.0)
+    cj = [mset(S("cj%d" % t, HF), 1792.0 + BIG + 128 * (1 - t)) for t in range(2)]
+    kc = S("kc", HF, 3)
+    for j, w in enumerate((1024.0, -1536.0, 448.0)):
+        mset(sub(kc, j, 1), w)
+    svc = ts(S("svc", F, 128), aff(S("sv0", F, 128), i128, 1.0, 1800.0 + H0), aff(C("n3"), sub(e16, 3, 1), -1.0, 1.0), mul, OFF - H0, plus)
 
-    def fid(w):
-        new = "fid%d" % w not in lay
-        o = S("fid%d" % w, F, 128)
-        return aff(o, idn, float(w), 0.0) if new else o
-    d16 = ts(S("d16", B, 16), i16, ic, OP.is_equal)
-    scat(mm, ts(S("mof", U, 1), aff(C("mo1"), hi8, -1023.0, aff(C("mo0"), ic, 128.0, g16)), 0.0, plus), d16)
-    rs = mset(S("rs", B, 195), 1.0)
-    mset(sub(rs, 65, 1), 0.0)
-    mset(sub(rs, 130, 1), 0.0)
-    seg = mset(S("seg", B, 195), 0.0)
-    w2 = mset(S("w2", F, 144), 0.0)
-    for w in (wc[1], wa[1]):
-        mset(sub(w, ZC, 8), 0.0)
-    for w in (wc[0], wa[0]):
-        mset(sub(w, ZC, 8 + 128), 0.0)
-    mset(sub(zz, L + ZC, 8), 0.0)
-
-    nd = ts(C("ndc"), ic, 12.0, OP.is_lt)
-    dc = aff(C("dcc"), nd, -1.0, 1.0)
-    did = aff(S("did", F, 256), io, dc, aff(C("i257"), aff(C("i256"), ic, 256.0, 0.0), dc, 0.0))
-    for j in range(2):
-        v = tt(S("nv%d" % j, F, 256), ts(S("nu", F, 256), sub(nat, 256 * j, 256), nd, mul, -2048.0, plus), did, plus)
-        hi = cp(S("nh%d" % j, B, 256), v, True)
-        lo = tt(S("nl%d" % j, B, 256), v, hi, minus)
-        dma("S", V("ex", p=slice(8 * j, 128, 16)), hi, 250)
-        dma("A", V("ex", p=slice(8 * j + 4, 128, 16)), lo, 250)
-    nj = ts(S("nj", I, 512), nat, 5, OP.arith_shift_right)
-    dma("S", V("ex", p=slice(1, 128, 16)), aff(S("njq", B, 256), tt(S("nje", B, 256), sub(nj, 0, 256), sub(nj, 256, 256), OP.is_equal), 1024.0, -512.0), 250)
-
-    dma("G", sub(zz, 0, 3 * L), sub(ex, 0, 3 * L), 1500)
-    dma("G", sub(zb, L, 2 * L), sub(ex, 0, 2 * L), 1000)
-
-    p8h = ts(V("p8h", p=P8), V("p8", p=P8), -2048.0, plus)
-    pw = wrap(V("qd", 0, 64), bpm, p8h, 64, p=P8)
-    hoff = ts(S("hoff", U), pw, 2048.0, plus)
-    nd0 = ts(S("nd"), pw, 1024.0, OP.is_lt)
+    pt = S("pt")
+    pf = cp(S("pf0"), p4)
+    add({"V": (tv(64), lambda q: q.transpose(pt[3], pf[3]))}, [pf], [pt])
+    so = S("so", U, 192)
+    s1, hoff, s2 = [sub(so, 64 * j, 64) for j in range(3)]
+    cp(hoff, pt)
+    rf = S("rf", HF, 192)
+    rfo, fr, ngo = [sub(rf, 64 * j, 64) for j in range(3)]
+    ts(ngo, pt, float(H0), OP.is_ge)
     for j, (a, w) in enumerate(HV):
-        act(sub(nl, a, w), sub(ab, a, w), AF.Sign, -1.0,
-            alt=(tv(w, 0.5), lambda q, x=sub(nl, a, w), y=sub(ab, a, w): q.tensor_scalar(x[3], y[3], 0.0, -1.0, OP.is_gt, mul)))
-        mms(acc(qs[j], [(id1, sub(nl, a, w))]))
-        tt(sub(wc[0], 2 * L + a, w), sub(cb, a, w), qs[j], mul)
-        act(sub(sn, a, w), sub(wc[0], 2 * L + a, w), AF.Sign, 1.0, EPS)
+        act(sub(nl, a, w), sub(ab, a, w), AF.Sign, -1.0, alt=tsv(sub(nl, a, w), sub(ab, a, w), 0.0, OP.is_gt, -1.0, mul))
+        mms(acc(qr[j], [(im, sub(nl, a, w))]))
+        tt(sub(c0, a, w), sub(cb, a, w), qr[j], mul)
+        ts(sub(mr, a, w), sub(c0, a, w), 0.0, OP.is_lt)
+    dma("G", sub(wc[0], OLD, L), c0, 512)
     for j in range(8):
         act(sub(sg, 512 * j, 512), sub(dm, 512 * j, 512), AF.Sigmoid, extra=1.3 if j == 0 else 0.0)
-    tw, on, ngo, rf, go = lid, S("on"), S("ngo", B), S("rf", F, 65), S("go")
-    lq = mset(S("lq", B, 130), 0.0)
-    eight = mset(S("eight", B), 8.0)
-    row0 = aff(S("row0", F, 128), ones, C("wg0"), 0.0)
+    mc_, n0a, n0b, nfc, nfa = [V("qm", j, 1) for j in (0, 1, 2, 8, 9)]
+    de, do, sf = [sub(seg, SW * j, SW) for j in range(3)]
+    scs = S("scs", B, 3 * SW)
+    ce, co, cf = [sub(scs, SW * j, SW) for j in range(3)]
+    pre = lid
 
     for t in range(STEPS):
-        cw, aw, cn, an = wc[t % 2], wa[t % 2], wc[1 - t % 2], wa[1 - t % 2]
-        wn = A0 + 128 * t
-        arr = wn - 128
-        c, A = sub(cw, 2 * L, L), sub(aw, 2 * L, L)
-        hl = V("qb", 128, 64)
-        if t:
-            mms([(hl, idk, ngo, True, False)])
-        wrap(hl, bhm, nl, 64, first=t == 0)
-        dh = V("qa", 0, 64)
-        mms([(dh, idn, eight, True, False)])
-        wrap(dh, bnm, sn, 64, first=False)
-        nrb = tt(S("nrb"), ts(S("nrz"), dh, 0.0, OP.is_equal, 64.0, mul), dh, plus)
-        nr2 = aff(S("nr2"), dh, 2.0, 0.0)
+        cw, aw, cn, an = wc[t], wa[t], wc[(t + 1) % 3], wa[(t + 1) % 3]
+        c, A = (c0, ab) if t == 0 else (sub(cw, OLD, L), sub(aw, OLD, L))
+        ws = ZC - 128 * t
+        hl, u = V("qa", 0, 64), V("qb", 0, 64)
+        wrap(hl, bm1, nl, 64)
+        mms(acc(u, [(km1, ngo)], last=False))
+        wrap(u, bm1, nl, 64, False, False)
+        wrap(u, bm2, mr, 64, False)
         if t == 0:
-            ts(on, hl, 0.0, OP.is_gt)
-            ts(sub(seg, 130, 64), hl, 0.0, OP.is_equal)
-            tt(go, nd0, on, mul)
-            scf = S("scs", B, 195)
-            scan(sub(scf, 130, 65), sub(rs, 130, 65), sub(seg, 130, 65))
-            pf = V("qd", 0, 65)
-            mms(acc(pf, [(tri, sub(seg, 130, 65)), (ones, sub(scf, 130, 65))]))
-            cp(rf, pf, True)
-        nf, rF = sub(rf, 64, 1), sub(rf, 0, 64)
-        hlg = hl if t else tt(S("hlg"), hl, go, mul)
+            ts(sub(sf, 0, 64), hl, 0.0, OP.is_equal)
+            cp(fr, sub(sf, 0, 64), True)
+            scan(cf, sub(rs, 2 * SW, SW), sf)
+            pf_ = V("qd", 0, 64)
+            mms(acc(pf_, [(tri, sub(sf, 0, 64)), (ones, sub(cf, 0, 64)), (km1, sub(sf, 0, 64)), (km1, sub(sf, 0, 64))]))
+            mms(acc(nfc, [(ones, sub(cf, 64, 1)), (km1, one1), (km1, one1)]) + acc(nfa, [(ones, sub(cf, KS - 1, 1)), (km1, one1), (km1, one1)]))
+            cp(rfo, pf_, True)
         for a, w in PV:
-            gat(sub(eg, a, w), ex, sub(hoff, a // 16, w // 16))
-        dxh, sm, jq = [wrap(V("qc", 64 * j, 64), b, eg, 64) for j, b in enumerate((bdx, bsm, bjq))]
-        for j, b in enumerate((bxl, bxr)):
-            wrap(V("qs1", 64 * j, 64), b, eg, 64)
-        xo = ts(S("xo", U, 128), V("qs1", 0, 128), 2048.0, plus)
+            aff(sub(eg, a, w), ex, 1.0, -2048.0, sub(hoff, a // 16, w // 16))
+        xl_, xr_ = wrap(V("qc", 0, 64), bx0, eg, 64), wrap(V("qc", 64, 64), bx8, eg, 64)
+        xo = ts(S("xo", U, 128), V("qc", 0, 128), 2048.0, plus)
         xlo, xro = sub(xo, 0, 64), sub(xo, 64, 64)
-        for j, (a, w) in enumerate(HV):
-            mms(acc(qs[j], [(idn, sub(sn, a, w))]))
-            tt(sub(ss, a, w), sub(A, a, w), qs[j], mul)
-            act(sub(mr, a, w), sub(sn, a, w), AF.Relu, -1.0,
-                alt=(tv(w, 0.5), lambda q, x=sub(mr, a, w), y=sub(sn, a, w): q.tensor_scalar(x[3], y[3], 0.0, None, OP.is_lt)))
+        xf = cp(S("xf", HF, 128), V("qc", 0, 128), True)
+        xl, xr = sub(xf, 0, 64), sub(xf, 64, 64)
+        jf = aff(S("jf", HF, 128), xf, 1.0 / 32, 1164.0 - 15.5 / 32)
+        jl, jr = sub(jf, 0, 64), sub(jf, 64, 64)
+        for a, w in HV:
+            aff(sub(ma, a, w), sub(mr, a, w), -8.0, 0.0)
+            aff(sub(ma, L + a, w), sub(mr, a, w), 8.0, -8.0)
         for a, w in PV:
             o = (a // 16, w // 16)
-            act(sub(ns, a, w), sub(ss, a, w), AF.Copy, -1.0)
             gtt(sub(kk, a, w), kp, sub(hoff, *o), sub(c, a, w), mul)
-            act(sub(cw, a, w), sub(kk, a, w), AF.Relu, 2.0)
+            act(sub(cw, LB + a, w), sub(kk, a, w), AF.Relu, 2.0, alt=tsv(sub(cw, LB + a, w), sub(kk, a, w), 2.0, mul, 0.0, OP.max))
             if NEG[t] > a // w:
-                act(sub(cw, L + a, w), act(sub(c1, a, w), sub(kk, a, w), AF.Relu, -2.0), AF.Copy, -1.0)
+                act(sub(cw, LB + L + a, w), act(sub(c1, a, w), sub(kk, a, w), AF.Relu, -2.0), AF.Copy, -1.0)
             else:
-                ts(sub(cw, L + a, w), sub(kk, a, w), 2.0, mul, 0.0, OP.min)
-            gtt(sub(aw, a, w), sg, sub(xlo, *o), sub(ss, a, w), mul)
-            gtt(sub(aw, L + a, w), sg, sub(xro, *o), sub(ns, a, w), mul)
+                ts(sub(cw, LB + L + a, w), sub(kk, a, w), 2.0, mul, 0.0, OP.min)
+            gtt(sub(aw, LB + a, w), sg, sub(xlo, *o), sub(A, a, w), mul)
+            gtt(sub(aw, LB + L + a, w), sg, sub(xro, *o), sub(A, a, w), mul)
         dma("G", nl, mr, 500, True)
-        dma("G", sub(cw, L, L), mr, 700, True)
-        dma("G", sub(cw, 0, L), nl, 700, True)
-        b0, b1, b2, brun, new = chain("kb", 2, B, F, F, 65)
-        if new:
-            mset(sub(b1[0], 64, 1), 0.0)
-            mset(sub(b1[1], 64, 1), 0.0)
-        v0, v1, v2, vrun, new = chain("kv", 4, F, F, HF)
-        x0, x1, x2, xrun, new = chain("kx", 3)
-        if new:
-            mset(x0[1], 1.0)
-        y0, y1, y2, yrun, new = chain("ky", 4, F, CI, F)
-        if new:
-            mset(y0[2], -1.0)
-        z0, z1, z2, zrun, new = chain("kz", 4, F, CI, I)
-        qp = V("qc", 192, 64)
-        mms(acc(qp, [(fid(1), aff(S("p00"), rF, -1.0, 2047.0)), (fid(-2048), on)]))
-        p0 = tt(sub(b1[1], 0, 64), qp, lid, OP.max)
-        gokh = aff(S("gokh"), go, 512.0, 0.0)
-        sp = [(fid(1), tt(S("sp0"), on, lidm, mul)), (fid(-1536), go)]
-        v2p = V("qc", 320, 64)
-        mms(acc(v2p, [(fid(1), lid1), (fid(-2048), on), (fid(1536), go)] + ([(fid(1), twl)] if t else [])))
+        dma("G", sub(cw, LB, 2 * L), mc, 1400, True)
+        dma("G", sub(aw, LB, 2 * L), ma, 1400, True)
+        qe = V("qe", 0, 128)
+        dj, jx, qp, qj, qz = every(qe, 0, 2, 64), every(qe, 1, 2, 64), V("qe", 128, 64), V("qe", 192, 64), V("qe", 256, 64)
+        mms(acc(qp, [(im, rfo), (km1, fr), (km1, fr), (km1, fr)]) + (acc(qz, [(kp1, fr), (kp1, fr)]) if t else []))
+        p0 = tt(S("p0"), qp, nlid, OP.min)
+        mms(acc(dj, [(ip, jl), (im, jr)]))
+        lw, capv, par = every(kd0, 1, 2, 64), every(kq0, 1, 2, 64), every(S("kq1", HF, 128), 0, 2, 64)
         if t == 0:
-            ts(v1[2], jq, -512.0, plus)
-            pre, nfm, twb, cm = aff(S("d0"), lid, 1.0, 2048.0), aff(C("nfm"), nf, 1.0, -2048.0), lid, 3071.0
+            key = tt(S("key", HF), ts(S("cap0", HF), dj, 0.0, OP.not_equal), fr, OP.is_gt)
         else:
-            tt(v1[2], jq, aff(S("ta"), twl, 0.5, 512.0), minus)
-            twb = V("qc", 256, 64)
-            mms(acc(twb, [(fid(1), twl), (fid(1), lid)]))
-            n0, n1 = sub(S("cnt", F, 16), 8 * (t - 1), 1), sub(S("cnt", F, 16), 8 * (t - 1) + 4, 1)
-            cm = aff(C("cm"), n1, -1.0, aff(C("cm0"), n0, -1.0, 3071.0))
-            nfm = aff(C("nfm"), cm, 1.0, aff(C("nf5"), nf, 1.0, -5119.0))
-            thi = aff(C("thi"), cm, 1.0, -1024.0)
-            isa = ts(S("isa"), p0, thi, OP.is_gt)
-            aj = tt(S("aj"), ts(S("aj0"), rF, n0, OP.is_ge, aff(C("c64"), n0, -1.0, 64.0), mul), aff(S("rfa"), rF, 1.0, float(arr)), plus)
-            a3 = tt(S("a3"), aj, isa, mul)
-            pre = tt(S("pre"), aff(S("d0"), twb, 1.0, 2048.0), a3, OP.max)
-            sp.append((fid(1), a3))
-        dis = b0[1]
-        tt(sub(dis, 0, 64), nrb, hlg, OP.is_lt)
-        lws = aff(S("lws"), tt(S("lw"), hlg, nr2, OP.is_ge), 2.0, -1.0)
-        scd = S("scd", B, 65)
-        scan(scd, sub(rs, 0, 65), dis)
-        pd = V("qb", 0, 65)
-        ndh, nfh = V("qb", 72, 1), V("qb", 80, 1)
-        mms(acc(pd, [(tri, dis), (idk, dis), (ones, scd)]) + acc(ndh, [(ones, sub(scd, KS - 1, 1))]) + acc(nfh, [(row0, sub(rf, KS, 1))]))
-        rD = V("qb", 0, 64)
-        ts(v0[1], rD, nfm, OP.is_lt, 2.0, mul)
-        par2 = ts(v0[3], rD, nfm, OP.is_lt, 2.0, mul)
-        hd = tt(v1[0], lws, dxh, mul)
-        winm = tt(v1[1], sm, hd, minus)
-        gq = tt(S("gq"), lws, gokh, mul)
-        tt(v1[3], v2p, gq, plus)
-        vrun()
-        qw = V("qd", 0, 128)
-        mms(acc(every(qw, 0, 2, 64), [(sub(ilo, 8, 128), v2[1]), (sub(ilo, 0, 128), v2[3])])
-            + acc(every(qw, 1, 2, 64), [(sub(ihi, 16, 128), v2[1]), (sub(ihi, 8, 128), v2[3])]))
-        wsb = cp(S("wsb", HF, 128), qw, True)
+            ts(capv, dj, 0.0, OP.is_equal, 2047.0, plus)
+            tt(jx, qz, jr, OP.max)
+            cnt = sub(S("cnt", F, 16), 8 * (t - 1), 8)
+            mms([(V("qm", 0, 3), ip, kc, True, False), (mc_, onh, sub(cnt, 0, 1), False, False), (n0a, onh, sub(cnt, 0, 1), False, False),
+                 (n0b, onh, sub(cnt, 0, 1), False, False), (mc_, osh, sub(cnt, 4, 1), False, True)])
+            isa = ts(S("isa", HF), rfo, 2048.0, plus, mc_, OP.is_lt)
+            aj0 = ts(S("aj0", HF), rfo, n0a, OP.is_ge, n0b, mul)
+        au = act(S("au"), u, AF.Abs)
+        ts(lw, u, 0.0, OP.is_ge)
+        tt(sub(dis, 0, 64), au, hl, OP.is_lt)
+        scd = scan(S("scd", B, 65), sub(rs, 0, 65), dis)
+        rd, ndc, nda = V("qa", 0, 64), V("qa", 64, 1), V("qa", 72, 1)
+        mms(acc(V("qa", 0, 65), [(tri, dis), (km1, dis), (km1, dis), (ones, scd)], last=False) + acc(ndc, [(km1, one1), (km1, one1)], first=False)
+            + acc(nda, [(ones, sub(scd, KS - 1, 1)), (km1, one1), (km1, one1)]))
+
+        def cmp(o, x, sign, y, op):
+            return ts(o, x, y, op) if t == 0 else ts(o, x, mc_, sign, y, op)
+        kq1 = S("kq1", HF, 128)
+        if t:
+            scan(kq1, kd0, qe)
+        cmp(par, rd, plus, nfc, OP.is_lt)
+        xa, xb = tt(S("xa", HF), lw, xl_, mul), tt(S("xb", HF), lw, xr_, mul)
+        if t:
+            key = every(scan(S("kq2", HF, 128), kq0, kq1, OP.max), 1, 2, 64)
+            mms(acc(qj, [(ip, cj[t - 1]), (ip, rfo), (im, aj0), (bm, isa)]))
+            pre = tt(S("pre"), qj, tw, OP.min)
+        fq = [V("qd", 64 * j, 64) for j in range(3)]
+        mms(acc(fq[0], [(ip, xl), (im, xa), (ip, xb)]) + acc(fq[1], [(ip, lidb), (km1, one64), (kp1, ngo), (bm, fr), (km1, lw)])
+            + acc(fq[2], [(ip, xr), (bm, fr), (ip, xa), (im, xb)]))
+        fc = cp(S("fc", HF, 192), V("qd", 0, 192), True)
+        qw = V("qd", 0, 256)
+        code = [key, lidk, sub(fc, 64, 64), sub(fc, 0, 64)]
+        mms(sum([acc(every(qw, u, 4, 64), [(sub(mu[u], 12 - 4 * (f - u), 128), code[f]) for f in (1, 3, 2, 0)]) for u in range(4)], []))
+        wsb = cp(S("wsb", HF, 256), qw, True)
         for j in range(2):
-            mms([(every(qr[j], r, 8, 64), sub(mm, 128 * r, 128), sub(wsb, 64 * j, 64), True, True) for r in range(8)])
-            aff(sub(zz, 3 * L + 512 * j, 512), qr[j], 1.0, OFF)
-        tt(sub(b1[0], 0, 64), rD, lc, plus)
-        par = aff(S("par"), par2, 0.5, 0.0)
-        thj = 2047.0 if t == 0 else thi
-        mnd = ts(C("mnd"), aff(C("mnd0"), V("qb", 64, 1), -1.0, thj), 1023.0, OP.max)
-        brun()
-        posf = sub(b2[1], 0, 64)
-        pos = cp(S("pos", U), posf)
-        aff(x1[0], posf, -1.0, cm)
-        scat(sub(zz, 0, 3 * L), sub(pos, 0, KS), sub(zz, 3 * L, 16 * KS), SILU, 1.5 if t == 0 else 0.0)
-        scat(sub(zb, 0, 3 * L), sub(pos, KS, 64 - KS), sub(zz, 3 * L + 16 * KS, L - 16 * KS))
-        hlo, hhi = aff(C("hlo"), nfh, -0.5, 511.5), aff(C("hhi"), ndh, 0.5, 512.0)
-        ts(x1[1], act(S("xab"), x1[0], AF.Abs, -1.0, aff(C("mid"), hlo, 1.0, hhi)), aff(C("rad"), hlo, -1.0, hhi), OP.is_ge, -3072.0, mul)
-        ba = ts(z0[3], p0, mnd, OP.is_gt)
-        born = cp(z0[1], ba, True) if t == 0 else tt(z0[1], ba, isa, minus)
-        mt = tt(x0[2], born, par, plus)
-        nmt = aff(S("nmt"), mt, -1.0, 1.0)
-        tt(x1[2], nmt, pre, mul)
-        xrun()
-        idx = ts(S("idx", U), x2[2], 3072.0, plus)
+            mms([(every(qr[j], r, 4, 128), sub(mmq, 128 * r, 128), sub(wsb, 128 * j, 128), True, True) for r in range(4)])
+            aff(sub(zz, ZC + 512 * j, 512), qr[j], 1.0, OFF)
+        posf = tt(S("posf"), rd, p0, OP.min)
+        pos = ts(S("pos", U), posf, 2048.0, plus)
+        scat(sub(zz, ZA, 2 * L + 8), sub(pos, 0, KS), sub(zz, ZC, 16 * KS), True, 1.5 if t == 0 else 0.0)
+        scat(sub(zz, ZB, 2 * L), sub(pos, KS, 64 - KS), sub(zz, ZC + 16 * KS, L - 16 * KS))
+        qv = aff(S("qv", HF), posf, -1.0, 0.0) if t == 0 else ts(S("qv", HF), posf, mc_, plus, -1.0, mul)
+        j1 = cmp(S("j1", HF), rd, plus, nfa, OP.is_lt)
+        j2 = cmp(S("j2", HF), rfo, minus, nda, OP.is_lt)
+        nba = cmp(S("nba", HF), rfo, minus, ndc, OP.is_ge)
+        pp = V("qb", 0, 64)
+        mms(acc(pp, [(ip, qv), (kp1, j1), (kp1, j1), (kp1, j2), (kp1, j2), (bp, par), (bm, nba)] + ([(bm, isa)] if t else [])))
+        idx = ts(S("idx", U), tt(S("idf"), pp, pre, OP.max), float(ZC - ws), plus)
         for a, w in PV:
-            o, zw, io_ = sub(g2, a, w), sub(zb, L, 3 * L + wn), sub(idx, a // 16, w // 16)
-            act(o, zw, AF.Identity, 1.0, -OFF, off=io_,
-                alt=(tv(w, GA), lambda q, o=o, zw=zw, io_=io_: q.tensor_scalar(o[3], zw[3].indirect(io_[3]), -OFF, None, plus)))
-        pg2 = wrap(V("qa", 0, 64), bjq, g2, 64)
-        pg1 = wrap(V("qd", 0, 64), bgm, g2, 64)
-        thr, ox, onp, kb = [V("qs0", 64 * j, 64) for j in range(4)]
-        mms(acc(ox, [(fid(1), lidx), (fid(1), gq)]) + (acc(onp, [(fid(1), on), (idn, ba)]) if t < STEPS - 1 else [])
-            + (acc(kb, [(fid(1), lid), (fid(1), kbe)]) if t else []))
-        tt(y1[3], ox, par, mul)
-        mms(acc(thr, [(fid(1), aff(S("th0"), born, -2048.0, 4096.0)), (fid(-1), tt(S("pj"), jq, par2, mul))]))
-        win = ts(S("win", I), winm, 2048.0, plus)
-        tt(z1[3], win, aff(S("nba"), ba, -1.0, 1.0), mul)
-        s1p = V("qc", 384, 64)
-        mms(acc(s1p, sp + [(i3k, ba)]))
-        tt(z1[1], s1p, gq, minus)
-        cp(y0[1], mt, True)
-        tt(y1[1], twb, nmt, mul)
-        aff(y0[3], par, 1.0, -1.0)
-        pq = ts(S("pq", I), pg2, 2048.0, plus)
-        low = ts(y1[0], pq, 1023, OP.bitwise_and)
-        hk = ts(y1[2], pq, 3072, OP.bitwise_and)
-        yrun()
-        ts(z1[0], pq, 2047, OP.bitwise_and)
-        pv = ts(z1[2], pg1, 2048.0, plus)
-        zrun()
-        f = tt(S("ge"), hk, thr, OP.is_ge)
-        if t > 0:
-            ej = tt(S("ej"), ts(S("key", I), pv, 4064, OP.bitwise_and), ts(S("wj", I), win, 4064, OP.bitwise_and), OP.is_equal)
-            f = tt(S("f"), f, tt(S("eq"), tt(S("el"), low, kb, OP.is_equal), ej, mul), plus)
-        tw, h = y2[1], z2[3]
-        lo = tt(S("lo"), tt(S("lt"), lid, tw, OP.is_lt), f, mul)
-        nup = tt(S("nup"), lo, f, OP.is_equal)
-        x34 = S("x34", F, 128)
-        tt(sub(x34, 0, 64), z2[1], nup, mul)
-        tt(sub(x34, 64, 64), y2[3], lo, mul)
-        s12 = ts(S("s12", U, 128), x34, float(ZC), plus)
-        s1, s2 = sub(s12, 0, 64), sub(s12, 64, 64)
-        hoff = cp(S("hoff", U), h)
-        c, A = sub(cn, 2 * L, L), sub(an, 2 * L, L)
-        cwin, awin = sub(cw, 0, wn), sub(aw, 0, wn)
+            aff(sub(g2, a, w), sub(zz, ws, ZA + 2 * L + 8 - ws), 1.0, -OFF, sub(idx, a // 16, w // 16))
+        mms(acc(V("qe", 320, 64), [(ip, lidb), (kp1, lw), (bp, par), (bm, one64)]) + acc(V("qe", 384, 64), [(bp, one64), (bm, fr), (bm, nba)]))
+        o2 = cp(S("o2", F, 128), V("qe", 320, 128), True)
+        q4 = V("qr0", 0, 256)
+        mms(acc(q4, [(sub(qb_, 3 - r, 128), every(g2, r, 4, 256)) for r in range(4)]))
+        qsb = cp(S("qsb", HF, 256), q4, True)
+
+        def back(m, f):
+            return [(sub(m, 12 - 4 * (u - f), 128), every(qsb, u, 4, 64)) for u in range(4)]
+        pk, qt = V("qa", 0, 64), V("qb", 0, 128)
+        pd = every(qt, 0, 2, 64)
+        mms(acc(pk, [(ip, key)] if t == 0 else [(im, key), (bp, fr), (bp, nba), (bp, isa)], last=False))
+        mms((acc(every(qt, 1, 2, 64), [(ip, lidh)]) if t == 1 else []) + acc(pd, [(im, lidk)], last=False))
+        mms(acc(pk, back(mu[0], 0), first=False))
+        mms(acc(pd, back(mu[1], 1), first=False))
+        mq = [V("qc", 64 * j, 64) for j in range(3)]
+        mms(acc(mq[0], [(ip, cdc), (bm, nba), (bm, nba)] + back(mu1d, 1) + back(mu2n, 2)) + acc(mq[1], [(bm, nba)] + back(mu[3], 3)))
+        f8 = ts(S("f8"), pk, 0.5, OP.is_lt, BIG, mul) if t == 0 else ts(S("f8"), pk, BIG, OP.is_equal, BIG, mul)
+        tt(sub(rt_, 0, 128), V("qc", 0, 128), sub(fc, 64, 128), OP.max)
+        mms(acc(mq[2], [(kp1, one64), (kp1, one64)] + back(mu[2], 2)))
+        eb = tt(V("qm", 64, 64), f8, pd, mul)
+        r2 = tt(S("r2"), mq[2], sub(o2, 0, 64), OP.max)
+        upn = tt(V("qm", 128, 64), eb, sub(o2, 64, 64), OP.min)
+        h = sub(rt_, 64, 64)
+        if t < STEPS - 1:
+            ts(sub(so, 0, 128), sub(rt_, 0, 128), 2048.0, plus)
+        else:
+            ts(s1, tt(S("s1f"), upn, sub(rt_, 0, 64), plus), 2048.0, plus)
+            ts(hoff, h, 2048.0, plus)
+        cp(s2, tt(S("s2f"), eb, r2, OP.min))
+        c, A = sub(cn, OLD, L), sub(an, OLD, L)
+        cwin, awin = sub(cw, 0, WW), sub(aw, 0, WW)
         for a, w in (PV if t < STEPS - 1 else [(j * L // LAST, L // LAST) for j in range(LAST)]):
             o = (a // 16, w // 16)
+            act(sub(a1, a, w), awin, AF.Relu, off=sub(s1, *o), alt=tsv(sub(a1, a, w), awin, 0.0, OP.max, off=sub(s1, *o)))
+            gtt(sub(A, a, w), awin, sub(s2, *o), sub(a1, a, w), OP.max)
             gat(sub(c1, a, w), cwin, sub(s1, *o))
             gtt(sub(c, a, w), cwin, sub(s2, *o), sub(c1, a, w), plus)
-            act(sub(a1, a, w), awin, AF.Relu, off=sub(s1, *o))
-            gtt(sub(A, a, w), awin, sub(s2, *o), sub(a1, a, w), OP.max)
             if t < STEPS - 1:
-                act(sub(sn, a, w), sub(c, a, w), AF.Sign, 1.0, EPS)
-                act(sub(nl, a, w), sub(A, a, w), AF.Sign, -1.0,
-                    alt=(tv(w), lambda q, x=sub(nl, a, w), y=sub(A, a, w): q.tensor_scalar(x[3], y[3], 0.0, -1.0, OP.is_gt, mul)))
+                act(sub(nl, a, w), sub(A, a, w), AF.Sign, -1.0, alt=tsv(sub(nl, a, w), sub(A, a, w), 0.0, OP.is_gt, -1.0, mul))
+                ts(sub(mr, a, w), sub(c, a, w), 0.0, OP.is_lt)
             else:
                 dma("S", T.yc[:, a:a + w], sub(c, a, w), w // 2)
                 gtt(sub(kk, a, w), kp, sub(hoff, *o), sub(A, a, w), mul)
                 dma("S", T.ya[:, a:a + w], sub(kk, a, w), w // 2)
         if t == STEPS - 1:
             break
-        onn = tt(S("onn"), onp, nup, mul)
-        dr = tt(S("dr"), ts(S("dr0"), h, float(H0), OP.is_ge), onn, mul)
-        se, so, sf = [sub(seg, 65 * j, 65) for j in range(3)]
-        tt(sub(so, 0, 64), dr, ts(S("od", I), h, 1, OP.bitwise_and), mul)
-        tt(sub(se, 0, 64), dr, sub(so, 0, 64), minus)
-        aff(sub(sf, 0, 64), onn, -1.0, 1.0)
-        scs = S("scs", B, 195)
+        if t == 0:
+            tw = tt(S("tw"), pd, lid, plus)
+        else:
+            ts(every(kt0, 1, 2, 64), pk, BIG + 200.0, OP.is_lt)
+            tw = every(scan(S("tw2", F, 128), kt0, qt), 1, 2, 64)
+        z = tt(S("z"), upn, ts(S("y", I), h, 3073, OP.bitwise_and), plus)
+        ts(sub(de, 0, 64), z, 1024.0, OP.is_equal)
+        ts(sub(do, 0, 64), z, 1025.0, OP.is_equal)
+        ts(sub(sf, 0, 64), upn, 0.0, OP.is_lt)
         scan(scs, rs, seg)
-        ce, co, cf = [sub(scs, 65 * j, 65) for j in range(3)]
-        be = V("qd", 0, 130)
-        mms(acc(be, [(ones, sub(scs, 0, 130))]))
-        rk, pe, po = [V("qr0", 65 * j, 65) for j in range(3)]
-        mms(acc(rk, [(tri, se), (tri, so), (ones, ce), (ones, co)])
-            + acc(pe, [(tri, se), (idn, se), (ones, ce)]) + acc(po, [(tri, so), (i64, so), (ones, co)]))
-        lt64 = ts(S("lt64"), sub(rk, 0, 64), float(CAP), OP.is_lt)
-        r64 = act(S("r64", F, 65), rk, AF.Relu, -1.0, float(CAP))
-        le, lo_ = tt(sub(lq, 0, 64), lt64, sub(se, 0, 64), mul), tt(sub(lq, 65, 64), lt64, sub(so, 0, 64), mul)
-        qn = V("qa", 64, 128)
-        mms([(sub(qn, 0, 64), ones, le, True, True), (sub(qn, 64, 64), osh, lo_, True, True)])
+        d64 = [sub(x, 0, 64) for x in (de, do, sf, ce, co, cf)]
+        rank_ = [(tri, d64[0]), (tri, d64[1]), (ones, d64[3]), (ones, d64[4])]
+        xe, xo_ = V("qb", 0, 64), V("qb", 64, 64)
+        mms(acc(xe, rank_ + [(bm, d64[0])]) + acc(xo_, rank_ + [(bm, d64[1])]))
         sc_, cnt = S("sc%d" % t, F, 16), S("cnt", F, 16)
-        for j in range(2):
-            add({"V": (tv(64), lambda q, o=sub(sc_, 4 * j, 1), x=sub(qn, 64 * j, 64): q.tensor_reduce(o[3], x[3], AX.X, plus))},
-                [sub(qn, 64 * j, 64)], [sub(sc_, 4 * j, 1)])
+        le, lo_ = [act(S("le%d" % j, HF), x, AF.Sign, -1.0, CAP - 0.5 - BIG, acc=sub(sc_, 4 * j, 1)) for j, x in enumerate((xe, xo_))]
         send([(sub(sc_, 0, 1), sub(cnt, 8 * t, 1), to1), (sub(sc_, 4, 1), sub(cnt, 8 * t + 4, 1), to2)], "rc%d" % t, [sub(cnt, 8 * t, 8)])
-        cd = tt(S("cd1", F, 130), V("qr0", 65, 130), lq, mul)
-        tt(sub(w2, 0, 64), sub(cd, 0, 64), sub(cd, 65, 64), plus)
-        qo, qg_, qf = V("qr0", 256, 64), V("qr0", 320, 64), V("qr0", 384, 65)
-        mms(acc(qo, [(fid(1), onn), (id1, le), (id1, lo_)]) + acc(qg_, [(fid(1), onn), (fid(-1), dr)])
-            + acc(qf, [(tri, sf), (ones, cf), (fid(-1), r64)]))
-        cp(on, qo, True)
-        cp(go, qg_, True)
-        aff(ngo, qg_, -1.0, 1.0)
-        aff(rf, qf, 1.0, float(CAP))
-        twl = tt(S("twl"), tt(S("twd"), tw, lid, minus), on, mul)
-        kbe = act(S("kbe"), act(S("kba"), twl, AF.Abs), AF.Relu, -2048.0, 2048.0)
-        ts(sub(w2, 72, 64), h, -float(H0 + 2048), plus)
-        kb2 = S("kbs", F, 16)
-        kbs = sub(kb2, 0, 8)
+        rk = V("qa", 0, 65)
+        mms(acc(rk, [(tri, sub(de, 0, 65)), (tri, sub(do, 0, 65)), (ones, sub(ce, 0, 65)), (ones, sub(co, 0, 65))]))
+        r64 = act(S("r64", HF, 65), rk, AF.Relu, -1.0, float(CAP))
+        be, cq = V("qd", 0, 2 * SW), V("qr1", 0, 2 * SW)
+        mms(acc(be, [(ones, sub(scs, 0, 2 * SW))]))
+        mms(acc(sub(cq, 0, SW), [(tri, de), (ones, ce), (bm, de)]) + acc(sub(cq, SW, SW), [(tri, do), (ones, co), (bm, do)]))
+        qf = [V("qr0", 64 * j, 64) for j in range(3)]
+        mms(acc(qf[0], [(tri, d64[2]), (ones, d64[5]), (ip, sub(c84, 0, 64)), (km1, d64[2]), (km1, d64[2]), (im, sub(r64, 0, 64)), (km1, le), (km1, lo_)])
+            + acc(qf[1], [(ip, d64[2]), (ip, one64), (hp, le), (hp, lo_)]) + acc(qf[2], [(ip, x) for x in d64[:3]]))
+        cp(rf, V("qr0", 0, 192), True)
+        mms(acc(nfc, [(ones, sub(cf, 64, 1)), (ip, sub(c84, 0, 1)), (im, sub(r64, 64, 1))])
+            + acc(nfa, [(ones, sub(cf, KS - 1, 1)), (ip, sub(c84, 0, 1)), (row0, sub(r64, KS, 1))]))
+        w2 = aff(S("w2", F, 2 * SW), cq, 1.0, BIG)
+        kbs = S("kbs", F, 8)
         for j in range(8):
-            act(S("jk%d" % (j + 2), B), V("qd", 65 * (j // 4), 64), AF.Sign, -1.0, sub(jh, j % 4, 1), acc=sub(kbs, j, 1))
-        aff(sub(kb2, 8, 8), kbs, 1.0, 144.0)
-        ko = ts(S("ko", U, 16), kb2, 0.5, mul, 32.0, plus)
-        kb16 = aff(S("kb16", F, 8), kbs, 8.0, 512.0)
-        gg = gat(S("gg", F, 256), w2, ko)
-        msk = tt(S("msk", B, 128), sub(gg, 0, 128), sub(io, 1, 128), OP.is_equal)
-        hvm = tt(S("hvm", HF, 128), sub(gg, 128, 128), msk, mul)
+            act(S("jk%d" % (j % 2), B), V("qd", SW * (j // 4), 64), AF.Sign, -1.0, sub(jh, j % 4, 1), acc=sub(kbs, j, 1))
+        ko = ts(S("ko", U, 8), kbs, 0.5, mul, 32.0, plus)
+        msk = S("msk", B, 128)
+        for j in range(2):
+            gtt(sub(msk, 64 * j, 64), sub(w2, SW * j, SW), sub(ko, 4 * j, 4), i64, OP.is_equal)
+        hvm = gtt(S("hvm", HF, 128), sub(rt_, 64, SW), ko, msk, mul)
         vr = V("qd", 256, 128)
-        mms([(sub(vr, 0, 64), ones, sub(hvm, 0, 64), True, True), (sub(vr, 64, 64), osh, sub(hvm, 64, 64), True, True)])
-        sv = aff(S("sv%d" % t, F, 128), vr, 1.0, OFF)
-        send([(sub(sv, 0, 64), sub(zz, L + wn, 64), to1), (sub(sv, 64, 64), sub(zz, L + wn + 64, 64), to2)], "rv%d" % t, [sub(zz, L + wn, 128)])
+        mms(acc(sub(vr, 0, 64), [(sub(b1, 28, 128), sub(hvm, 0, 64))]) + acc(sub(vr, 64, 64), [(sub(b1, a, 128), sub(hvm, 64, 64)) for a in (12, 140)]))
+        sv = tt(S("sv%d" % (t + 1), F, 128), vr, svc, plus)
+        av = ws - 128
+        send([(sub(sv, 0, 64), sub(zz, av, 64), to1), (sub(sv, 64, 64), sub(zz, av + 64, 64), to2)], "rv%d" % t, [sub(zz, av, 128)])
         ql = V("qr1", 256, 8)
         wrap(ql, bim, msk, 8, last=False)
-        mms([(ql, fid(1), kb16, False, True)])
-        lno = cp(S("lno", U, 8), ql)
+        mms([(ql, f8i, kbs, False, True)])
+        lno = ts(S("lno", U, 8), ql, 512.0, plus)
         sd, sh = S("sd%d" % t, F, 256), S("sh%d" % t, F, 128)
-        gat(sub(sd, 0, 128), sub(cn, 2 * L, L + 8), lno)
-        gat(sub(sd, 128, 64), sub(an, 2 * L, L + 8), sub(lno, 4, 4))
-        gat(sub(sd, 192, 64), sub(an, 2 * L, L + 8), sub(lno, 0, 4))
+        gat(sub(sd, 0, 128), sub(cn, OLD, L + 8), lno)
+        gat(sub(sd, 128, 64), sub(an, OLD, L + 8), sub(lno, 4, 4))
+        gat(sub(sd, 192, 64), sub(an, OLD, L + 8), sub(lno, 0, 4))
         dma("S", sub(sh, 0, 128, slice(16, 128)), sub(sd, 64, 128, slice(0, 112)), 64)
         dma("S", sub(sh, 0, 128, slice(0, 16)), sub(sd, 64, 128, slice(112, 128)), 64)
-        send([(sub(sd, 0, 64), sub(cn, wn, 64), to1), (sub(sd, 192, 64), sub(an, wn, 64), to1),
-              (sub(sh, 0, 64), sub(cn, wn + 64, 64), to2), (sub(sh, 64, 64), sub(an, wn + 64, 64), to2)],
-             "rd%d" % t, [sub(cn, wn, 128), sub(an, wn, 128)])
+        send([(sub(sd, 0, 64), sub(cn, ARR, 64), to1), (sub(sd, 192, 64), sub(an, ARR, 64), to1),
+              (sub(sh, 0, 64), sub(cn, ARR + 64, 64), to2), (sub(sh, 64, 64), sub(an, ARR + 64, 64), to2)],
+             "rd%d" % t, [sub(cn, ARR, 128), sub(an, ARR, 128)])
     for o in ops:
         o["all"] = list(o["deps"]) + o["after"]
     return ops

@@ -1,5 +1,5 @@
 from concourse.bass import DstId, RemoteDMATransfer
-from concourse.mybir import AluOpType as OP, ActivationFunctionType as AF, AxisListType as AX
+from concourse.mybir import AluOpType as OP, ActivationFunctionType as AF
 
 H, H0, L, CAP, STEPS = 4096, 3072, 1024, 64, 3
 ARR, LB = 8, 640
@@ -10,12 +10,12 @@ BIG = 8192.0
 SW = 72
 F, B, I, U, HF = "float32", "bfloat16", "int32", "uint16", "float16"
 SIZE = {F: 4, B: 2, I: 4, U: 2, HF: 2}
-POOL = {F: ("pf", 4000), B: ("pb", 5800), I: ("pi", 600), U: ("pu", 640), HF: ("ph", 4000)}
+POOL = {F: ("pf", 4200), B: ("pb", 6600), I: ("pi", 400), U: ("pu", 640), HF: ("ph", 4000)}
 SCRATCH = {
     "kp": ("sbuf", [128, H], B), "dm": ("sbuf", [128, H], B), "sg": ("sbuf", [128, H], F), "ex": ("sbuf", [128, H], I),
     "wn": ("sbuf", [128, 6 * WW + 8], F), "zz": ("sbuf", [128, ZA + 2 * L + 8], F),
     "kk": ("sbuf", [128, L], F), "c1": ("sbuf", [128, L], F), "a1": ("sbuf", [128, L], F),
-    "mc": ("sbuf", [128, 2 * L], B), "ma": ("sbuf", [128, 2 * L], B), "eg": ("sbuf", [128, L], HF),
+    "mc": ("sbuf", [128, L], B), "ma": ("sbuf", [128, 4 * L], B), "eg": ("sbuf", [128, L], HF),
     "g2": ("sbuf", [128, L], HF), "cb": ("sbuf", [128, L], B), "ab": ("sbuf", [128, L], B), "c0": ("sbuf", [128, L], B),
 }
 for _d, (_n, _w) in POOL.items():
@@ -25,15 +25,17 @@ for _n in ("qr0", "qr1", "qa", "qb", "qc", "qd", "qe", "qm"):
 SEMAPHORES = ["eV", "eA", "eP", "eG"] + ["d%d" % k for k in range(60)] + ["rv0", "rv1", "rd0", "rd1", "rc0", "rc1"]
 
 CY, FAC, GA, SC, PEC, HOP, BIAS = 0.00083, 1.1, 1.45, 3.5, 0.00042, 0.14, 0.3
-CASES = [(1.0, 1.3, 3.0, 0.15, 0.08, 1.0, 0.5, 0.8), (1.0, 1.55, 3.8, 0.1, 0.1, 2.0, 0.0, 0.8),
-         (1.25, 1.55, 3.8, 0.2, 0.1, 2.0, 1.0, 1.0), (1.45, 1.9, 5.5, 0.15, 0.05, 0.5, 0.3, 1.2)]
-PIECES, LAST, TRIES, CLIMB, PIN = 2, 2, 150, 4800, 0.5
-NEG = [0, 0, 0]
-KS = 40
+CASES = [(1.0, 1.56, 3.8, 0.15, 0.08, 1.0, 0.5, 0.8, 1.0, 1.2, 1.0), (1.05, 1.2, 2.4, 0.2, 0.1, 2.5, 1.0, 0.8, 1.4, 1.7, 1.2),
+         (1.35, 1.8, 4.8, 0.15, 0.08, 1.5, 0.5, 1.15, 1.0, 1.2, 1.0), (1.2, 1.4, 3.2, 0.2, 0.08, 4.0, 1.5, 0.95, 1.2, 1.4, 1.1)]
+PIECES, LAST, TRIES, CLIMB, PIN, HEAT, SEED, MEAN, ANY, FAR, EARLY, LAM = 2, 2, 6, 190000, 1.5, 0.7, 7, 0.5, 2, 4, 0.1, 0.3
+SA = [1, 1, 2]
+KG = 1
+KORD = [[(0,), (2, 3)], [(2, 3), (0,)], [(2, 3), (0,)]]
+KS = [0, 32, 32]
 OFF = 6144.0
 
 
-def build(T, topo, core, FAC, GA, SC):
+def build(T, topo, core, FAC, GA, SC, GI=1.0, AC=1.0, PF=1.0):
     ops, hist, lay, top, nsem = [], {}, {}, {}, [0]
 
     def V(name, a=0, n=None, p=None, step=1):
@@ -137,6 +139,9 @@ def build(T, topo, core, FAC, GA, SC):
     def aff(o, x, mul, plus, off=None):
         return act(o, x, AF.Identity, mul, plus, off=off, alt=tsv(o, x, mul, OP.mult, plus, OP.add, off))
 
+    def to16(o, x, mul=1.0, plus=0.0):
+        return act(o, x, AF.Relu, mul, plus, alt=tsv(o, x, mul, OP.mult, plus, OP.add))
+
     def cp(o, x, both=False):
         v = (tv(o[6], 0.5 if two(o, x) else 1), lambda q: q.tensor_copy(o[3], x[3]))
         if both:
@@ -151,27 +156,33 @@ def build(T, topo, core, FAC, GA, SC):
         add({"V": (tv(o[6], GA), lambda q: q.tensor_tensor(o[3], win[3].indirect(off[3]), y[3], op))}, [win, off, y], [o])
         return o
 
-    def scat(win, off, x, silu=False, extra=0.0):
+    def scat(win, off, x, silu=None):
         if silu:
-            add({"A": (tv(x[6], SC) + extra, lambda q: q.activation(win[3].indirect(off[3]), x[3], AF.Silu))}, [off, x, sg], [win])
+            add({"A": (tv(x[6], SC), lambda q: q.activation(win[3].indirect(off[3]), x[3], AF.Silu))}, [off, x, silu], [win])
         else:
             add({"V": (tv(x[6], SC), lambda q: q.tensor_copy(win[3].indirect(off[3]), x[3]))}, [off, x], [win])
 
+    def iog(o, pat, base, cm):
+        kw = {} if SCRATCH[o[0]][2] == I else {"allow_small_or_imprecise_dtypes": True}
+        return (0.13 + 2 * o[6] * CY * FAC, lambda q: q.iota(o[3], pat, base, cm, **kw))
+
+    def iota(o, pat, base=0, cm=0):
+        add({"G": iog(o, pat, base, cm)}, [], [o])
+        return o
+
     def mset(o, c):
-        add({"V": (tv(o[6], 0.5 if two(o) else 1), lambda q: q.memset(o[3], c))}, [], [o])
+        alts = {"V": (tv(o[6], 0.5 if two(o) else 1), lambda q: q.memset(o[3], c))}
+        if SCRATCH[o[0]][2] != HF and o[5] == 1:
+            alts["G"] = iog(o, [[0, o[6]]], int(c), 0)
+        add(alts, [], [o])
         return o
 
     def scan(o, d0, d1, op1=OP.add):
         add({"V": (tv(o[6], 0.5 if two(o, d0, d1) else 1), lambda q: q.tensor_tensor_scan(o[3], d0[3], d1[3], 0.0, OP.mult, op1))}, [d0, d1], [o])
         return o
 
-    def iota(o, pat, base=0, cm=0):
-        kw = {} if SCRATCH[o[0]][2] == I else {"allow_small_or_imprecise_dtypes": True}
-        add({"G": (0.13 + 2 * o[6] * CY * FAC, lambda q: q.iota(o[3], pat, base, cm, **kw))}, [], [o])
-        return o
-
-    def pick(o, x, pat, base):
-        add({"G": (0.17 + 2 * o[6] * CY * FAC, lambda q: q.affine_select(o[3], x[3], pat, OP.is_equal, 0.0, base, 1))}, [x], [o])
+    def pick(o, x, pat, base, op=OP.is_equal):
+        add({"G": (0.17 + 2 * o[6] * CY * FAC, lambda q: q.affine_select(o[3], x[3], pat, op, 0.0, base, 1))}, [x], [o])
         return o
 
     def mms(lst):
@@ -180,7 +191,7 @@ def build(T, topo, core, FAC, GA, SC):
             for o, l, x, s0, s1 in lst:
                 r = q.matmul(o[3], l[3], x[3], s0, s1)
             return r
-        add({"P": (0.05 + sum(max(64, m[0][6]) * PEC * FAC * (SIZE[SCRATCH[m[1][0]][2]] // 2) ** 2 + 0.01 for m in lst), emit)}, [v for m in lst for v in m[1:3]], [m[0] for m in lst])
+        add({"P": (0.05 + sum(max(64, m[0][6]) * PEC * PF * FAC * (SIZE[SCRATCH[m[1][0]][2]] // 2) ** 2 + 0.01 for m in lst), emit)}, [v for m in lst for v in m[1:3]], [m[0] for m in lst])
 
     def acc(o, terms, first=True, last=True):
         return [(o, l, x, first and j == 0, last and j == len(terms) - 1) for j, (l, x) in enumerate(terms)]
@@ -192,8 +203,9 @@ def build(T, topo, core, FAC, GA, SC):
     def dma(eng, o, x, kb, acc=False):
         s = "d%d" % nsem[0]
         nsem[0] += 1
+        kb *= AC if acc else 1.0
         kw = {"accum_op": OP.add, "max_dma_last_dim": 8192} if acc else {}
-        add({eng: (1.0 if eng == "G" else 0.1, lambda q: q.dma_start(ap(o), ap(x), **kw))},
+        add({e: (GI if e == "G" else 0.1, lambda q: q.dma_start(ap(o), ap(x), **kw)) for e in ("G" if eng == "G" else "SA")},
             [v for v in (x, o if acc else None) if isv(v)], [o] if isv(o) else [], lat=1.6 + kb / 600.0, sem=(s, 16))
         ops[-1]["pipe"] = kb / 600.0
 
@@ -208,64 +220,80 @@ def build(T, topo, core, FAC, GA, SC):
             rid, pid, _ = topo.addr(to)
             trs.append(RemoteDMATransfer(dst_ids=[DstId(rid=rid, pnc=pid)], dma_engine_mask=m, remote_sem=T.sem[rsem], src=src[3], dst=dst[3]))
             tot += w
-        k = add({"G": (1.0, lambda q: q.remote_dma_fused(trs, local_sem=T.sem[s]))}, [i[0] for i in items], [], lat=1.5, sem=(s, tot))
+        k = add({"G": (GI, lambda q: q.remote_dma_fused(trs, local_sem=T.sem[s]))}, [i[0] for i in items], [], lat=1.5 + (2.0 if rsem == "rc0" else 0.0), sem=(s, tot))
         ops[k]["remote"] = True
         add({}, [], land, lat=0.3, sem=(rsem, tot), after=[k])
 
     rank, n = T.rank_of(core), len(T.cores)
     to1, to2 = T.cores[(rank + 1) % n], T.cores[(rank + 2) % n]
-    kp, dm, sg, ex, zz, mc, ma = [V(x) for x in ("kp", "dm", "sg", "ex", "zz", "mc", "ma")]
+    kp, dm, sg, ex, zz, mc = [V(x) for x in ("kp", "dm", "sg", "ex", "zz", "mc")]
     kk, c1, a1, eg, g2, cb, ab, c0 = [V(x) for x in ("kk", "c1", "a1", "eg", "g2", "cb", "ab", "c0")]
-    nl, mr = sub(mc, 0, L), sub(mc, L, L)
+    nl = mc
     wc, wa = [V("wn", 2 * t * WW, WW + 8) for t in range(3)], [V("wn", (2 * t + 1) * WW, WW + 8) for t in range(3)]
     qr = [V("qr0"), V("qr1")]
     HV = [(0, 512), (512, 512)]
     PV = [(j * L // PIECES, L // PIECES) for j in range(PIECES)]
     mul, plus, minus = OP.mult, OP.add, OP.subtract
 
-    mset(sub(ex, 0, 2 * L), 0)
-    iota(sub(ex, 2 * L, L), [[1, L]])
+    mset(sub(ex, 0, L), 0)
+    cp(sub(ex, L, L), sub(ex, 0, L), True)
+    mset(sub(ex, 2 * L, L), 0)
     p4 = S("p4", I)
     dma("S", ab, T.amp[:], 256)
-    dma("A", cb, T.cro[:], 256)
+    dma("S", cb, T.cro[:], 256)
     for j in range(4):
-        dma("SA"[j % 2], sub(p4, 16 * j, 16), T.place[j % 2::2, 512 * (j // 2):512 * (j // 2) + 512], 30)
-    dma("S", V("ex", 0, H0, slice(0, 128, 16)), T.lf[:, 0:H0], 300)
-    dma("A", V("ex", 0, H0, slice(8, 128, 16)), T.rt[:, 0:H0], 300)
+        dma("S", sub(p4, 16 * j, 16), T.place[j % 2::2, 512 * (j // 2):512 * (j // 2) + 512], 30)
+    for a in (0, 2 * L, L):
+        dma("S", V("ex", a, L, slice(0, 128, 16)), T.lf[:, a:a + L], 100)
+        dma("S", V("ex", a, L, slice(8, 128, 16)), T.rt[:, a:a + L], 100)
     dma("S", dm, T.dam[:], 1000)
+    ops[-1]["after"] += [len(ops) - 3, len(ops) - 2]
     dma("S", kp, T.kap[:], 1000)
     for j, o in enumerate(ops):
         o["first"] = 1000.0 - j
 
     pi = iota(S("pi", I, 1), [[0, 1]], 0, 1)
+    pc = iota(C("pc"), [[0, 1]], 0, 1)
     io = iota(S("io", F, 272), [[1, 272]])
     qg = iota(S("qg", F, 128), [[16, 8], [0, 16]])
     l16 = iota(S("l16"), [[16, 64]])
     iota(sub(ex, H0, L), [[1, L]], H0)
-    dma("G", sub(wa[0], OLD, L), T.amp[:], 512)
-    mset(V("wn", 0, 6 * WW + 1, None, WW), 0.0)
+    mset(V("wn", 0, 6 * WW + 1, None, 2 * WW), -8.0)
+    mset(V("wn", WW, 4 * WW + 1, None, 2 * WW), 0.0)
     all1 = mset(S("all1", B, 512), 1.0)
-    one = mset(S("one", HF, SW), 1.0)
-    one64, one1 = sub(one, 0, 64), sub(one, 0, 1)
+    rs = mset(S("rs", B, 3 * SW), 1.0)
+    mset(every(rs, SW, SW, 2), 0.0)
+    one64, one1 = sub(all1, 0, 64), sub(all1, 0, 1)
+    nil = S("nil", B, 4 * SW + 128)
+    mset(sub(nil, 0, 4 * SW + 64), 0.0)
+    seg = sub(nil, 0, 3 * SW)
+    dis, cdc = sub(nil, 3 * SW, 65), sub(nil, 4 * SW, 128)
+    mset(sub(cdc, 64, 64), -3840.0)
+    qb_ = S("qbm", B, 144)
+    mset(sub(qb_, 0, 3), 0.0)
+    zeros = mset(S("zeros", HF, 384), 0.0)
+    kd0, kq0, kt0 = [sub(zeros, 128 * j, 128) for j in range(3)]
     ici = ts(S("ici", I, 1), pi, 15, OP.bitwise_and)
     ic = cp(C("ic"), ici)
-    pc = cp(C("pc"), pi)
-    g16 = tt(C("g16"), pc, ic, minus)
+    g16 = aff(C("g16"), ic, -1.0, pc)
     lid = aff(S("lid"), l16, 1.0, ic)
     nlid = aff(S("nlid"), lid, -1.0, 0.0)
-    lidh, lidb, lidk = [aff(S(x, HF), lid, 1.0, w) for x, w in (("lidh", 0.0), ("lidb", float(LB)), ("lidk", 1024.0))]
+    lidh = cp(S("lidh", HF), lid, True)
     jh = aff(S("jh", F, 4), sub(lid, 0, 4), 1.0, 0.5)
     i128, i64 = sub(io, 0, 128), sub(io, 0, 64)
-    b1 = ts(S("b1", B, 272), io, aff(C("g31"), g16, 1.0, 31.0), OP.is_equal)
+    b1 = ts(S("b1", B, 272), io, -31.0, plus, g16, OP.is_equal)
 
     def sel(name, w):
         return aff(S(name, B, 144), sub(b1, 16, 144), w, 0.0)
     e16 = ts(S("e16", F, 16), sub(io, 0, 16), ic, OP.is_equal)
-    bm1, bm2, bim, bx0, bx8 = sel("bm1", -1.0), sel("bm2", -2.0), sel("bim", ic), sel("bx0", sub(e16, 0, 1)), sel("bx8", sub(e16, 8, 1))
+    bim, bx0, bx8 = [sel("bs%d" % j, w) for j, w in enumerate((ic, sub(e16, 0, 1), sub(e16, 8, 1)))]
+    bw = sub(b1, 16, 144)
     ones = ts(S("ones", B, 128), qg, g16, OP.is_equal)
-    tri = tt(S("tri", B, 128), ts(S("tri0", B, 128), i128, pc, OP.is_le, -1.0, mul), ones, mul)
-    gn = tt(C("gn"), ts(C("gn0"), g16, 112.0, OP.is_ge, -128.0, mul), g16, plus)
-    osh = ts(S("osh", F, 128), qg, aff(C("gn2"), gn, 1.0, 16.0), OP.is_equal, 0.5, mul)
+    tri = pick(S("tri", B, 128), aff(S("tri0", B, 128), ones, -1.0, 0.0), [[-1, 128]], 0, OP.is_ge)
+    qn = S("qn", F, 128)
+    iota(sub(qn, 0, 16), [[0, 16]], 112)
+    iota(sub(qn, 16, 112), [[16, 7], [0, 16]])
+    osh = ts(S("osh", F, 128), qn, g16, OP.is_equal, 0.5, mul)
     onh = aff(S("onh", F, 128), ones, 0.5, 0.0)
     row0 = ts(S("row0", B, 128), ones, sub(e16, 0, 1), mul, -1.0, mul)
     i12 = pick(S("i12", B, 152), sub(all1, 0, 152), [[-1, 152]], 12)
@@ -276,42 +304,42 @@ def build(T, topo, core, FAC, GA, SC):
     mu = [aff(S("mu%d" % u, B, 152), i12, sub(e4, u, 1), 0.0) for u in range(4)]
     mu1d, mu2n = aff(S("mu1d", B, 152), mu[1], 2.0, 0.0), aff(S("mu2n", B, 152), mu[2], -1.0, 0.0)
     mmq = pick(S("mmq", B, 512), all1, [[-1, 4], [-16, 8], [-4, 16]], 0)
-    qb_ = S("qbm", B, 144)
-    mset(sub(qb_, 0, 3), 0.0)
     pick(sub(qb_, 3, 128), sub(all1, 0, 128), [[-16, 8], [-1, 4], [1000, 4]], 0)
-    rs = mset(S("rs", B, 3 * SW), 1.0)
-    mset(every(rs, SW, SW, 2), 0.0)
-    seg = mset(S("seg", B, 3 * SW), 0.0)
-    dis = mset(S("dis", B, 65), 0.0)
-    zeros = mset(S("zeros", HF, 384), 0.0)
-    kd0, kq0, kt0 = [sub(zeros, 128 * j, 128) for j in range(3)]
-    rt_ = S("rt", I, 128 + 8)
-    mset(sub(rt_, 128, 8), 0)
-    cdc, c84 = mset(S("cdc", HF), -3840.0), mset(S("c84", HF, 65), -1984.0)
-    cj = [mset(S("cj%d" % t, HF), 1792.0 + BIG + 128 * (1 - t)) for t in range(2)]
-    kc = S("kc", HF, 3)
-    for j, w in enumerate((1024.0, -1536.0, 448.0)):
+    rt_ = S("rt", I, 128)
+    c84 = mset(S("c84", B, 64), -1984.0)
+    idq = ts(S("idq", HF, 256), sub(io, 0, 256), aff(C("id0"), sub(e4, 1, 1), 4.0, 0.0), mul, ts(C("id1"), ic, 1020.0, plus, sub(e4, 1, 1), mul), plus)
+    xf = S("xf", HF, 192)
+    own = aff(sub(xf, 128, 64), lid, 1.0, LB - 1024.0)
+    cj = [mset(S("cj%d" % t, B), 1792.0 + BIG + 128 * (1 - t)) for t in range(2)]
+    kc = S("kc", B, 3)
+    for j, w in enumerate((-2048.0, -1536.0, 448.0)):
         mset(sub(kc, j, 1), w)
-    svc = ts(S("svc", F, 128), aff(S("sv0", F, 128), i128, 1.0, 1800.0 + H0), aff(C("n3"), sub(e16, 3, 1), -1.0, 1.0), mul, OFF - H0, plus)
 
     pt = S("pt")
     pf = cp(S("pf0"), p4)
     add({"V": (tv(64), lambda q: q.transpose(pt[3], pf[3]))}, [pf], [pt])
     so = S("so", U, 192)
-    s1, hoff, s2 = [sub(so, 64 * j, 64) for j in range(3)]
-    cp(hoff, pt)
+    hoff, s1, s2 = [sub(so, 64 * j, 64) for j in range(3)]
+    to16(hoff, pt)
     rf = S("rf", HF, 192)
     rfo, fr, ngo = [sub(rf, 64 * j, 64) for j in range(3)]
     ts(ngo, pt, float(H0), OP.is_ge)
     for j, (a, w) in enumerate(HV):
         act(sub(nl, a, w), sub(ab, a, w), AF.Sign, -1.0, alt=tsv(sub(nl, a, w), sub(ab, a, w), 0.0, OP.is_gt, -1.0, mul))
-        mms(acc(qr[j], [(im, sub(nl, a, w))]))
-        tt(sub(c0, a, w), sub(cb, a, w), qr[j], mul)
-        ts(sub(mr, a, w), sub(c0, a, w), 0.0, OP.is_lt)
+        mms(acc(qr[j], [(km1, all1), (km1, sub(nl, a, w)), (ip, sub(cb, a, w))]))
+        cp(sub(c0, a, w), qr[j], True)
+        ts(V("ma", a, w), sub(c0, a, w), 0.0, OP.is_lt, -8.0, mul)
     dma("G", sub(wc[0], OLD, L), c0, 512)
+    dma("G", sub(wa[0], OLD, L), T.amp[:], 512)
     for j in range(8):
         act(sub(sg, 512 * j, 512), sub(dm, 512 * j, 512), AF.Sigmoid, extra=1.3 if j == 0 else 0.0)
-    mc_, n0a, n0b, nfc, nfa = [V("qm", j, 1) for j in (0, 1, 2, 8, 9)]
+        if j:
+            ops[-1]["after"].append(len(ops) - 1 - j)
+    sv0 = S("sv0", F, 128)
+    add({"A": (tv(128) + 1.5, lambda q: q.activation(sv0[3], i128[3], AF.Silu, bias=1800.0 + H0))}, [i128, sg], [sv0])
+    svc = ts(S("svc", F, 128), sv0, aff(C("n3"), sub(e16, 3, 1), -1.0, 1.0), mul, OFF - H0, plus)
+    mc_, nfc, nfa = [V("qm", j, 1) for j in (0, 8, 9)]
+    n0a, n0b = V("qe", 448, 1), V("qe", 449, 1)
     de, do, sf = [sub(seg, SW * j, SW) for j in range(3)]
     scs = S("scs", B, 3 * SW)
     ce, co, cf = [sub(scs, SW * j, SW) for j in range(3)]
@@ -320,72 +348,68 @@ def build(T, topo, core, FAC, GA, SC):
     for t in range(STEPS):
         cw, aw, cn, an = wc[t], wa[t], wc[(t + 1) % 3], wa[(t + 1) % 3]
         c, A = (c0, ab) if t == 0 else (sub(cw, OLD, L), sub(aw, OLD, L))
-        ws = ZC - 128 * t
+        ws, ks = ZC - 128 * t, KS[t]
+        ma, mn = V("ma", 2 * L * (t % 2), 2 * L), V("ma", 2 * L * (1 - t % 2), 2 * L)
         hl, u = V("qa", 0, 64), V("qb", 0, 64)
-        wrap(hl, bm1, nl, 64)
+        wrap(hl, bw, nl, 64)
+        hs = aff(S("hs", HF), hl, -2.0 if t else -4.0, 32.0 if t else 0.0)
         mms(acc(u, [(km1, ngo)], last=False))
-        wrap(u, bm1, nl, 64, False, False)
-        wrap(u, bm2, mr, 64, False)
+        wrap(u, bw, sub(ma, 0, L), 64, False, False)
+        mms(acc(u, [(im, hs)], first=False))
         if t == 0:
             ts(sub(sf, 0, 64), hl, 0.0, OP.is_equal)
             cp(fr, sub(sf, 0, 64), True)
             scan(cf, sub(rs, 2 * SW, SW), sf)
             pf_ = V("qd", 0, 64)
             mms(acc(pf_, [(tri, sub(sf, 0, 64)), (ones, sub(cf, 0, 64)), (km1, sub(sf, 0, 64)), (km1, sub(sf, 0, 64))]))
-            mms(acc(nfc, [(ones, sub(cf, 64, 1)), (km1, one1), (km1, one1)]) + acc(nfa, [(ones, sub(cf, KS - 1, 1)), (km1, one1), (km1, one1)]))
+            mms(acc(nfc, [(ones, sub(cf, 64, 1)), (ip, sub(kc, 0, 1))]) + (acc(nfa, [(ones, sub(cf, ks - 1, 1)), (ip, sub(kc, 0, 1))]) if ks else []))
             cp(rfo, pf_, True)
         for a, w in PV:
             aff(sub(eg, a, w), ex, 1.0, -2048.0, sub(hoff, a // 16, w // 16))
         xl_, xr_ = wrap(V("qc", 0, 64), bx0, eg, 64), wrap(V("qc", 64, 64), bx8, eg, 64)
-        xo = ts(S("xo", U, 128), V("qc", 0, 128), 2048.0, plus)
+        xo = to16(S("xo", U, 128), V("qc", 0, 128), 1.0, 2048.0)
         xlo, xro = sub(xo, 0, 64), sub(xo, 64, 64)
-        xf = cp(S("xf", HF, 128), V("qc", 0, 128), True)
-        xl, xr = sub(xf, 0, 64), sub(xf, 64, 64)
-        jf = aff(S("jf", HF, 128), xf, 1.0 / 32, 1164.0 - 15.5 / 32)
+        cp(sub(xf, 0, 128), V("qc", 0, 128), True)
+        jf = aff(S("jf", HF, 128), sub(xf, 0, 128), 1.0 / 32, 1164.0 - 15.5 / 32)
         jl, jr = sub(jf, 0, 64), sub(jf, 64, 64)
-        for a, w in HV:
-            aff(sub(ma, a, w), sub(mr, a, w), -8.0, 0.0)
-            aff(sub(ma, L + a, w), sub(mr, a, w), 8.0, -8.0)
-        for a, w in PV:
-            o = (a // 16, w // 16)
-            gtt(sub(kk, a, w), kp, sub(hoff, *o), sub(c, a, w), mul)
-            act(sub(cw, LB + a, w), sub(kk, a, w), AF.Relu, 2.0, alt=tsv(sub(cw, LB + a, w), sub(kk, a, w), 2.0, mul, 0.0, OP.max))
-            if NEG[t] > a // w:
-                act(sub(cw, LB + L + a, w), act(sub(c1, a, w), sub(kk, a, w), AF.Relu, -2.0), AF.Copy, -1.0)
-            else:
-                ts(sub(cw, LB + L + a, w), sub(kk, a, w), 2.0, mul, 0.0, OP.min)
-            gtt(sub(aw, LB + a, w), sg, sub(xlo, *o), sub(A, a, w), mul)
-            gtt(sub(aw, LB + L + a, w), sg, sub(xro, *o), sub(A, a, w), mul)
-        dma("G", nl, mr, 500, True)
-        dma("G", sub(cw, LB, 2 * L), mc, 1400, True)
-        dma("G", sub(aw, LB, 2 * L), ma, 1400, True)
+        aff(sub(ma, L, L), sub(ma, 0, L), -1.0, -8.0)
+        gtt(kk, kp, hoff, c, mul)
+        for j in range(2):
+            aff(sub(cw, LB + j * L, L), kk, 2.0, 2.0 * j - 1)
+        dma("G", sub(cw, LB, 2 * L), ma, 1400, True)
+        gtt(sub(aw, LB, L), sg, xlo, A, mul)
+        gtt(sub(aw, LB + L, L), sg, xro, A, mul)
+        for j in range(SA[t]):
+            w = 2 * L // SA[t]
+            dma("G", sub(aw, LB + j * w, w), sub(ma, j * w, w), 1400 // SA[t], True)
         qe = V("qe", 0, 128)
         dj, jx, qp, qj, qz = every(qe, 0, 2, 64), every(qe, 1, 2, 64), V("qe", 128, 64), V("qe", 192, 64), V("qe", 256, 64)
         mms(acc(qp, [(im, rfo), (km1, fr), (km1, fr), (km1, fr)]) + (acc(qz, [(kp1, fr), (kp1, fr)]) if t else []))
         p0 = tt(S("p0"), qp, nlid, OP.min)
         mms(acc(dj, [(ip, jl), (im, jr)]))
-        lw, capv, par = every(kd0, 1, 2, 64), every(kq0, 1, 2, 64), every(S("kq1", HF, 128), 0, 2, 64)
+        kq1 = S("kq1", HF, 128)
+        lw, capv, par = every(kd0, 1, 2, 64), every(kq0, 1, 2, 64), every(kq1, 0, 2, 64)
         if t == 0:
             key = tt(S("key", HF), ts(S("cap0", HF), dj, 0.0, OP.not_equal), fr, OP.is_gt)
         else:
             ts(capv, dj, 0.0, OP.is_equal, 2047.0, plus)
             tt(jx, qz, jr, OP.max)
             cnt = sub(S("cnt", F, 16), 8 * (t - 1), 8)
-            mms([(V("qm", 0, 3), ip, kc, True, False), (mc_, onh, sub(cnt, 0, 1), False, False), (n0a, onh, sub(cnt, 0, 1), False, False),
-                 (n0b, onh, sub(cnt, 0, 1), False, False), (mc_, osh, sub(cnt, 4, 1), False, True)])
+            mms([(V("qe", 448, 2), ip, sub(kc, 1, 2), True, False), (n0a, onh, sub(cnt, 0, 1), False, False), (n0b, onh, sub(cnt, 0, 1), False, True)])
+            mms(acc(mc_, [(kp1, one1)], last=False))
+            mms(acc(mc_, [(onh, sub(cnt, 0, 1)), (osh, sub(cnt, 4, 1))], first=False))
             isa = ts(S("isa", HF), rfo, 2048.0, plus, mc_, OP.is_lt)
             aj0 = ts(S("aj0", HF), rfo, n0a, OP.is_ge, n0b, mul)
-        au = act(S("au"), u, AF.Abs)
-        ts(lw, u, 0.0, OP.is_ge)
-        tt(sub(dis, 0, 64), au, hl, OP.is_lt)
+        au = act(S("au"), u, AF.Abs, 1.0, 128.0)
+        ts(lw, u, -128.0, OP.is_ge)
+        tt(sub(dis, 0, 64), au, hs, OP.is_lt)
         scd = scan(S("scd", B, 65), sub(rs, 0, 65), dis)
         rd, ndc, nda = V("qa", 0, 64), V("qa", 64, 1), V("qa", 72, 1)
-        mms(acc(V("qa", 0, 65), [(tri, dis), (km1, dis), (km1, dis), (ones, scd)], last=False) + acc(ndc, [(km1, one1), (km1, one1)], first=False)
-            + acc(nda, [(ones, sub(scd, KS - 1, 1)), (km1, one1), (km1, one1)]))
+        mms(acc(V("qa", 0, 65), [(tri, dis), (km1, dis), (km1, dis), (ones, scd)], last=False) + acc(ndc, [(ip, sub(kc, 0, 1))], first=False)
+            + (acc(nda, [(ones, sub(scd, ks - 1, 1)), (ip, sub(kc, 0, 1))]) if ks else []))
 
         def cmp(o, x, sign, y, op):
             return ts(o, x, y, op) if t == 0 else ts(o, x, mc_, sign, y, op)
-        kq1 = S("kq1", HF, 128)
         if t:
             scan(kq1, kd0, qe)
         cmp(par, rd, plus, nfc, OP.is_lt)
@@ -395,30 +419,32 @@ def build(T, topo, core, FAC, GA, SC):
             mms(acc(qj, [(ip, cj[t - 1]), (ip, rfo), (im, aj0), (bm, isa)]))
             pre = tt(S("pre"), qj, tw, OP.min)
         fq = [V("qd", 64 * j, 64) for j in range(3)]
-        mms(acc(fq[0], [(ip, xl), (im, xa), (ip, xb)]) + acc(fq[1], [(ip, lidb), (km1, one64), (kp1, ngo), (bm, fr), (km1, lw)])
-            + acc(fq[2], [(ip, xr), (bm, fr), (ip, xa), (im, xb)]))
+        mms([(V("qd", 0, 192), ip, xf, True, False)] + [(fq[j], l, x, False, False) for j, l, x in ((1, bm, fr), (2, bm, fr), (2, kp1, ngo))])
+        mms([(fq[j], l, x, False, j == 2) for j, l, x in ((0, im, xa), (0, ip, xb), (1, ip, xa), (1, im, xb), (2, km1, lw))])
         fc = cp(S("fc", HF, 192), V("qd", 0, 192), True)
-        qw = V("qd", 0, 256)
-        code = [key, lidk, sub(fc, 64, 64), sub(fc, 0, 64)]
-        mms(sum([acc(every(qw, u, 4, 64), [(sub(mu[u], 12 - 4 * (f - u), 128), code[f]) for f in (1, 3, 2, 0)]) for u in range(4)], []))
+        qw = V("qr1", 0, 256)
+        code = [key, None, sub(fc, 128, 64), sub(fc, 0, 64)]
+        mms([(qw, ip, idq, True, False)])
+        for fs in KORD[t]:
+            mms([(every(qw, u, 4, 64), sub(mu[u], 12 - 4 * (f - u), 128), code[f], False, fs is KORD[t][-1] and f == fs[-1] and u == 3) for f in fs for u in range(4)])
         wsb = cp(S("wsb", HF, 256), qw, True)
         for j in range(2):
             mms([(every(qr[j], r, 4, 128), sub(mmq, 128 * r, 128), sub(wsb, 128 * j, 128), True, True) for r in range(4)])
             aff(sub(zz, ZC + 512 * j, 512), qr[j], 1.0, OFF)
         posf = tt(S("posf"), rd, p0, OP.min)
-        pos = ts(S("pos", U), posf, 2048.0, plus)
-        scat(sub(zz, ZA, 2 * L + 8), sub(pos, 0, KS), sub(zz, ZC, 16 * KS), True, 1.5 if t == 0 else 0.0)
-        scat(sub(zz, ZB, 2 * L), sub(pos, KS, 64 - KS), sub(zz, ZC + 16 * KS, L - 16 * KS))
+        pos = to16(S("pos", U), posf, 1.0, 2048.0)
+        if ks:
+            scat(sub(zz, ZA, 2 * L + 8), sub(pos, 0, ks), sub(zz, ZC, 16 * ks), sv0)
+        scat(sub(zz, ZB, 2 * L + (0 if ks else 8)), sub(pos, ks, 64 - ks), sub(zz, ZC + 16 * ks, L - 16 * ks))
         qv = aff(S("qv", HF), posf, -1.0, 0.0) if t == 0 else ts(S("qv", HF), posf, mc_, plus, -1.0, mul)
-        j1 = cmp(S("j1", HF), rd, plus, nfa, OP.is_lt)
-        j2 = cmp(S("j2", HF), rfo, minus, nda, OP.is_lt)
+        js = [cmp(S("j1", HF), rd, plus, nfa, OP.is_lt), cmp(S("j2", HF), rfo, minus, nda, OP.is_lt)] if ks else []
         nba = cmp(S("nba", HF), rfo, minus, ndc, OP.is_ge)
         pp = V("qb", 0, 64)
-        mms(acc(pp, [(ip, qv), (kp1, j1), (kp1, j1), (kp1, j2), (kp1, j2), (bp, par), (bm, nba)] + ([(bm, isa)] if t else [])))
-        idx = ts(S("idx", U), tt(S("idf"), pp, pre, OP.max), float(ZC - ws), plus)
+        mms(acc(pp, [(ip, qv), (bp, par), (bm, nba)] + [(kp1, x) for x in js + js] + ([(bm, isa)] if t else [])))
+        idx = to16(S("idx", U), tt(S("idf"), pp, pre, OP.max), 1.0, float(ZC - ws))
         for a, w in PV:
             aff(sub(g2, a, w), sub(zz, ws, ZA + 2 * L + 8 - ws), 1.0, -OFF, sub(idx, a // 16, w // 16))
-        mms(acc(V("qe", 320, 64), [(ip, lidb), (kp1, lw), (bp, par), (bm, one64)]) + acc(V("qe", 384, 64), [(bp, one64), (bm, fr), (bm, nba)]))
+        mms(acc(V("qe", 320, 64), [(ip, own), (kp1, one64), (kp1, lw), (bp, par), (bm, one64)]) + acc(V("qe", 384, 64), [(bp, one64), (bm, fr), (bm, nba)]))
         o2 = cp(S("o2", F, 128), V("qe", 320, 128), True)
         q4 = V("qr0", 0, 256)
         mms(acc(q4, [(sub(qb_, 3 - r, 128), every(g2, r, 4, 256)) for r in range(4)]))
@@ -429,38 +455,61 @@ def build(T, topo, core, FAC, GA, SC):
         pk, qt = V("qa", 0, 64), V("qb", 0, 128)
         pd = every(qt, 0, 2, 64)
         mms(acc(pk, [(ip, key)] if t == 0 else [(im, key), (bp, fr), (bp, nba), (bp, isa)], last=False))
-        mms((acc(every(qt, 1, 2, 64), [(ip, lidh)]) if t == 1 else []) + acc(pd, [(im, lidk)], last=False))
+        mms((acc(every(qt, 1, 2, 64), [(ip, lidh)]) if t == 1 else []) + acc(pd, [(im, lidh), (km1, one64)], last=False))
         mms(acc(pk, back(mu[0], 0), first=False))
         mms(acc(pd, back(mu[1], 1), first=False))
-        mq = [V("qc", 64 * j, 64) for j in range(3)]
-        mms(acc(mq[0], [(ip, cdc), (bm, nba), (bm, nba)] + back(mu1d, 1) + back(mu2n, 2)) + acc(mq[1], [(bm, nba)] + back(mu[3], 3)))
+        mq = [V("qc", 0, 64), V("qc", 64, 64), V("qe", 0, 64)]
+        end = t == STEPS - 1
+        if end:
+            mq[0] = V("qd", 0, 64)
+            mms(acc(mq[0], [(bm, nba)], last=False))
+            mms(acc(mq[0], back(mu[3], 3), False))
+            tt(sub(rt_, 0, 64), mq[0], sub(fc, 64, 64), OP.max)
+            mms(acc(mq[1], [(ip, sub(cdc, 64, 64)), (bm, nba), (bm, nba)], last=False))
+        else:
+            mms([(V("qc", 0, 128), ip, cdc, True, False)] + [(mq[j], bm, nba, False, False) for j in (0, 1, 1)])
+        mms(acc(mq[2], [(kp1, one64), (kp1, one64)], last=False))
+        mms(([] if end else acc(mq[0], back(mu[3], 3), False, False)) + acc(mq[1], back(mu1d, 1) + back(mu2n, 2), False))
         f8 = ts(S("f8"), pk, 0.5, OP.is_lt, BIG, mul) if t == 0 else ts(S("f8"), pk, BIG, OP.is_equal, BIG, mul)
-        tt(sub(rt_, 0, 128), V("qc", 0, 128), sub(fc, 64, 128), OP.max)
-        mms(acc(mq[2], [(kp1, one64), (kp1, one64)] + back(mu[2], 2)))
+        if end:
+            tt(sub(rt_, 64, 64), mq[1], sub(fc, 128, 64), OP.max)
+        else:
+            tt(rt_, V("qc", 0, 128), sub(fc, 64, 128), OP.max)
+        mms(acc(mq[2], back(mu[2], 2), False))
         eb = tt(V("qm", 64, 64), f8, pd, mul)
         r2 = tt(S("r2"), mq[2], sub(o2, 0, 64), OP.max)
         upn = tt(V("qm", 128, 64), eb, sub(o2, 64, 64), OP.min)
-        h = sub(rt_, 64, 64)
+        h = sub(rt_, 0, 64)
         if t < STEPS - 1:
-            ts(sub(so, 0, 128), sub(rt_, 0, 128), 2048.0, plus)
+            to16(sub(so, 0, 128), rt_, 1.0, 2048.0)
         else:
-            ts(s1, tt(S("s1f"), upn, sub(rt_, 0, 64), plus), 2048.0, plus)
-            ts(hoff, h, 2048.0, plus)
-        cp(s2, tt(S("s2f"), eb, r2, OP.min))
+            to16(s1, tt(S("s1f"), upn, sub(rt_, 64, 64), plus), 1.0, 2048.0)
+            to16(hoff, h, 1.0, 2048.0)
+        to16(s2, tt(S("s2f"), eb, r2, OP.min))
         c, A = sub(cn, OLD, L), sub(an, OLD, L)
         cwin, awin = sub(cw, 0, WW), sub(aw, 0, WW)
         for a, w in (PV if t < STEPS - 1 else [(j * L // LAST, L // LAST) for j in range(LAST)]):
             o = (a // 16, w // 16)
-            act(sub(a1, a, w), awin, AF.Relu, off=sub(s1, *o), alt=tsv(sub(a1, a, w), awin, 0.0, OP.max, off=sub(s1, *o)))
-            gtt(sub(A, a, w), awin, sub(s2, *o), sub(a1, a, w), OP.max)
+            if end:
+                act(sub(a1, a, w), awin, AF.Relu, off=sub(s1, *o), alt=tsv(sub(a1, a, w), awin, 0.0, OP.max, off=sub(s1, *o)))
+                gtt(sub(A, a, w), awin, sub(s2, *o), sub(a1, a, w), OP.max)
+            elif a == 0:
+                act(a1, awin, AF.Relu, off=s1, alt=tsv(a1, awin, 0.0, OP.max, off=s1))
+                gtt(A, awin, s2, a1, OP.max)
             gat(sub(c1, a, w), cwin, sub(s1, *o))
-            gtt(sub(c, a, w), cwin, sub(s2, *o), sub(c1, a, w), plus)
+            gtt(sub(c, a, w), cwin, sub(s2, *o), sub(c1, a, w), OP.max)
             if t < STEPS - 1:
-                act(sub(nl, a, w), sub(A, a, w), AF.Sign, -1.0, alt=tsv(sub(nl, a, w), sub(A, a, w), 0.0, OP.is_gt, -1.0, mul))
-                ts(sub(mr, a, w), sub(c, a, w), 0.0, OP.is_lt)
+                act(sub(nl, a, w), sub(c, a, w), AF.Sign, -1.0, -2.0)
+                ts(sub(mn, a, w), sub(c, a, w), 0.0, OP.is_lt, -8.0, mul)
             else:
-                dma("S", T.yc[:, a:a + w], sub(c, a, w), w // 2)
-                gtt(sub(kk, a, w), kp, sub(hoff, *o), sub(A, a, w), mul)
+                lv = aff(V("qr%d" % (a // w % 2), 0, w), sub(A, a, w), -BIG, 0.0)
+                dma("S", T.yc[:, a:a + w], tt(sub(a1, a, w), sub(c, a, w), lv, OP.max), w // 2)
+                if a // w < KG:
+                    kq = V(("qc", "qd")[a // w % 2], 0, w)
+                    mms(acc(kq, [(ip, gat(sub(c0, a, w), kp, sub(hoff, *o)))]))
+                    tt(sub(kk, a, w), sub(A, a, w), kq, mul)
+                else:
+                    gtt(sub(kk, a, w), kp, sub(hoff, *o), sub(A, a, w), mul)
                 dma("S", T.ya[:, a:a + w], sub(kk, a, w), w // 2)
         if t == STEPS - 1:
             break
@@ -476,8 +525,9 @@ def build(T, topo, core, FAC, GA, SC):
         scan(scs, rs, seg)
         d64 = [sub(x, 0, 64) for x in (de, do, sf, ce, co, cf)]
         rank_ = [(tri, d64[0]), (tri, d64[1]), (ones, d64[3]), (ones, d64[4])]
-        xe, xo_ = V("qb", 0, 64), V("qb", 64, 64)
-        mms(acc(xe, rank_ + [(bm, d64[0])]) + acc(xo_, rank_ + [(bm, d64[1])]))
+        xe, xo_ = V("qb", 0, 64), V("qd", 0, 64)
+        mms(acc(xe, rank_ + [(bm, d64[0])]))
+        mms(acc(xo_, rank_ + [(bm, d64[1])]))
         sc_, cnt = S("sc%d" % t, F, 16), S("cnt", F, 16)
         le, lo_ = [act(S("le%d" % j, HF), x, AF.Sign, -1.0, CAP - 0.5 - BIG, acc=sub(sc_, 4 * j, 1)) for j, x in enumerate((xe, xo_))]
         send([(sub(sc_, 0, 1), sub(cnt, 8 * t, 1), to1), (sub(sc_, 4, 1), sub(cnt, 8 * t + 4, 1), to2)], "rc%d" % t, [sub(cnt, 8 * t, 8)])
@@ -488,20 +538,21 @@ def build(T, topo, core, FAC, GA, SC):
         mms(acc(be, [(ones, sub(scs, 0, 2 * SW))]))
         mms(acc(sub(cq, 0, SW), [(tri, de), (ones, ce), (bm, de)]) + acc(sub(cq, SW, SW), [(tri, do), (ones, co), (bm, do)]))
         qf = [V("qr0", 64 * j, 64) for j in range(3)]
-        mms(acc(qf[0], [(tri, d64[2]), (ones, d64[5]), (ip, sub(c84, 0, 64)), (km1, d64[2]), (km1, d64[2]), (im, sub(r64, 0, 64)), (km1, le), (km1, lo_)])
+        mms(acc(qf[0], [(tri, d64[2]), (ones, d64[5]), (ip, c84), (km1, d64[2]), (km1, d64[2]), (im, sub(r64, 0, 64)), (km1, le), (km1, lo_)])
             + acc(qf[1], [(ip, d64[2]), (ip, one64), (hp, le), (hp, lo_)]) + acc(qf[2], [(ip, x) for x in d64[:3]]))
         cp(rf, V("qr0", 0, 192), True)
+        k2 = KS[t + 1]
         mms(acc(nfc, [(ones, sub(cf, 64, 1)), (ip, sub(c84, 0, 1)), (im, sub(r64, 64, 1))])
-            + acc(nfa, [(ones, sub(cf, KS - 1, 1)), (ip, sub(c84, 0, 1)), (row0, sub(r64, KS, 1))]))
+            + (acc(nfa, [(ones, sub(cf, k2 - 1, 1)), (ip, sub(c84, 0, 1)), (row0, sub(r64, k2, 1))]) if k2 else []))
         w2 = aff(S("w2", F, 2 * SW), cq, 1.0, BIG)
         kbs = S("kbs", F, 8)
         for j in range(8):
             act(S("jk%d" % (j % 2), B), V("qd", SW * (j // 4), 64), AF.Sign, -1.0, sub(jh, j % 4, 1), acc=sub(kbs, j, 1))
-        ko = ts(S("ko", U, 8), kbs, 0.5, mul, 32.0, plus)
+        ko = to16(S("ko", U, 8), kbs, 0.5, 32.0)
         msk = S("msk", B, 128)
         for j in range(2):
             gtt(sub(msk, 64 * j, 64), sub(w2, SW * j, SW), sub(ko, 4 * j, 4), i64, OP.is_equal)
-        hvm = gtt(S("hvm", HF, 128), sub(rt_, 64, SW), ko, msk, mul)
+        hvm = gtt(S("hvm", HF, 128), sub(rt_, 0, SW), ko, msk, mul)
         vr = V("qd", 256, 128)
         mms(acc(sub(vr, 0, 64), [(sub(b1, 28, 128), sub(hvm, 0, 64))]) + acc(sub(vr, 64, 64), [(sub(b1, a, 128), sub(hvm, 64, 64)) for a in (12, 140)]))
         sv = tt(S("sv%d" % (t + 1), F, 128), vr, svc, plus)
@@ -510,7 +561,7 @@ def build(T, topo, core, FAC, GA, SC):
         ql = V("qr1", 256, 8)
         wrap(ql, bim, msk, 8, last=False)
         mms([(ql, f8i, kbs, False, True)])
-        lno = ts(S("lno", U, 8), ql, 512.0, plus)
+        lno = to16(S("lno", U, 8), ql, 1.0, 512.0)
         sd, sh = S("sd%d" % t, F, 256), S("sh%d" % t, F, 128)
         gat(sub(sd, 0, 128), sub(cn, OLD, L + 8), lno)
         gat(sub(sd, 128, 64), sub(an, OLD, L + 8), sub(lno, 4, 4))
@@ -520,88 +571,158 @@ def build(T, topo, core, FAC, GA, SC):
         send([(sub(sd, 0, 64), sub(cn, ARR, 64), to1), (sub(sd, 192, 64), sub(an, ARR, 64), to1),
               (sub(sh, 0, 64), sub(cn, ARR + 64, 64), to2), (sub(sh, 64, 64), sub(an, ARR + 64, 64), to2)],
              "rd%d" % t, [sub(cn, ARR, 128), sub(an, ARR, 128)])
+    up = []
     for o in ops:
-        o["all"] = list(o["deps"]) + o["after"]
+        for d in [d for d, hard in o["deps"].items() if not hard and len(o["alts"]) == 1 and list(ops[d]["alts"]) == list(o["alts"])]:
+            del o["deps"][d]
+        near = list(o["deps"]) + o["after"]
+        far = 0
+        for d in near:
+            far |= up[d]
+        o["all"] = [d for d in near if not far >> d & 1]
+        up.append(far | sum(1 << d for d in set(near) if not far >> d & 1))
+        o.setdefault("remote", False)
+        o.setdefault("pipe", 0.1 if o["remote"] else None)
     return ops
 
 
 BEST = []
 
 
-def replay(ops, seq, eng, hop, own, rem, dma):
-    fin, free, last, why = [0.0] * len(ops), {}, {}, [None] * len(ops)
-    for k in seq:
-        o, e = ops[k], eng[k]
-        t = free.get(e, 0.0)
-        why[k] = last.get(e)
-        for d in o["all"]:
-            u = fin[d] + (own if eng[d] == e else hop)
-            if u > t:
-                t = u
-                why[k] = d
-        if e:
-            t += o["alts"][e][0]
-            free[e] = t
-            last[e] = k
-        if "pipe" in o:
-            t = max(t, free.get("pipe", 0.0))
-            free["pipe"] = t + o["pipe"]
-            t += dma
-        fin[k] = t + o["lat"] + (rem if o.get("remote") else 0.0)
-    k = fin.index(max(fin))
-    while why[k] is not None:
-        if why[k] not in ops[k]["deps"] and why[k] not in ops[k]["after"]:
-            WAY.append((why[k], k))
-        k = why[k]
-    return max(fin)
-
-
-WAY = []
-
-
 def schedule(ops, others):
-    def schedule1(*a):
-        order, m, seq, eng = listing(*a)
-        return order, sum(replay(o, seq, eng, *w[3:7]) / w[7] for o, w in zip(others, CASES)) / len(CASES)
+    n = len(ops)
+    deps = [o["all"] for o in ops]
+    pipe = [o["pipe"] for o in ops]
+    cost = [[dict([(None, 0.0)] + [(e, a[0]) for e, a in o["alts"].items()]) for o in oth] for oth in others]
+    late = [[o["lat"] + (0.0 if o["pipe"] is None else w[5] if o["remote"] else w[6]) for o in oth] for oth, w in zip(others, CASES)]
+
+    succ = [[s for s in range(n) if k in deps[s]] for k in range(n)]
+    flex = [k for k, o in enumerate(ops) if len(o["alts"]) > 1 and "V" in o["alts"]]
+
+    def length(seq, eng, i=0, old=None, room=1e9):
+        before = {}
+        for k in seq[:i]:
+            before[eng[k]] = k
+            if pipe[k] is not None:
+                before["pipe"] = k
+        new, total, way = [], 0.0, []
+        for c, w in enumerate(CASES):
+            fin, why, end, pend = [x[:] for x in old[c][:4]] if old else ([0.0] * n, [None] * n, [0.0] * n, [0.0] * n)
+            last, hop, own, co, la = dict(before), w[3], w[4], cost[c], late[c]
+            for k in seq[i:]:
+                e = eng[k]
+                y = last.get(e) if e else None
+                t = 0.0 if y is None else end[y]
+                for d in deps[k]:
+                    u = fin[d] + (own if eng[d] == e else hop)
+                    if u > t:
+                        t = u
+                        y = d
+                t += co[k][e]
+                end[k] = t
+                last[e] = k
+                p = pipe[k]
+                if p is not None:
+                    d = last.get("pipe")
+                    if d is not None and pend[d] > t:
+                        t = pend[d]
+                        y = d
+                    pend[k] = t + p
+                    last["pipe"] = k
+                fin[k] = t + la[k]
+                why[k] = y
+            m = max(fin)
+            part = (m + MEAN * sum(fin) / n) / w[7]
+            total += part
+            if old:
+                room -= part - old[c][4]
+                if room < -EARLY * (len(CASES) - 1 - c) - 1.0 * (c == len(CASES) - 1):
+                    return 1e9, None, None
+            k = fin.index(m)
+            while why[k] is not None:
+                if why[k] not in deps[k]:
+                    way.append((why[k], k))
+                k = why[k]
+            new.append((fin, why, end, pend, part))
+        return total / len(CASES) + LAM * sum(cost[0][k]["V"] for k in flex if eng[k] == "V"), way, new
     if not BEST:
-        flex = [k for k, o in enumerate(ops) if len(o["alts"]) > 1]
-        shift, pin = {}, {k: "A" for k in flex if ops[k]["alts"]["A"][0] < PIN}
-        seed = min(range(TRIES), key=lambda s: schedule1(ops, s, shift, pin)[1])
-        del WAY[:]
-        best = schedule1(ops, seed, shift, pin)[1]
-        way, now = list(WAY), [o.get("eng") for o in ops]
-        x = 12345
-        for _ in range(CLIMB):
-            s2, p2 = dict(shift), dict(pin)
-            for _ in range(1 + (x >> 9) % 2):
+        pin = {k: "S" if pipe[k] is not None else "A" for k, o in enumerate(ops) if len(o["alts"]) > 1 and o["alts"].get("A", [PIN])[0] < PIN}
+        seq, eng = min((listing(ops, s, pin) for s in range(TRIES)), key=lambda r: length(*r)[0])
+        now, way, old = length(seq, eng)
+        best, keep = now, (seq, eng, old)
+        x = SEED
+        for it in range(CLIMB):
+            x = (x * 1103515245 + 12345) % 2 ** 31
+            a, b = way[(x >> 8) % len(way)]
+            if (x >> 23) % 8 < ANY:
+                k = (x >> 8) % n
+                y = old[(x >> 5) % len(CASES)][1][k]
+                if y is None or y in deps[k]:
+                    continue
+                a, b = y, k
+            u = (x >> 20) % 8
+            s2, e2 = seq, eng
+            if (x >> 26) % 8 < FAR:
+                k = (a, b, (x >> 6) % n)[(x >> 4) % 3]
+                j = seq.index(k)
+                s2 = seq[:j] + seq[j + 1:]
+                lo = max([s2.index(d) + 1 for d in deps[k]] or [0])
+                hi = min([s2.index(d) for d in succ[k]] or [n - 1])
                 x = (x * 1103515245 + 12345) % 2 ** 31
-                a, b = way[(x >> 8) % len(way)]
-                d = (1 + (x >> 3) % 16) / 4.0
-                u = (x >> 20) % 8
-                if u < 2 and len(ops[a]["alts"]) > 1:
-                    p2[a] = "V" if now[a] == "A" else "A"
-                elif u < 3 and len(ops[b]["alts"]) > 1:
-                    p2[b] = "V" if now[b] == "A" else "A"
-                elif u < 5:
-                    s2[a] = s2.get(a, 0.0) - d
-                elif u < 7:
-                    up = [b]
-                    for _ in range(3):
-                        up = set(up) | set(j for i in up for j in ops[i]["all"])
-                    for i in up:
-                        s2[i] = s2.get(i, 0.0) + d
+                i = lo + (x >> 8) % (hi - lo + 1)
+                s2.insert(i, k)
+                i = min(i, j)
+                if len(ops[k]["alts"]) > 1 and (x >> 5) % 3 == 0:
+                    e2 = list(eng)
+                    e2[k] = [e for e in ops[k]["alts"] if e != eng[k]][0]
+            elif u < 2:
+                k = a if u else b
+                if len(ops[k]["alts"]) < 2:
+                    continue
+                e2 = list(eng)
+                e2[k] = [e for e in ops[k]["alts"] if e != eng[k]][0]
+                i = seq.index(k)
+            else:
+                i, j = seq.index(a), seq.index(b)
+                if u == 7:
+                    i = max(0, i - 1 - (x >> 4) % 12)
+                elif u == 6:
+                    j = min(len(seq) - 1, j + 1 + (x >> 4) % 12)
+                part = seq[i:j + 1]
+                if u % 2:
+                    need = set(deps[b])
+                    go = {b}
+                    for k in part[::-1]:
+                        if k in need:
+                            go.add(k)
+                            need.update(deps[k])
+                    if a in go:
+                        continue
+                    part = [k for k in part if k in go] + [k for k in part if k not in go]
                 else:
-                    k = (x >> 8) % len(ops)
-                    s2[k] = s2.get(k, 0.0) + 2 * d - 4
-            del WAY[:]
-            m = schedule1(ops, seed, s2, p2)[1]
-            if m <= best:
-                best, shift, pin, way, now = m, s2, p2, list(WAY), [o.get("eng") for o in ops]
-        BEST.append((seed, shift, pin))
-    return schedule1(ops, *BEST[0])
+                    go = {a}
+                    for k in part:
+                        if not go.isdisjoint(deps[k]):
+                            go.add(k)
+                    if b in go:
+                        continue
+                    part = [k for k in part if k not in go] + [k for k in part if k in go]
+                s2 = seq[:i] + part + seq[j + 1:]
+            x = (x * 1103515245 + 12345) % 2 ** 31
+            room = HEAT * (1 - it / CLIMB) * (x / 2.0 ** 31) ** 3
+            m, w2, new = length(s2, e2, i, old, len(CASES) * room + (LAM if e2 is not eng else 0.0))
+            if m <= now + room:
+                now, seq, eng, way, old = m, s2, e2, w2, new
+                if m < best:
+                    best, keep = m, (seq, eng, old)
+        BEST.append(keep + (best,))
+    seq, eng = BEST[0][:2]
+    for o, e in zip(ops, eng):
+        o["eng"] = e
+    return {e: [k for k in seq if eng[k] == e] for e in "VAPGS"}
 
 
-def listing(ops, seed, shift, pin):
+def listing(ops, seed, pin):
     n = len(ops)
     x = [seed * 7919 + 1]
 
@@ -613,22 +734,20 @@ def listing(ops, seed, shift, pin):
     look, gap = 0.6 * rnd(), 0.5 + 3 * rnd()
     succ = [[] for _ in range(n)]
     for k, o in enumerate(ops):
-        for d in list(o["deps"]) + o["after"]:
+        for d in o["all"]:
             succ[d].append(k)
     pr = [0.0] * n
     for k in range(n - 1, -1, -1):
         o = ops[k]
         pr[k] = min([a[0] for a in o["alts"].values()] or [0.0]) * (1 + noise * (rnd() - 0.5)) + o["lat"] + HOP + max([pr[s] for s in succ[k]] or [0.0])
-    pr = [o.get("first", pr[k] + shift.get(k, 0.0)) for k, o in enumerate(ops)]
+    pr = [o.get("first", pr[k]) for k, o in enumerate(ops)]
     engs = [[pin[k]] if k in pin else list(o["alts"]) for k, o in enumerate(ops)]
-    left = [len(o["deps"]) + len(o["after"]) for o in ops]
-    ready, fin, seq = [0.0] * n, [0.0] * n, []
+    left = [len(o["all"]) for o in ops]
+    ready, seq, eng = [0.0] * n, [], [None] * n
     free = {e: 0.0 for e in list("VAPGS") + ["pipe"]}
-    order = {e: [] for e in "VAPGS"}
     cand = [k for k in range(n) if left[k] == 0]
 
     def done(k, t):
-        fin[k] = t
         seq.append(k)
         cand.remove(k)
         for s in succ[k]:
@@ -650,31 +769,44 @@ def listing(ops, seed, shift, pin):
         e = min(engs[k], key=lambda x: max(free[x], ready[k]) + ops[k]["alts"][x][0] * (1 + bias if x == "V" else 1) + (bias if x == "V" else 0.0))
         t = max(free[e], ready[k])
         free[e] = t + ops[k]["alts"][e][0]
-        ops[k]["eng"], ops[k]["t0"] = e, t
-        order[e].append(k)
+        eng[k] = e
         t = free[e]
-        if "pipe" in ops[k]:
+        if ops[k]["pipe"] is not None:
             t = max(t, free["pipe"])
             free["pipe"] = t + ops[k]["pipe"]
         done(k, t + ops[k]["lat"])
-    return order, max(fin), seq, [o.get("eng") for o in ops]
+    return seq, eng
 
 
 def plan(T, topo, core):
-    others = [] if BEST else [build(T, topo, core, *w[:3]) for w in CASES]
+    others = [] if BEST else [build(T, topo, core, *(w[:3] + w[8:])) for w in CASES]
     ops = build(T, topo, core, FAC, GA, SC)
     for o in ops:
-        o["lat"] += 1.5 if o.get("remote") else 0.5 if "pipe" in o else 0.0
+        o["lat"] += 1.5 if o["remote"] else 0.5 if o["pipe"] is not None else 0.0
     return ops, schedule(ops, others)
 
 
 def rank_program(g, core, T, topo):
     if T.rank_of(core) is None:
         return
-    ops, (order, _) = plan(T, topo, core)
+    ops, order = plan(T, topo, core)
     qs = {"V": g.vector, "A": g.scalar, "P": g.tensor, "G": g, "S": g.sync}
-    for o in ops:
-        o["wait"] = [d for d, hard in o["deps"].items() if hard or ops[d].get("eng") != o.get("eng")]
+    known, done = dict((e, 0) for e in order), {}
+    for k in BEST[0][0]:
+        o = ops[k]
+        e = o["eng"]
+        o["wait"] = []
+        if e is None:
+            done[k] = 1 << k
+            continue
+        for d in sorted(o["deps"], reverse=True, key=BEST[0][0].index):
+            if (o["deps"][d] or ops[d]["eng"] != e) and not known[e] >> d & 1:
+                o["wait"].append(d)
+                known[e] |= done[d]
+        done[k] = known[e] | 1 << k
+        if o["sem"] is None:
+            done[k] |= done.get(e, 0)
+            done[e] = done[k]
     needed = set(d for o in ops for d in o["wait"])
     cnt = {}
     for e in order:
@@ -699,7 +831,7 @@ def rank_program(g, core, T, topo):
             r = o["alts"][e][1](qs[e])
             if o.get("one"):
                 r.then_inc(T.sem[o["sem"][0]], 1)
-            elif o["sem"] is not None and not o.get("remote"):
+            elif o["sem"] is not None and not o["remote"]:
                 r.then_inc(T.sem[o["sem"][0]], o["sem"][1])
     for o in ops:
         if o["sem"] is not None and not o.get("one") and top.get(o["sem"][0], 0) < o["sem"][1]:

@@ -6,37 +6,51 @@ ARR, LB = 8, 640
 OLD = LB + 2 * L
 WW = OLD + L
 ZC, ZB, ZA = 256, 1280, 3328
-BIG = 8192.0
+BIG, TOP, STEEP = 8192.0, 196608.0, 2.0 ** 53
+COPY, TWICE, HALF = [False, False, False], [0, 1, 0], True
+LAG = [[], []]
+EARLYA = 0
+FILL = [0, 1, 2]
+HALVE = 1
+FIRST = EARLYG = True
+ONCE = 2.0
+MERGE = [False, False]
+HALFA = [True, True, True]
+SPAN, SWEEPS = 140, 30
+UNIT = 2.0 ** -18
 SW = 72
 F, B, I, U, HF = "float32", "bfloat16", "int32", "uint16", "float16"
 SIZE = {F: 4, B: 2, I: 4, U: 2, HF: 2}
-POOL = {F: ("pf", 4200), B: ("pb", 6600), I: ("pi", 400), U: ("pu", 640), HF: ("ph", 4000)}
+POOL = {F: ("pf", 4200), B: ("pb", 8000), I: ("pi", 400), U: ("pu", 760), HF: ("ph", 4000)}
 SCRATCH = {
-    "kp": ("sbuf", [128, H], B), "dm": ("sbuf", [128, H], B), "sg": ("sbuf", [128, H], F), "ex": ("sbuf", [128, H], I),
+    "kp": ("sbuf", [128, H + 16], B), "dm": ("sbuf", [128, H + 16], B), "w0": ("sbuf", [128, WW], B), "ex": ("sbuf", [128, H], I),
+    "sg": ("sbuf", [128, L], F), "xs": ("sbuf", [128, L], F), "cs": ("sbuf", [128, L + 8], F), "mp": ("sbuf", [128, L], B),
     "wn": ("sbuf", [128, 6 * WW + 8], F), "zz": ("sbuf", [128, ZA + 2 * L + 8], F),
     "kk": ("sbuf", [128, L], F), "c1": ("sbuf", [128, L], F), "a1": ("sbuf", [128, L], F),
-    "mc": ("sbuf", [128, L], B), "ma": ("sbuf", [128, 4 * L], B), "eg": ("sbuf", [128, L], HF),
-    "g2": ("sbuf", [128, L], HF), "cb": ("sbuf", [128, L], B), "ab": ("sbuf", [128, L], B), "c0": ("sbuf", [128, L], B),
+    "mc": ("sbuf", [128, L], B), "eg": ("sbuf", [128, L], HF),
+    "g2": ("sbuf", [128, L], HF), "cb": ("sbuf", [128, L], B), "c0": ("sbuf", [128, L], B),
 }
 for _d, (_n, _w) in POOL.items():
     SCRATCH[_n] = ("sbuf", [128, _w], _d)
 for _n in ("qr0", "qr1", "qa", "qb", "qc", "qd", "qe", "qm"):
     SCRATCH[_n] = ("psum", [128, 512], F)
-SEMAPHORES = ["eV", "eA", "eP", "eG"] + ["d%d" % k for k in range(60)] + ["rv0", "rv1", "rd0", "rd1", "rc0", "rc1"]
+SEMAPHORES = ["eV", "eA", "eP", "eG"] + ["d%d" % k for k in range(70)] + ["rv0", "rv1", "rd0", "rd1", "rc0", "rc1", "ra0", "ra1"]
 
 CY, FAC, GA, SC, PEC, HOP, BIAS = 0.00083, 1.1, 1.45, 3.5, 0.00042, 0.14, 0.3
-CASES = [(1.0, 1.56, 3.8, 0.15, 0.08, 1.0, 0.5, 0.8, 1.0, 1.2, 1.0), (1.05, 1.2, 2.4, 0.2, 0.1, 2.5, 1.0, 0.8, 1.4, 1.7, 1.2),
-         (1.35, 1.8, 4.8, 0.15, 0.08, 1.5, 0.5, 1.15, 1.0, 1.2, 1.0), (1.2, 1.4, 3.2, 0.2, 0.08, 4.0, 1.5, 0.95, 1.2, 1.4, 1.1)]
-PIECES, LAST, TRIES, CLIMB, PIN, HEAT, SEED, MEAN, ANY, FAR, EARLY, LAM = 2, 2, 6, 190000, 1.5, 0.7, 7, 0.5, 2, 4, 0.1, 0.3
-SA = [1, 1, 2]
-KG = 1
-KORD = [[(0,), (2, 3)], [(2, 3), (0,)], [(2, 3), (0,)]]
-KS = [0, 32, 32]
-OFF = 6144.0
+CASES = [(1.0, 1.56, 3.8, 0.15, 0.13, 1.0, 0.3, 0.8, 1.0, 1.2, 0.9), (1.05, 1.2, 2.4, 0.2, 0.16, 2.0, 0.8, 0.8, 1.2, 1.4, 1.2, 1.4),
+         (1.35, 1.8, 4.8, 0.15, 0.13, 1.5, 0.5, 1.15, 1.0, 1.2, 1.0), (1.2, 1.4, 3.2, 0.2, 0.16, 4.0, 1.5, 0.95, 1.2, 1.4, 1.1)]
+PIECES, LAST, TRIES, CLIMB, PIN, HEAT, SEED, MEAN, ANY, FAR, EARLY, LAM = 2, 2, 6, 330000, 1.5, 0.7, 7, 0.5, 2, 4, 0.1, 0.3
+SA = [2, 1, 1]
+KG = 2
+KORD = [[(1,), (0,), (2, 3)], [(0,), (1,), (2, 3)], [(1,), (2, 3), (0,)]]
+KS = [32, 32, 32]
+EPS, MID = 5e-5, 1600.0
+BETA = EPS / 4 * (1 - (1024 * EPS) ** 2 / 16)
+JO, LO = 1152.0, 1280.0
 
 
-def build(T, topo, core, FAC, GA, SC, GI=1.0, AC=1.0, PF=1.0):
-    ops, hist, lay, top, nsem = [], {}, {}, {}, [0]
+def build(T, topo, core, FAC, GA, SC, GI=1.0, AC=1.0, PF=1.0, BW=1.0):
+    ops, hist, lay, top, nsem, firstg = [], {}, {}, {}, [0], []
 
     def V(name, a=0, n=None, p=None, step=1):
         t = T[name]
@@ -79,16 +93,17 @@ def build(T, topo, core, FAC, GA, SC, GI=1.0, AC=1.0, PF=1.0):
         k = len(ops)
         deps = {}
         use = [(x, False) for x in rd if x[0] in SCRATCH] + [(x, True) for x in wr if x[0] in SCRATCH]
+        pe = "P" in alts
         for v, w in use:
             ps = psum(v)
             for u, w2, k2 in hist.get(v[0], ()):
-                if (w or w2) and (ps or meet(v, u)):
+                if (w or w2) and (meet(v, u) or (ps and (pe or "P" in ops[k2]["alts"]))):
                     deps[k2] = True
                 elif ps:
                     deps.setdefault(k2, False)
         for v, w in use:
             hs = hist.setdefault(v[0], [])
-            if w and psum(v):
+            if w and psum(v) and pe:
                 hs[:] = [e for e in hs if e[2] == k]
             elif w:
                 hs[:] = [e for e in hs if not (v[1] <= e[0][1] and e[0][1] + e[0][2] <= v[1] + v[2] and e[0][4] & ~v[4] == 0
@@ -142,6 +157,9 @@ def build(T, topo, core, FAC, GA, SC, GI=1.0, AC=1.0, PF=1.0):
     def to16(o, x, mul=1.0, plus=0.0):
         return act(o, x, AF.Relu, mul, plus, alt=tsv(o, x, mul, OP.mult, plus, OP.add))
 
+    def over(o, x, v):
+        return act(o, x, AF.Sigmoid, STEEP, 100.0 - v * STEEP, alt=tsv(o, x, v, OP.is_ge))
+
     def cp(o, x, both=False):
         v = (tv(o[6], 0.5 if two(o, x) else 1), lambda q: q.tensor_copy(o[3], x[3]))
         if both:
@@ -158,7 +176,7 @@ def build(T, topo, core, FAC, GA, SC, GI=1.0, AC=1.0, PF=1.0):
 
     def scat(win, off, x, silu=None):
         if silu:
-            add({"A": (tv(x[6], SC), lambda q: q.activation(win[3].indirect(off[3]), x[3], AF.Silu))}, [off, x, silu], [win])
+            add({"A": (tv(x[6], SC), lambda q: q.activation(win[3].indirect(off[3]), x[3], AF.Sigmoid))}, [off, x], [win])
         else:
             add({"V": (tv(x[6], SC), lambda q: q.tensor_copy(win[3].indirect(off[3]), x[3]))}, [off, x], [win])
 
@@ -172,7 +190,7 @@ def build(T, topo, core, FAC, GA, SC, GI=1.0, AC=1.0, PF=1.0):
 
     def mset(o, c):
         alts = {"V": (tv(o[6], 0.5 if two(o) else 1), lambda q: q.memset(o[3], c))}
-        if SCRATCH[o[0]][2] != HF and o[5] == 1:
+        if SCRATCH[o[0]][2] != HF and o[5] == 1 and c == int(c):
             alts["G"] = iog(o, [[0, o[6]]], int(c), 0)
         add(alts, [], [o])
         return o
@@ -203,10 +221,12 @@ def build(T, topo, core, FAC, GA, SC, GI=1.0, AC=1.0, PF=1.0):
     def dma(eng, o, x, kb, acc=False):
         s = "d%d" % nsem[0]
         nsem[0] += 1
-        kb *= AC if acc else 1.0
+        kb *= (AC if acc else 1.0) * BW
         kw = {"accum_op": OP.add, "max_dma_last_dim": 8192} if acc else {}
-        add({e: (GI if e == "G" else 0.1, lambda q: q.dma_start(ap(o), ap(x), **kw)) for e in ("G" if eng == "G" else "SA")},
-            [v for v in (x, o if acc else None) if isv(v)], [o] if isv(o) else [], lat=1.6 + kb / 600.0, sem=(s, 16))
+        add({e: (GI + (0.0 if firstg else ONCE * GI) if e == "G" else 0.1, lambda q: q.dma_start(ap(o), ap(x), **kw)) for e in ("G" if eng == "G" else "SA")},
+            [v for v in (x, o if acc else None) if isv(v)], [o] if isv(o) else [], lat=1.6 + kb / 600.0, sem=(s, 16), after=firstg if eng == "G" else ())
+        if eng == "G" and not firstg:
+            firstg.append(len(ops) - 1)
         ops[-1]["pipe"] = kb / 600.0
 
     def send(items, rsem, land):
@@ -215,20 +235,20 @@ def build(T, topo, core, FAC, GA, SC, GI=1.0, AC=1.0, PF=1.0):
         trs, tot = [], 0
         for j, (src, dst, to) in enumerate(items):
             en = topo.engines(core, to)
-            w = len(en) // len(items)
+            w = len(en) // len(items) // (HALVE if rsem == "rc0" else 1)
             m = sum(1 << e for e in en[j * w:(j + 1) * w])
             rid, pid, _ = topo.addr(to)
             trs.append(RemoteDMATransfer(dst_ids=[DstId(rid=rid, pnc=pid)], dma_engine_mask=m, remote_sem=T.sem[rsem], src=src[3], dst=dst[3]))
             tot += w
-        k = add({"G": (GI, lambda q: q.remote_dma_fused(trs, local_sem=T.sem[s]))}, [i[0] for i in items], [], lat=1.5 + (2.0 if rsem == "rc0" else 0.0), sem=(s, tot))
+        k = add({"G": (GI, lambda q: q.remote_dma_fused(trs, local_sem=T.sem[s]))}, [i[0] for i in items], [], lat=1.5 + (2.0 * AC if rsem == "rc0" else 0.0), sem=(s, tot))
         ops[k]["remote"] = True
         add({}, [], land, lat=0.3, sem=(rsem, tot), after=[k])
 
     rank, n = T.rank_of(core), len(T.cores)
     to1, to2 = T.cores[(rank + 1) % n], T.cores[(rank + 2) % n]
     kp, dm, sg, ex, zz, mc = [V(x) for x in ("kp", "dm", "sg", "ex", "zz", "mc")]
-    kk, c1, a1, eg, g2, cb, ab, c0 = [V(x) for x in ("kk", "c1", "a1", "eg", "g2", "cb", "ab", "c0")]
-    nl = mc
+    kk, c1, a1, eg, g2, cb, c0, w0, xs = [V(x) for x in ("kk", "c1", "a1", "eg", "g2", "cb", "c0", "w0", "xs")]
+    nl, ab, mp, cs, kq_ = mc, sub(w0, OLD, L), V("mp"), V("cs"), V("kp", 0, H0 + 16)
     wc, wa = [V("wn", 2 * t * WW, WW + 8) for t in range(3)], [V("wn", (2 * t + 1) * WW, WW + 8) for t in range(3)]
     qr = [V("qr0"), V("qr1")]
     HV = [(0, 512), (512, 512)]
@@ -246,11 +266,21 @@ def build(T, topo, core, FAC, GA, SC, GI=1.0, AC=1.0, PF=1.0):
     for a in (0, 2 * L, L):
         dma("S", V("ex", a, L, slice(0, 128, 16)), T.lf[:, a:a + L], 100)
         dma("S", V("ex", a, L, slice(8, 128, 16)), T.rt[:, a:a + L], 100)
-    dma("S", dm, T.dam[:], 1000)
+    dma("S", sub(kq_, 0, H0), T.kap[:, 0:H0], 750)
     ops[-1]["after"] += [len(ops) - 3, len(ops) - 2]
-    dma("S", kp, T.kap[:], 1000)
     for j, o in enumerate(ops):
         o["first"] = 1000.0 - j
+    k = len(ops) - 1
+    for j in range(2):
+        dma("G" if j and EARLYG else "S", sub(w0, LB + j * L, L), T.amp[:], 256)
+        ops[-1]["after"].append(k - (6 if j and EARLYG else 0))
+    dma("S", sub(dm, 0, H), T.dam[:], 1000)
+    ops[-1]["after"].append(k)
+    mset(sub(kq_, H0, 1), 0.5)
+    mset(sub(cs, L, 1), -8.0)
+    mset(sub(dm, H, 1), 40.0)
+    mset(sub(kp, H, 1), 0.0)
+    mset(sub(w0, 0, 1), 0.0)
 
     pi = iota(S("pi", I, 1), [[0, 1]], 0, 1)
     pc = iota(C("pc"), [[0, 1]], 0, 1)
@@ -261,14 +291,15 @@ def build(T, topo, core, FAC, GA, SC, GI=1.0, AC=1.0, PF=1.0):
     mset(V("wn", 0, 6 * WW + 1, None, 2 * WW), -8.0)
     mset(V("wn", WW, 4 * WW + 1, None, 2 * WW), 0.0)
     all1 = mset(S("all1", B, 512), 1.0)
-    rs = mset(S("rs", B, 3 * SW), 1.0)
+    rs = act(S("rs", B, 3 * SW), sub(io, 0, 3 * SW), AF.Sigmoid, 1.0, 40.0, extra=1.3)
     mset(every(rs, SW, SW, 2), 0.0)
     one64, one1 = sub(all1, 0, 64), sub(all1, 0, 1)
     nil = S("nil", B, 4 * SW + 128)
-    mset(sub(nil, 0, 4 * SW + 64), 0.0)
+    mset(sub(nil, 0, 4 * SW), 0.0)
     seg = sub(nil, 0, 3 * SW)
     dis, cdc = sub(nil, 3 * SW, 65), sub(nil, 4 * SW, 128)
-    mset(sub(cdc, 64, 64), -3840.0)
+    mset(sub(cdc, 0, 64), -2048.0 - LO - 32 * JO)
+    mset(sub(cdc, 64, 64), LB - 1024.0)
     qb_ = S("qbm", B, 144)
     mset(sub(qb_, 0, 3), 0.0)
     zeros = mset(S("zeros", HF, 384), 0.0)
@@ -299,15 +330,36 @@ def build(T, topo, core, FAC, GA, SC, GI=1.0, AC=1.0, PF=1.0):
     i12 = pick(S("i12", B, 152), sub(all1, 0, 152), [[-1, 152]], 12)
     ip = sub(i12, 12, 128)
     im, kp1, km1, bp, bm, hp = [aff(S("wt%d" % j, B, 128), ip, w, 0.0) for j, w in enumerate((-1.0, 1024.0, -1024.0, BIG, -BIG, 0.5))]
-    f8i = aff(S("f8i", F, 128), ip, 8.0, 0.0)
+
+
+    def late(name, w, dt=B):
+        iota(S(name, dt, 128), [[0, 128]], w)
+        ops[-1]["after"] += soon
+        return pick(S(name), S(name), [[-1, 128]], 0)
+    mmq = pick(S("mmq", B, 512), all1, [[-1, 4], [-16, 8], [-4, 16]], 0)
+    soon = firstg + [len(ops) - 1]
+    f8i, m2, k4, whole = late("f8i", 8, F), late("m2", -2), late("k4", -4096), late("whole", int(8 / UNIT))
+    kp2, km2, km3 = late("kp2", 2048), late("km2", -2048), late("km3", -3072)
     e4 = ts(S("e4", F, 4), sub(io, 0, 4), cp(C("q4"), ts(S("q4i", I, 1), ici, 2, OP.arith_shift_right)), OP.is_equal)
     mu = [aff(S("mu%d" % u, B, 152), i12, sub(e4, u, 1), 0.0) for u in range(4)]
-    mu1d, mu2n = aff(S("mu1d", B, 152), mu[1], 2.0, 0.0), aff(S("mu2n", B, 152), mu[2], -1.0, 0.0)
-    mmq = pick(S("mmq", B, 512), all1, [[-1, 4], [-16, 8], [-4, 16]], 0)
+    muk = [aff(S("muk%d" % u, B, 152), mu[u], 1024.0, 0.0) for u in range(4)]
+    mu32 = aff(S("mu32", B, 152), mu[2], 32.0, 0.0)
+    p32, m32 = [aff(S("w32%d" % j, B, 128), ip, w, 0.0) for j, w in enumerate((32.0, -32.0))]
+    kilo = mset(S("kilo", B), 1024.0)
+    lidb, lidc = aff(S("lidb"), lid, BIG, 0.0), aff(S("lidc"), lid, 1.0, -511.5)
+    step = S("step", F, 128)
+    iota(sub(step, 0, 16), [[1, 16]], 112)
+    iota(sub(step, 16, 112), [[1, 112]])
+    for o in ops[-2:]:
+        o["after"] += soon
+    ts(step, step, pc, OP.is_equal)
+    ntop, cfar = mset(S("top", B), -TOP), mset(S("cfar", B), LB + 2048.0)
+    e1 = sub(e16, 1, 1)
+    inb, inx, outb = [aff(C("cb%d" % j), e1, w * MID, b - w * MID) for j, (w, b) in enumerate(((BETA, 0.5), (EPS, 0.0), (-1.0, -0.5 / BETA)))]
     pick(sub(qb_, 3, 128), sub(all1, 0, 128), [[-16, 8], [-1, 4], [1000, 4]], 0)
     rt_ = S("rt", I, 128)
     c84 = mset(S("c84", B, 64), -1984.0)
-    idq = ts(S("idq", HF, 256), sub(io, 0, 256), aff(C("id0"), sub(e4, 1, 1), 4.0, 0.0), mul, ts(C("id1"), ic, 1020.0, plus, sub(e4, 1, 1), mul), plus)
+    idq = ts(S("idq", HF, 256), sub(io, 0, 256), aff(C("id0"), sub(e4, 1, 1), 4.0, 0.0), mul, ts(C("id1"), ic, -1028.0, plus, sub(e4, 1, 1), mul), plus)
     xf = S("xf", HF, 192)
     own = aff(sub(xf, 128, 64), lid, 1.0, LB - 1024.0)
     cj = [mset(S("cj%d" % t, B), 1792.0 + BIG + 128 * (1 - t)) for t in range(2)]
@@ -321,43 +373,53 @@ def build(T, topo, core, FAC, GA, SC, GI=1.0, AC=1.0, PF=1.0):
     so = S("so", U, 192)
     hoff, s1, s2 = [sub(so, 64 * j, 64) for j in range(3)]
     to16(hoff, pt)
+    hk = ts(S("hkk", U), pt, float(H0), OP.min)
     rf = S("rf", HF, 192)
-    rfo, fr, ngo = [sub(rf, 64 * j, 64) for j in range(3)]
-    ts(ngo, pt, float(H0), OP.is_ge)
+    rfo, fr, rest = [sub(rf, 64 * j, 64) for j in range(3)]
+    ts(rest, pt, float(H0), OP.is_ge, -1.0, mul)
     for j, (a, w) in enumerate(HV):
-        act(sub(nl, a, w), sub(ab, a, w), AF.Sign, -1.0, alt=tsv(sub(nl, a, w), sub(ab, a, w), 0.0, OP.is_gt, -1.0, mul))
-        mms(acc(qr[j], [(km1, all1), (km1, sub(nl, a, w)), (ip, sub(cb, a, w))]))
-        cp(sub(c0, a, w), qr[j], True)
-        ts(V("ma", a, w), sub(c0, a, w), 0.0, OP.is_lt, -8.0, mul)
-    dma("G", sub(wc[0], OLD, L), c0, 512)
-    dma("G", sub(wa[0], OLD, L), T.amp[:], 512)
-    for j in range(8):
-        act(sub(sg, 512 * j, 512), sub(dm, 512 * j, 512), AF.Sigmoid, extra=1.3 if j == 0 else 0.0)
-        if j:
-            ops[-1]["after"].append(len(ops) - 1 - j)
-    sv0 = S("sv0", F, 128)
-    add({"A": (tv(128) + 1.5, lambda q: q.activation(sv0[3], i128[3], AF.Silu, bias=1800.0 + H0))}, [i128, sg], [sv0])
-    svc = ts(S("svc", F, 128), sv0, aff(C("n3"), sub(e16, 3, 1), -1.0, 1.0), mul, OFF - H0, plus)
+        ts(sub(nl, a, w), sub(ab, a, w), 0.0, OP.is_equal)
+        mms(acc(qr[j], [(km1, sub(nl, a, w)), (ip, sub(cb, a, w))]))
+        if FIRST:
+            over(sub(mp, a, w), qr[j], 0.0)
+        aff(sub(c0, a, w), qr[j], UNIT, 0.0)
+        if not FIRST:
+            over(sub(mp, a, w), sub(c0, a, w), 0.0)
+    n1 = aff(C("n1"), e1, ARR - LB - 1024.0 - JO - 32, JO + 32)
+    svc = ts(S("svc", HF, 128), i128, e1, mul, aff(C("n3"), sub(e16, 3, 1), LO - 2048.0 - JO - 32, n1), plus)
     mc_, nfc, nfa = [V("qm", j, 1) for j in (0, 8, 9)]
-    n0a, n0b = V("qe", 448, 1), V("qe", 449, 1)
+    n0a, n0b = V("qc", 384, 1), V("qc", 385, 1)
     de, do, sf = [sub(seg, SW * j, SW) for j in range(3)]
     scs = S("scs", B, 3 * SW)
     ce, co, cf = [sub(scs, SW * j, SW) for j in range(3)]
     pre = lid
+    mark, held = {}, []
+
+    def leave(t, j, win, sd):
+        sh = S("sh%d%d" % (t, j))
+        if j:
+            dma("S", sub(sh, 0, 64, slice(16, 128)), sub(sd, 64, 64, slice(0, 112)), 32)
+            dma("S", sub(sh, 0, 64, slice(0, 16)), sub(sd, 64, 64, slice(112, 128)), 32)
+        else:
+            mms([(V("qd", 416, 64), step, sub(sd, 64, 64), True, True)])
+            cp(sh, V("qd", 416, 64), True)
+        held.append(([(sub(sd, 0, 64), sub(win, ARR, 64), to1), (sh, sub(win, ARR + 64, 64), to2)], sub(win, ARR, 128)))
+        if j or not MERGE[t]:
+            send([x for h in held for x in h[0]], "%s%d" % (("rd", "ra")[j], t), [h[1] for h in held])
+            held.clear()
 
     for t in range(STEPS):
         cw, aw, cn, an = wc[t], wa[t], wc[(t + 1) % 3], wa[(t + 1) % 3]
-        c, A = (c0, ab) if t == 0 else (sub(cw, OLD, L), sub(aw, OLD, L))
+        c, A = (c0, ab) if t == 0 else (sub(cs, 0, L), sub(aw, OLD, L))
         ws, ks = ZC - 128 * t, KS[t]
-        ma, mn = V("ma", 2 * L * (t % 2), 2 * L), V("ma", 2 * L * (1 - t % 2), 2 * L)
         hl, u = V("qa", 0, 64), V("qb", 0, 64)
         wrap(hl, bw, nl, 64)
-        hs = aff(S("hs", HF), hl, -2.0 if t else -4.0, 32.0 if t else 0.0)
-        mms(acc(u, [(km1, ngo)], last=False))
-        wrap(u, bw, sub(ma, 0, L), 64, False, False)
+        hs = aff(S("hs", HF), hl, 0.5 if t else -0.5, 0.0 if t else 8.0)
+        mms(acc(u, [(kp1, rest)] + ([(km1, fr)] if t else []), last=False))
+        wrap(u, bw, mp, 64, False, False)
         mms(acc(u, [(im, hs)], first=False))
         if t == 0:
-            ts(sub(sf, 0, 64), hl, 0.0, OP.is_equal)
+            ts(sub(sf, 0, 64), hl, 16.0, OP.is_equal)
             cp(fr, sub(sf, 0, 64), True)
             scan(cf, sub(rs, 2 * SW, SW), sf)
             pf_ = V("qd", 0, 64)
@@ -366,25 +428,39 @@ def build(T, topo, core, FAC, GA, SC, GI=1.0, AC=1.0, PF=1.0):
             cp(rfo, pf_, True)
         for a, w in PV:
             aff(sub(eg, a, w), ex, 1.0, -2048.0, sub(hoff, a // 16, w // 16))
-        xl_, xr_ = wrap(V("qc", 0, 64), bx0, eg, 64), wrap(V("qc", 64, 64), bx8, eg, 64)
-        xo = to16(S("xo", U, 128), V("qc", 0, 128), 1.0, 2048.0)
-        xlo, xro = sub(xo, 0, 64), sub(xo, 64, 64)
+        wrap(V("qc", 0, 64), bx0, eg, 64)
+        wrap(V("qc", 64, 64), bx8, eg, 64)
+        jf = aff(S("jf", HF, 128), V("qc", 0, 128), 1.0 / 32, JO + 64 - 15.5 / 32)
         cp(sub(xf, 0, 128), V("qc", 0, 128), True)
-        jf = aff(S("jf", HF, 128), sub(xf, 0, 128), 1.0 / 32, 1164.0 - 15.5 / 32)
-        jl, jr = sub(jf, 0, 64), sub(jf, 64, 64)
-        aff(sub(ma, L, L), sub(ma, 0, L), -1.0, -8.0)
-        gtt(kk, kp, hoff, c, mul)
+        jl, jr, xl, xr, off = sub(jf, 0, 64), sub(jf, 64, 64), sub(xf, 0, 64), sub(xf, 64, 64), sub(cdc, 0, 64)
+        pj, pl = V("qc", 128, 128), V("qc", 256, 128)
+        mms(acc(every(pj, 0, 2, 64), [(ip, jr), (im, jl)]) + acc(every(pj, 1, 2, 64), [(ip, jl)])
+            + acc(every(pl, 0, 2, 64), [(ip, xr), (im, xl), (m32, jr), (p32, jl)]) + acc(every(pl, 1, 2, 64), [(ip, xl), (m32, jl), (im, off)]))
+        unit = UNIT / 2 ** (t + 1)
         for j in range(2):
-            aff(sub(cw, LB + j * L, L), kk, 2.0, 2.0 * j - 1)
-        dma("G", sub(cw, LB, 2 * L), ma, 1400, True)
-        gtt(sub(aw, LB, L), sg, xlo, A, mul)
-        gtt(sub(aw, LB + L, L), sg, xro, A, mul)
-        for j in range(SA[t]):
-            w = 2 * L // SA[t]
-            dma("G", sub(aw, LB + j * w, w), sub(ma, j * w, w), 1400 // SA[t], True)
+            aff(sub(cw, LB + j * L, L), mp, (6.0 - unit, -6.0)[j], (-6.0, unit)[j])
+        for a, w in (PV if HALF else [(0, L)]):
+            gtt(sub(cw, OLD + a, w), kq_, sub(hk, a // 16, w // 16), sub(c, a, w), mul)
+        if t == 0:
+            aw = w0
+        if t == STEPS - 1:
+            dma("S", sub(kp, H0, L), T.kap[:, H0:H], 256)
+        for j in range(2):
+            if FILL[t] == 2:
+                aff(sub(aw, LB + j * L, L), mp, (6.0, -6.0)[j], (-6.0, 0.0)[j])
+            elif FILL[t]:
+                dma("S", sub(aw, LB + j * L, L), sub(cw, LB + j * L, L), 512)
+            dma("G", sub(cw, LB + j * L, L), sub(cw, OLD, L), 700, True)
+
+        def sections():
+            for j in range(2 if t else 0):
+                dma("G" if FILL[t] else "S", sub(aw, LB + j * L, L), A, 700 if FILL[t] else 512, FILL[t] > 0)
+            for j in range(0 if FILL[t] else SA[t]):
+                w = 2 * L // SA[t]
+                dma("G", sub(aw, LB + j * w, w), sub(cw, LB + j * w, w), (1400 if t else 1000) // SA[t], True)
         qe = V("qe", 0, 128)
         dj, jx, qp, qj, qz = every(qe, 0, 2, 64), every(qe, 1, 2, 64), V("qe", 128, 64), V("qe", 192, 64), V("qe", 256, 64)
-        mms(acc(qp, [(im, rfo), (km1, fr), (km1, fr), (km1, fr)]) + (acc(qz, [(kp1, fr), (kp1, fr)]) if t else []))
+        mms(acc(qp, [(im, rfo), (km3, fr)]) + acc(qz, [(kp2, fr)]) if t else acc(qp, [(im, rfo), (km1, fr), (km1, fr), (km1, fr)]))
         p0 = tt(S("p0"), qp, nlid, OP.min)
         mms(acc(dj, [(ip, jl), (im, jr)]))
         kq1 = S("kq1", HF, 128)
@@ -394,18 +470,20 @@ def build(T, topo, core, FAC, GA, SC, GI=1.0, AC=1.0, PF=1.0):
         else:
             ts(capv, dj, 0.0, OP.is_equal, 2047.0, plus)
             tt(jx, qz, jr, OP.max)
+            keyl = tt(S("keyl", HF), qz, capv, OP.max) if TWICE[t] else None
             cnt = sub(S("cnt", F, 16), 8 * (t - 1), 8)
-            mms([(V("qe", 448, 2), ip, sub(kc, 1, 2), True, False), (n0a, onh, sub(cnt, 0, 1), False, False), (n0b, onh, sub(cnt, 0, 1), False, True)])
-            mms(acc(mc_, [(kp1, one1)], last=False))
-            mms(acc(mc_, [(onh, sub(cnt, 0, 1)), (osh, sub(cnt, 4, 1))], first=False))
+            mms(acc(mc_, [(kp1, one1), (onh, sub(cnt, 0, 1)), (osh, sub(cnt, 4, 1))]))
             isa = ts(S("isa", HF), rfo, 2048.0, plus, mc_, OP.is_lt)
-            aj0 = ts(S("aj0", HF), rfo, n0a, OP.is_ge, n0b, mul)
-        au = act(S("au"), u, AF.Abs, 1.0, 128.0)
-        ts(lw, u, -128.0, OP.is_ge)
+        au = act(S("au"), u, AF.Abs)
+        act(lw, u, AF.Sigmoid, 200.0, 50.0, alt=tsv(lw, u, 0.0, OP.is_ge))
         tt(sub(dis, 0, 64), au, hs, OP.is_lt)
+        mark["dis"] = len(ops) - 1
+        if t:
+            amps(*later, [mark[x] for x in LAG[t - 1]])
+        sections()
         scd = scan(S("scd", B, 65), sub(rs, 0, 65), dis)
         rd, ndc, nda = V("qa", 0, 64), V("qa", 64, 1), V("qa", 72, 1)
-        mms(acc(V("qa", 0, 65), [(tri, dis), (km1, dis), (km1, dis), (ones, scd)], last=False) + acc(ndc, [(ip, sub(kc, 0, 1))], first=False)
+        mms(acc(V("qa", 0, 65), [(tri, dis)] + ([(km2, dis)] if t else [(km1, dis)] * 2) + [(ones, scd)], last=False) + acc(ndc, [(ip, sub(kc, 0, 1))], first=False)
             + (acc(nda, [(ones, sub(scd, ks - 1, 1)), (ip, sub(kc, 0, 1))]) if ks else []))
 
         def cmp(o, x, sign, y, op):
@@ -413,121 +491,167 @@ def build(T, topo, core, FAC, GA, SC, GI=1.0, AC=1.0, PF=1.0):
         if t:
             scan(kq1, kd0, qe)
         cmp(par, rd, plus, nfc, OP.is_lt)
-        xa, xb = tt(S("xa", HF), lw, xl_, mul), tt(S("xb", HF), lw, xr_, mul)
+        jo, lo = [every(scan(S(nm, HF, 128), kd0, x), 1, 2, 64) for nm, x in (("jo", pj), ("lo", pl))]
         if t:
             key = every(scan(S("kq2", HF, 128), kq0, kq1, OP.max), 1, 2, 64)
+            mms([(V("qc", 384, 2), ip, sub(kc, 1, 2), True, False), (n0a, onh, sub(cnt, 0, 1), False, False), (n0b, onh, sub(cnt, 0, 1), False, True)])
+            aj0 = ts(S("aj0", HF), rfo, n0a, OP.is_ge, n0b, mul)
             mms(acc(qj, [(ip, cj[t - 1]), (ip, rfo), (im, aj0), (bm, isa)]))
             pre = tt(S("pre"), qj, tw, OP.min)
-        fq = [V("qd", 64 * j, 64) for j in range(3)]
-        mms([(V("qd", 0, 192), ip, xf, True, False)] + [(fq[j], l, x, False, False) for j, l, x in ((1, bm, fr), (2, bm, fr), (2, kp1, ngo))])
-        mms([(fq[j], l, x, False, j == 2) for j, l, x in ((0, im, xa), (0, ip, xb), (1, ip, xa), (1, im, xb), (2, km1, lw))])
-        fc = cp(S("fc", HF, 192), V("qd", 0, 192), True)
+        end = t == STEPS - 1
+        fb = V("qd", 0, 128)
+        fq = [sub(fb, 64 * j, 64) for j in range(2)]
+        mms([(fb, ip, sub(xf, 64, 128), True, False)]
+            + [(fq[j], l, x, False, False) for j, l, x in ((0, ip, xl), (0, im, off), (0, bm, fr), (1, bm, fr), (1, km1, rest), (1, km1, lw), (0, m32, jo))]
+            + [(fq[0], im, lo, False, True)])
+        fc = cp(S("fc", HF, 128), fb, True)
         qw = V("qr1", 0, 256)
-        code = [key, None, sub(fc, 128, 64), sub(fc, 0, 64)]
-        mms([(qw, ip, idq, True, False)])
-        for fs in KORD[t]:
-            mms([(every(qw, u, 4, 64), sub(mu[u], 12 - 4 * (f - u), 128), code[f], False, fs is KORD[t][-1] and f == fs[-1] and u == 3) for f in fs for u in range(4)])
+        code = [(mu, key), (muk, lw), (mu, jo), (mu, lo)]
+
+        def ahead(f, m, x, last=False):
+            return [(every(qw, u, 4, 64), sub(m[u], 12 - 4 * (f - u), 128), x, False, last and u == 3) for u in range(4)]
+        def rows(j, x):
+            mms([(every(qr[j], r, 4, 128), sub(mmq, 128 * r, 128), sub(x, 128 * j, 128), True, True) for r in range(4)])
+        split = TWICE[t]
+        if split:
+            code[0] = (mu, keyl)
+        mms([(qw, ip, idq, True, False)] + (ahead(0, muk, one64) if t == 0 else [] if split else ahead(1, muk, rest)))
+        kord = KORD[1 if split else 2 if t else 0]
+        for fs in kord:
+            mms([m for f in fs for m in ahead(f, code[f][0], code[f][1], fs is kord[-1] and f == fs[-1])])
         wsb = cp(S("wsb", HF, 256), qw, True)
         for j in range(2):
-            mms([(every(qr[j], r, 4, 128), sub(mmq, 128 * r, 128), sub(wsb, 128 * j, 128), True, True) for r in range(4)])
-            aff(sub(zz, ZC + 512 * j, 512), qr[j], 1.0, OFF)
+            rows(j, wsb)
+            if j == 0:
+                aff(sub(xs, 0, 512), qr[j], EPS, inx)
+            if j or (t and not split):
+                aff(sub(xs if split else zz, (0 if split else ZC) + 512 * j, 512), qr[j], BETA, inb)
         posf = tt(S("posf"), rd, p0, OP.min)
         pos = to16(S("pos", U), posf, 1.0, 2048.0)
-        if ks:
-            scat(sub(zz, ZA, 2 * L + 8), sub(pos, 0, ks), sub(zz, ZC, 16 * ks), sv0)
-        scat(sub(zz, ZB, 2 * L + (0 if ks else 8)), sub(pos, ks, 64 - ks), sub(zz, ZC + 16 * ks, L - 16 * ks))
+        scat(sub(zz, ZA, 2 * L + 8), sub(pos, 0, ks), sub(xs, 0, 16 * ks), True)
+        scat(sub(zz, ZB, 2 * L), sub(pos, ks, 64 - ks), sub(xs, 512, 512) if split else sub(zz, ZC + 16 * ks, L - 16 * ks))
+        if split:
+            qw = V("qd", 256, 256)
+            mms([(qw, ip, idq, True, False)] + ahead(1, muk, rest) + ahead(1, muk, lw))
+            mms(ahead(0, mu, key, True))
+            wsb = cp(S("wsb2", HF, 256), qw, True)
+            for j in range(2):
+                rows(j, wsb)
+                aff(sub(zz, ZC + 512 * j, 512), qr[j], BETA, inb)
         qv = aff(S("qv", HF), posf, -1.0, 0.0) if t == 0 else ts(S("qv", HF), posf, mc_, plus, -1.0, mul)
         js = [cmp(S("j1", HF), rd, plus, nfa, OP.is_lt), cmp(S("j2", HF), rfo, minus, nda, OP.is_lt)] if ks else []
         nba = cmp(S("nba", HF), rfo, minus, ndc, OP.is_ge)
         pp = V("qb", 0, 64)
-        mms(acc(pp, [(ip, qv), (bp, par), (bm, nba)] + [(kp1, x) for x in js + js] + ([(bm, isa)] if t else [])))
-        idx = to16(S("idx", U), tt(S("idf"), pp, pre, OP.max), 1.0, float(ZC - ws))
+        mms(acc(pp, [(ip, qv), (bp, par), (bm, nba)] + ([(kp2, x) for x in js] + [(bm, isa)] if t else [(kp1, x) for x in js + js])))
+        if t:
+            idx = to16(S("idx", U), tt(S("idf"), pp, pre, OP.max), 1.0, float(ZC - ws))
+        else:
+            idx = ts(S("idx", U), pp, L - 1.0, OP.max)
         for a, w in PV:
-            aff(sub(g2, a, w), sub(zz, ws, ZA + 2 * L + 8 - ws), 1.0, -OFF, sub(idx, a // 16, w // 16))
-        mms(acc(V("qe", 320, 64), [(ip, own), (kp1, one64), (kp1, lw), (bp, par), (bm, one64)]) + acc(V("qe", 384, 64), [(bp, one64), (bm, fr), (bm, nba)]))
-        o2 = cp(S("o2", F, 128), V("qe", 320, 128), True)
+            aff(sub(g2, a, w), sub(zz, ws, ZA + 2 * L + 8 - ws), 1.0 / BETA, outb, sub(idx, a // 16, w // 16))
+        still, o2 = V("qe", 320, 64), V("qe", 384, 64)
+        mms(([] if end and EARLYA else acc(still, [(k4, rest), (k4, fr), (m2, kilo)] + ([(bp, isa)] if t else []))) + acc(o2, [(bp, one64), (bm, fr), (bm, nba)])
+            + acc(qp, [(ip, own), (kp1, one64), (kp1, lw), (bp, par), (bm, one64)]))
+        mine = cp(S("mine"), qp, True)
         q4 = V("qr0", 0, 256)
         mms(acc(q4, [(sub(qb_, 3 - r, 128), every(g2, r, 4, 256)) for r in range(4)]))
         qsb = cp(S("qsb", HF, 256), q4, True)
 
         def back(m, f):
             return [(sub(m, 12 - 4 * (u - f), 128), every(qsb, u, 4, 64)) for u in range(4)]
-        pk, qt = V("qa", 0, 64), V("qb", 0, 128)
-        pd = every(qt, 0, 2, 64)
-        mms(acc(pk, [(ip, key)] if t == 0 else [(im, key), (bp, fr), (bp, nba), (bp, isa)], last=False))
-        mms((acc(every(qt, 1, 2, 64), [(ip, lidh)]) if t == 1 else []) + acc(pd, [(im, lidh), (km1, one64)], last=False))
-        mms(acc(pk, back(mu[0], 0), first=False))
-        mms(acc(pd, back(mu[1], 1), first=False))
-        mq = [V("qc", 0, 64), V("qc", 64, 64), V("qe", 0, 64)]
+        pk, pr, r1 = V("qa", 0, 64), V("qb", 0, 64), V("qb", 64, 64)
         end = t == STEPS - 1
-        if end:
-            mq[0] = V("qd", 0, 64)
-            mms(acc(mq[0], [(bm, nba)], last=False))
-            mms(acc(mq[0], back(mu[3], 3), False))
-            tt(sub(rt_, 0, 64), mq[0], sub(fc, 64, 64), OP.max)
-            mms(acc(mq[1], [(ip, sub(cdc, 64, 64)), (bm, nba), (bm, nba)], last=False))
-        else:
-            mms([(V("qc", 0, 128), ip, cdc, True, False)] + [(mq[j], bm, nba, False, False) for j in (0, 1, 1)])
-        mms(acc(mq[2], [(kp1, one64), (kp1, one64)], last=False))
-        mms(([] if end else acc(mq[0], back(mu[3], 3), False, False)) + acc(mq[1], back(mu1d, 1) + back(mu2n, 2), False))
-        f8 = ts(S("f8"), pk, 0.5, OP.is_lt, BIG, mul) if t == 0 else ts(S("f8"), pk, BIG, OP.is_equal, BIG, mul)
-        if end:
-            tt(sub(rt_, 64, 64), mq[1], sub(fc, 128, 64), OP.max)
-        else:
-            tt(rt_, V("qc", 0, 128), sub(fc, 64, 128), OP.max)
-        mms(acc(mq[2], back(mu[2], 2), False))
-        eb = tt(V("qm", 64, 64), f8, pd, mul)
-        r2 = tt(S("r2"), mq[2], sub(o2, 0, 64), OP.max)
-        upn = tt(V("qm", 128, 64), eb, sub(o2, 64, 64), OP.min)
+        mq = [V("qc", 0, 64), V("qc", 64, 64)]
+        mms([(V("qc", 0, 128), ip, cdc, True, False)] + [(mq[j], bm, nba, False, False) for j in (0, 1, 1)])
+        mms(acc(pk, [(ip, key), (bp, nba), (bm, par)] if t == 0 else [(im, key), (bp, fr), (bp, nba), (bp, isa)], last=False))
+        mms(acc(pr, [(im, lidh), (kp1, one64), (im, ntop)], last=False))
+        far = V("qd", 0, 64)
+        mms(acc(far, [(bm, par), (m2, ntop), (ip, cfar)], last=False))
+        mms(acc(mq[0], back(mu32, 2) + back(mu[3], 3), False, False) + acc(mq[1], back(mu[1], 1), False))
+        mms(acc(pr, back(mu[1], 1), first=False))
+        mms(acc(pk, back(mu[0], 0), first=False))
+        tt(rt_, V("qc", 0, 128), fc, OP.max)
+        side = tt(S("side", B), pr, lidc, plus)
+        pd = tt(S("pd", I), pr, side, minus)
+        mms(acc(far, back(mu[1], 1) + [(m2, side)], first=False))
+        f8 = V("qm", 64, 64)
+        ts(f8, pk, 1024.5, OP.is_lt, BIG, mul) if t == 0 else ts(f8, pk, BIG, OP.is_equal, BIG, mul)
+        eb = tt(S("eb"), f8, pd, mul)
+        upn = tt(V("qm", 128, 64), eb, o2, OP.min)
         h = sub(rt_, 0, 64)
-        if t < STEPS - 1:
-            to16(sub(so, 0, 128), rt_, 1.0, 2048.0)
+        hsg = S("hsg", U)
+        if end:
+            to16(s1, sub(rt_, 64, 64), 1.0, 2048.0)
+            s1c = to16(S("s1c", U), tt(S("s1f"), upn, sub(rt_, 64, 64), plus), 1.0, 2048.0)
+            ts(hoff, tt(S("hk"), h, upn, minus), 2048.0, OP.min, 2048.0, plus)
         else:
-            to16(s1, tt(S("s1f"), upn, sub(rt_, 64, 64), plus), 1.0, 2048.0)
-            to16(hoff, h, 1.0, 2048.0)
-        to16(s2, tt(S("s2f"), eb, r2, OP.min))
-        c, A = sub(cn, OLD, L), sub(an, OLD, L)
+            to16(sub(so, 0, 128), rt_, 1.0, 2048.0)
+            ts(hk, h, 2048.0, plus, float(H0), OP.min)
+        to16(s2, tt(S("s2f"), eb, tt(V("qm", 320, 64), far, mine, OP.max), OP.min))
+        if not (end and EARLYA):
+            to16(hsg, tt(S("hsf"), still, h, OP.max), 1.0, 2048.0)
+            mate = to16(S("mate", U), tt(S("matef"), eb, lidb, plus), 1.0 / BIG)
+        c, A = sub(cs, 0, L), sub(an, OLD, L)
         cwin, awin = sub(cw, 0, WW), sub(aw, 0, WW)
-        for a, w in (PV if t < STEPS - 1 else [(j * L // LAST, L // LAST) for j in range(LAST)]):
+        for a, w in PV:
+            gat(sub(c1, a, w), cwin, sub(s1c if end else s1, a // 16, w // 16))
+
+        def amps(t, A, awin, an, mate, behind):
+            cut = PV if HALFA[t] else [(0, L)]
+            for a, w in cut:
+                act(sub(sg, a, w), dm, AF.Sigmoid, off=sub(hsg, a // 16, w // 16))
+                ops[-1]["after"] += behind
+                gtt(sub(a1, a, w), awin, sub(s1, a // 16, w // 16), sub(sg, a, w), mul)
+                if COPY[t]:
+                    dma("S", sub(kk, a, w), sub(a1, a, w), w // 2)
+                else:
+                    act(sub(kk, a, w), sub(a1, a, w), AF.Relu, alt=tsv(sub(kk, a, w), sub(a1, a, w), 0.0, OP.max))
+            for a, w in cut:
+                gtt(sub(A, a, w), a1, sub(mate, a // 16, w // 16), sub(kk, a, w), OP.max)
+            if t < STEPS - 1:
+                leave(t, 1, an, gat(S("sa%d" % t, F, 128), sub(an, OLD, L + 8), S("lno")))
+        if not end:
+            later = (t, A, awin, an, mate)
+        elif not EARLYA:
+            amps(t, A, awin, an, mate, [])
+        for a, w in PV:
             o = (a // 16, w // 16)
-            if end:
+            gtt(sub(c, a, w), cwin, sub(s2, *o), sub(c1, a, w), OP.max)
+            if not end:
+                over(sub(nl, a, w), sub(c, a, w), -4 * UNIT)
+                over(sub(mp, a, w), sub(c, a, w), 0.0)
+                mark["mp"] = len(ops) - 1
+                continue
+            if EARLYA:
                 act(sub(a1, a, w), awin, AF.Relu, off=sub(s1, *o), alt=tsv(sub(a1, a, w), awin, 0.0, OP.max, off=sub(s1, *o)))
                 gtt(sub(A, a, w), awin, sub(s2, *o), sub(a1, a, w), OP.max)
-            elif a == 0:
-                act(a1, awin, AF.Relu, off=s1, alt=tsv(a1, awin, 0.0, OP.max, off=s1))
-                gtt(A, awin, s2, a1, OP.max)
-            gat(sub(c1, a, w), cwin, sub(s1, *o))
-            gtt(sub(c, a, w), cwin, sub(s2, *o), sub(c1, a, w), OP.max)
-            if t < STEPS - 1:
-                act(sub(nl, a, w), sub(c, a, w), AF.Sign, -1.0, -2.0)
-                ts(sub(mn, a, w), sub(c, a, w), 0.0, OP.is_lt, -8.0, mul)
+            y = sub(sg, a, w)
+            if a // w < KG:
+                kq = V(("qd", "qc")[a // w % 2], 0, w)
+                mms(acc(kq, [(ip, gat(sub(c0, a, w), kp, sub(hoff, *o)))]))
+                tt(y, sub(A, a, w), kq, mul)
             else:
-                lv = aff(V("qr%d" % (a // w % 2), 0, w), sub(A, a, w), -BIG, 0.0)
-                dma("S", T.yc[:, a:a + w], tt(sub(a1, a, w), sub(c, a, w), lv, OP.max), w // 2)
-                if a // w < KG:
-                    kq = V(("qc", "qd")[a // w % 2], 0, w)
-                    mms(acc(kq, [(ip, gat(sub(c0, a, w), kp, sub(hoff, *o)))]))
-                    tt(sub(kk, a, w), sub(A, a, w), kq, mul)
-                else:
-                    gtt(sub(kk, a, w), kp, sub(hoff, *o), sub(A, a, w), mul)
-                dma("S", T.ya[:, a:a + w], sub(kk, a, w), w // 2)
-        if t == STEPS - 1:
+                gtt(y, kp, sub(hoff, *o), sub(A, a, w), mul)
+            lv = V("qr%d" % (a // w % 2), 0, w)
+            on = over(sub(mp, a, w), sub(c, a, w), -4 * UNIT)
+            mms(acc(lv, [(whole, on)]))
+            dma("S", T.ya[:, a:a + w], y, w // 2)
+            dma("S", T.yc[:, a:a + w], tt(sub(xs, a, w), sub(c, a, w), lv, mul), w // 2)
+        if end:
             break
-        if t == 0:
-            tw = tt(S("tw"), pd, lid, plus)
-        else:
-            ts(every(kt0, 1, 2, 64), pk, BIG + 200.0, OP.is_lt)
-            tw = every(scan(S("tw2", F, 128), kt0, qt), 1, 2, 64)
+        bound, stays = BIG + 200.0 if t else BIG / 2, S("stays", HF)
+        act(stays, pk, AF.Sigmoid, -1.0, bound, alt=tsv(stays, pk, bound, OP.is_lt))
+        tw = tt(S("tw"), tt(V("qm", 192, 64), stays, pd, mul), lid, plus)
         z = tt(S("z"), upn, ts(S("y", I), h, 3073, OP.bitwise_and), plus)
         ts(sub(de, 0, 64), z, 1024.0, OP.is_equal)
         ts(sub(do, 0, 64), z, 1025.0, OP.is_equal)
-        ts(sub(sf, 0, 64), upn, 0.0, OP.is_lt)
+        act(sub(sf, 0, 64), upn, AF.Sigmoid, -1.0, -100.0, alt=tsv(sub(sf, 0, 64), upn, 0.0, OP.is_lt))
         scan(scs, rs, seg)
         d64 = [sub(x, 0, 64) for x in (de, do, sf, ce, co, cf)]
         rank_ = [(tri, d64[0]), (tri, d64[1]), (ones, d64[3]), (ones, d64[4])]
-        xe, xo_ = V("qb", 0, 64), V("qd", 0, 64)
-        mms(acc(xe, rank_ + [(bm, d64[0])]))
-        mms(acc(xo_, rank_ + [(bm, d64[1])]))
+        xe, xo_ = V("qb", 0, 64), V("qb", 64, 64)
+        mms([(xe, bm, d64[0], True, False), (xo_, bm, d64[1], False, False)] + [(x, tri, y, False, False) for x in (xe, xo_) for y in d64[:2]])
+        mms([(x, ones, y, False, x is xo_ and y is d64[4]) for x in (xe, xo_) for y in d64[3:5]])
         sc_, cnt = S("sc%d" % t, F, 16), S("cnt", F, 16)
         le, lo_ = [act(S("le%d" % j, HF), x, AF.Sign, -1.0, CAP - 0.5 - BIG, acc=sub(sc_, 4 * j, 1)) for j, x in enumerate((xe, xo_))]
         send([(sub(sc_, 0, 1), sub(cnt, 8 * t, 1), to1), (sub(sc_, 4, 1), sub(cnt, 8 * t + 4, 1), to2)], "rc%d" % t, [sub(cnt, 8 * t, 8)])
@@ -538,8 +662,9 @@ def build(T, topo, core, FAC, GA, SC, GI=1.0, AC=1.0, PF=1.0):
         mms(acc(be, [(ones, sub(scs, 0, 2 * SW))]))
         mms(acc(sub(cq, 0, SW), [(tri, de), (ones, ce), (bm, de)]) + acc(sub(cq, SW, SW), [(tri, do), (ones, co), (bm, do)]))
         qf = [V("qr0", 64 * j, 64) for j in range(3)]
-        mms(acc(qf[0], [(tri, d64[2]), (ones, d64[5]), (ip, c84), (km1, d64[2]), (km1, d64[2]), (im, sub(r64, 0, 64)), (km1, le), (km1, lo_)])
-            + acc(qf[1], [(ip, d64[2]), (ip, one64), (hp, le), (hp, lo_)]) + acc(qf[2], [(ip, x) for x in d64[:3]]))
+        mms(acc(qf[0], [(tri, d64[2]), (ones, d64[5]), (ip, c84), (km2, d64[2]), (im, sub(r64, 0, 64)), (km1, le), (km1, lo_)])
+            + acc(qf[1], [(ip, d64[2]), (ip, one64), (hp, le), (hp, lo_)])
+            + acc(qf[2], [(ip, one64), (hp, le), (hp, lo_), (im, d64[0]), (im, d64[1])]))
         cp(rf, V("qr0", 0, 192), True)
         k2 = KS[t + 1]
         mms(acc(nfc, [(ones, sub(cf, 64, 1)), (ip, sub(c84, 0, 1)), (im, sub(r64, 64, 1))])
@@ -547,30 +672,23 @@ def build(T, topo, core, FAC, GA, SC, GI=1.0, AC=1.0, PF=1.0):
         w2 = aff(S("w2", F, 2 * SW), cq, 1.0, BIG)
         kbs = S("kbs", F, 8)
         for j in range(8):
-            act(S("jk%d" % (j % 2), B), V("qd", SW * (j // 4), 64), AF.Sign, -1.0, sub(jh, j % 4, 1), acc=sub(kbs, j, 1))
+            act(S("jk%d" % j, B), V("qd", SW * (j // 4), 64), AF.Sign, -1.0, sub(jh, j % 4, 1), acc=sub(kbs, j, 1))
         ko = to16(S("ko", U, 8), kbs, 0.5, 32.0)
         msk = S("msk", B, 128)
         for j in range(2):
             gtt(sub(msk, 64 * j, 64), sub(w2, SW * j, SW), sub(ko, 4 * j, 4), i64, OP.is_equal)
+        ql = V("qd", 400, 8)
+        mms([(ql, f8i, kbs, True, False)])
+        wrap(ql, bim, msk, 8, first=False)
+        lno = to16(S("lno", U, 8), ql, 1.0, 512.0)
         hvm = gtt(S("hvm", HF, 128), sub(rt_, 0, SW), ko, msk, mul)
         vr = V("qd", 256, 128)
-        mms(acc(sub(vr, 0, 64), [(sub(b1, 28, 128), sub(hvm, 0, 64))]) + acc(sub(vr, 64, 64), [(sub(b1, a, 128), sub(hvm, 64, 64)) for a in (12, 140)]))
-        sv = tt(S("sv%d" % (t + 1), F, 128), vr, svc, plus)
+        mms([(vr, ip, svc, True, False)] + acc(sub(vr, 0, 64), [(sub(b1, 28, 128), sub(hvm, 0, 64))], False, False)
+            + acc(sub(vr, 64, 64), [(sub(b1, a, 128), sub(hvm, 64, 64)) for a in (12, 140)], False))
+        sv = aff(S("sv%d" % (t + 1), F, 128), vr, BETA, inb)
         av = ws - 128
         send([(sub(sv, 0, 64), sub(zz, av, 64), to1), (sub(sv, 64, 64), sub(zz, av + 64, 64), to2)], "rv%d" % t, [sub(zz, av, 128)])
-        ql = V("qr1", 256, 8)
-        wrap(ql, bim, msk, 8, last=False)
-        mms([(ql, f8i, kbs, False, True)])
-        lno = to16(S("lno", U, 8), ql, 1.0, 512.0)
-        sd, sh = S("sd%d" % t, F, 256), S("sh%d" % t, F, 128)
-        gat(sub(sd, 0, 128), sub(cn, OLD, L + 8), lno)
-        gat(sub(sd, 128, 64), sub(an, OLD, L + 8), sub(lno, 4, 4))
-        gat(sub(sd, 192, 64), sub(an, OLD, L + 8), sub(lno, 0, 4))
-        dma("S", sub(sh, 0, 128, slice(16, 128)), sub(sd, 64, 128, slice(0, 112)), 64)
-        dma("S", sub(sh, 0, 128, slice(0, 16)), sub(sd, 64, 128, slice(112, 128)), 64)
-        send([(sub(sd, 0, 64), sub(cn, ARR, 64), to1), (sub(sd, 192, 64), sub(an, ARR, 64), to1),
-              (sub(sh, 0, 64), sub(cn, ARR + 64, 64), to2), (sub(sh, 64, 64), sub(an, ARR + 64, 64), to2)],
-             "rd%d" % t, [sub(cn, ARR, 128), sub(an, ARR, 128)])
+        leave(t, 0, cn, aff(S("sd%d" % t, F, 128), cs, 0.5, 0.0, lno))
     up = []
     for o in ops:
         for d in [d for d, hard in o["deps"].items() if not hard and len(o["alts"]) == 1 and list(ops[d]["alts"]) == list(o["alts"])]:
@@ -593,24 +711,34 @@ def schedule(ops, others):
     n = len(ops)
     deps = [o["all"] for o in ops]
     pipe = [o["pipe"] for o in ops]
+    pipes = [[o["pipe"] for o in oth] for oth in others]
     cost = [[dict([(None, 0.0)] + [(e, a[0]) for e, a in o["alts"].items()]) for o in oth] for oth in others]
     late = [[o["lat"] + (0.0 if o["pipe"] is None else w[5] if o["remote"] else w[6]) for o in oth] for oth, w in zip(others, CASES)]
 
     succ = [[s for s in range(n) if k in deps[s]] for k in range(n)]
     flex = [k for k, o in enumerate(ops) if len(o["alts"]) > 1 and "V" in o["alts"]]
 
-    def length(seq, eng, i=0, old=None, room=1e9):
+    QS = list("VAPGS") + ["pipe", None]
+
+    def length(seq, eng, i=0, old=None, room=1e9, j=10 ** 9, touched=()):
         before = {}
         for k in seq[:i]:
             before[eng[k]] = k
-            if pipe[k] is not None:
+            if pipes[0][k] is not None:
                 before["pipe"] = k
         new, total, way = [], 0.0, []
         for c, w in enumerate(CASES):
             fin, why, end, pend = [x[:] for x in old[c][:4]] if old else ([0.0] * n, [None] * n, [0.0] * n, [0.0] * n)
-            last, hop, own, co, la = dict(before), w[3], w[4], cost[c], late[c]
-            for k in seq[i:]:
+            last, hop, own, co, la, pipe = dict(before), w[3], w[4], cost[c], late[c], pipes[c]
+            moved, stale = dict.fromkeys(QS, True), set(touched)
+            for at, k in enumerate(seq[i:], i):
                 e = eng[k]
+                p = pipe[k]
+                if at > j and not moved[e] and k not in stale and (p is None or not moved["pipe"]):
+                    last[e] = k
+                    if p is not None:
+                        last["pipe"] = k
+                    continue
                 y = last.get(e) if e else None
                 t = 0.0 if y is None else end[y]
                 for d in deps[k]:
@@ -619,17 +747,21 @@ def schedule(ops, others):
                         t = u
                         y = d
                 t += co[k][e]
+                moved[e] = at <= j or t != end[k]
                 end[k] = t
                 last[e] = k
-                p = pipe[k]
                 if p is not None:
                     d = last.get("pipe")
                     if d is not None and pend[d] > t:
                         t = pend[d]
                         y = d
+                    moved["pipe"] = at <= j or t + p != pend[k]
                     pend[k] = t + p
                     last["pipe"] = k
-                fin[k] = t + la[k]
+                t += la[k]
+                if t != fin[k]:
+                    fin[k] = t
+                    stale.update(succ[k])
                 why[k] = y
             m = max(fin)
             part = (m + MEAN * sum(fin) / n) / w[7]
@@ -671,7 +803,7 @@ def schedule(ops, others):
                 x = (x * 1103515245 + 12345) % 2 ** 31
                 i = lo + (x >> 8) % (hi - lo + 1)
                 s2.insert(i, k)
-                i = min(i, j)
+                i, j = min(i, j), max(i, j)
                 if len(ops[k]["alts"]) > 1 and (x >> 5) % 3 == 0:
                     e2 = list(eng)
                     e2[k] = [e for e in ops[k]["alts"] if e != eng[k]][0]
@@ -681,7 +813,7 @@ def schedule(ops, others):
                     continue
                 e2 = list(eng)
                 e2[k] = [e for e in ops[k]["alts"] if e != eng[k]][0]
-                i = seq.index(k)
+                i = j = seq.index(k)
             else:
                 i, j = seq.index(a), seq.index(b)
                 if u == 7:
@@ -710,12 +842,199 @@ def schedule(ops, others):
                 s2 = seq[:i] + part + seq[j + 1:]
             x = (x * 1103515245 + 12345) % 2 ** 31
             room = HEAT * (1 - it / CLIMB) * (x / 2.0 ** 31) ** 3
-            m, w2, new = length(s2, e2, i, old, len(CASES) * room + (LAM if e2 is not eng else 0.0))
+            m, w2, new = length(s2, e2, i, old, len(CASES) * room + (LAM if e2 is not eng else 0.0), j, succ[k] if e2 is not eng else ())
             if m <= now + room:
                 now, seq, eng, way, old = m, s2, e2, w2, new
                 if m < best:
                     best, keep = m, (seq, eng, old)
         BEST.append(keep + (best,))
+    seq, eng = BEST[0][:2]
+    for o, e in zip(ops, eng):
+        o["eng"] = e
+    return {e: [k for k in seq if eng[k] == e] for e in "VAPGS"}
+
+
+def improve(ops, others, seq, eng):
+    n = len(ops)
+    deps = [o["all"] for o in ops]
+    succ = [[] for _ in range(n)]
+    for k in range(n):
+        for d in deps[k]:
+            succ[d].append(k)
+    pipes = [[o["pipe"] for o in oth] for oth in others]
+    cost = [[dict([(None, 0.0)] + [(e, a[0]) for e, a in o["alts"].items()]) for o in oth] for oth in others]
+    late = [[o["lat"] + (0.0 if o["pipe"] is None else w[5] if o["remote"] else w[6]) for o in oth] for oth, w in zip(others, CASES)]
+    other = [dict(zip(o["alts"], list(o["alts"])[::-1])) if len(o["alts"]) > 1 else None for o in ops]
+    fee = [LAM * cost[0][k]["V"] if other[k] and "V" in other[k] else 0.0 for k in range(n)]
+    QS = list("VAPGS") + ["pipe"]
+
+    def rest(seq, eng, old, a, b):
+        behind, res = set(seq[b:]), []
+        for c, w in enumerate(CASES):
+            hop, own, co, la, pipe = w[3], w[4], cost[c], late[c], pipes[c]
+            q, nxt = [0.0] * n, dict.fromkeys(QS + [None], 0.0)
+            for k in reversed(seq[b:]):
+                e = eng[k]
+                t = la[k] + max([q[s] + (own if eng[s] == e else hop) for s in succ[k]] or [0.0])
+                if pipe[k] is not None:
+                    t = nxt["pipe"] = max(t, pipe[k] + nxt["pipe"])
+                q[k] = co[k][e] + (max(t, nxt[e]) if e else t)
+                nxt[e] = q[k]
+
+            def out(k, e):
+                return max([q[s] + (own if eng[s] == e else hop) for s in succ[k] if s in behind] or [0.0])
+            outs = [(k, dict((e, out(k, e)) for e in co[k])) for k in seq[a:b] if not succ[k] or not behind.isdisjoint(succ[k])]
+            res.append((outs, nxt, max([old[c][0][k] + out(k, eng[k]) for k in seq[:a]] or [0.0])))
+        return res
+
+    def length(seq, eng, i, b, old, far, room=1e9):
+        before = dict.fromkeys(QS + [None], n)
+        for k in seq[:i]:
+            before[eng[k]] = k
+            if pipes[0][k] is not None:
+                before["pipe"] = k
+        new, total, way, part = [], 0.0, [], seq[i:b]
+        for c, w in enumerate(CASES):
+            fin, why, end, pend = [x[:] for x in old[c][:4]]
+            last, hop, own, co, la, pipe = dict(before), w[3], w[4], cost[c], late[c], pipes[c]
+            for k in part:
+                e = eng[k]
+                y = last[e] if e else n
+                t = end[y]
+                for d in deps[k]:
+                    u = fin[d] + (own if eng[d] == e else hop)
+                    if u > t:
+                        t = u
+                        y = d
+                t += co[k][e]
+                end[k] = t
+                last[e] = k
+                p = pipe[k]
+                if p is not None:
+                    d = last["pipe"]
+                    if pend[d] > t:
+                        t = pend[d]
+                        y = d
+                    pend[k] = t + p
+                    last["pipe"] = k
+                fin[k] = t + la[k]
+                why[k] = y
+            outs, nxt, m = far[c]
+            y = n
+            for k, o in outs:
+                t = fin[k] + o[eng[k]]
+                if t > m:
+                    m, y = t, k
+            for e in QS:
+                k = last[e]
+                t = (pend if e == "pipe" else end)[k] + nxt[e]
+                if t > m:
+                    m, y = t, k
+            v = (m + MEAN * sum(fin) / n) / w[7]
+            total += v
+            room -= v - old[c][4]
+            if room < -EARLY * (len(CASES) - 1 - c) - 1e-9:
+                return 1e9, None, None
+            while y < n:
+                if why[y] < n and why[y] not in deps[y]:
+                    way.append((why[y], y))
+                y = why[y]
+            new.append((fin, why, end, pend, v, m))
+        return total / len(CASES), way, new
+    none = [([], dict.fromkeys(QS, 0.0), 0.0)] * len(CASES)
+    zero = [([0.0] * (n + 1), [n] * (n + 1), [0.0] * (n + 1), [0.0] * (n + 1), 1e9)] * len(CASES)
+    starts = [a for _ in range(SWEEPS) for a in list(range(0, n - SPAN, SPAN // 2)) + [n - SPAN]]
+    x, keep = SEED, None
+    for turn, a0 in enumerate(starts):
+        b0 = a0 + SPAN
+        old = length(seq, eng, 0, n, zero, none)[2]
+        now = sum((max(o[0]) + MEAN * sum(o[0]) / n) / w[7] for o, w in zip(old, CASES)) / len(CASES) + sum(f for f, e in zip(fee, eng) if e == "V")
+        if keep is None or now < keep[3]:
+            keep = (seq, eng, old, now)
+        order = sorted(range(n), key=lambda j: (old[0][2][seq[j]] - cost[0][seq[j]][eng[seq[j]]], j))
+        if turn % (len(starts) // SWEEPS) == 0:
+            s2 = [seq[j] for j in order]
+            o2 = length(s2, eng, 0, n, zero, none)[2]
+            if sum(max(o[0]) for o in o2) <= sum(max(o[0]) for o in old) + 0.2:
+                seq, old = s2, o2
+        far = rest(seq, eng, old, a0, b0)
+        now, way, old = length(seq, eng, a0, b0, old, far)
+        inside = set(seq[a0:b0])
+        way = [p for p in way if p[0] in inside]
+        for it in range(CLIMB // len(starts)):
+            x = (x * 1103515245 + 12345) % 2 ** 31
+            if (x >> 23) % 8 < ANY or not way:
+                b = seq[a0 + (x >> 8) % SPAN]
+                a = old[(x >> 5) % len(CASES)][1][b]
+                if a not in inside or a in deps[b]:
+                    continue
+            else:
+                a, b = way[(x >> 8) % len(way)]
+            u = (x >> 20) % 8
+            s2, e2, flip = seq, eng, None
+            if (x >> 26) % 8 < FAR:
+                k = (a, b, seq[a0 + (x >> 6) % SPAN])[(x >> 4) % 3]
+                j = seq.index(k, a0)
+                s2 = seq[:j] + seq[j + 1:]
+                lo = max([s2.index(d, a0) + 1 for d in deps[k] if d in inside] or [a0])
+                hi = min([s2.index(d, a0) for d in succ[k] if d in inside] or [b0 - 1])
+                x = (x * 1103515245 + 12345) % 2 ** 31
+                i = lo + (x >> 8) % (hi - lo + 1)
+                s2.insert(i, k)
+                i = min(i, j)
+                if other[k] and (x >> 5) % 3 == 0:
+                    flip = k
+            elif u < 2:
+                flip = a if u else b
+                if not other[flip]:
+                    continue
+                i = seq.index(flip, a0)
+            else:
+                i, j = seq.index(a, a0), seq.index(b, a0)
+                if u == 7:
+                    i = max(a0, i - 1 - (x >> 4) % 12)
+                elif u == 6:
+                    j = min(b0 - 1, j + 1 + (x >> 4) % 12)
+                part = seq[i:j + 1]
+                if u % 2:
+                    need = set(deps[b])
+                    go = {b}
+                    for k in part[::-1]:
+                        if k in need:
+                            go.add(k)
+                            need.update(deps[k])
+                    if a in go:
+                        continue
+                    part = [k for k in part if k in go] + [k for k in part if k not in go]
+                else:
+                    go = {a}
+                    for k in part:
+                        if not go.isdisjoint(deps[k]):
+                            go.add(k)
+                    if b in go:
+                        continue
+                    part = [k for k in part if k not in go] + [k for k in part if k in go]
+                s2 = seq[:i] + part + seq[j + 1:]
+            extra = 0.0
+            if flip is not None:
+                e2 = list(eng)
+                e2[flip] = other[flip][eng[flip]]
+                extra = fee[flip] if e2[flip] == "V" else -fee[flip]
+            x = (x * 1103515245 + 12345) % 2 ** 31
+            room = HEAT * (1 - (turn + 1.0) / len(starts)) * (x / 2.0 ** 31) ** 3 - extra
+            m, w2, new = length(s2, e2, i, b0, old, far, len(CASES) * room)
+            if m <= now + room:
+                now, seq, eng, old = m, s2, e2, new
+                way = [p for p in w2 if p[0] in inside]
+    old = length(seq, eng, 0, n, zero, none)[2]
+    now = sum((max(o[0]) + MEAN * sum(o[0]) / n) / w[7] for o, w in zip(old, CASES)) / len(CASES) + sum(f for f, e in zip(fee, eng) if e == "V")
+    return keep if keep[3] < now else (seq, eng, old, now)
+
+
+def schedule2(ops, others):
+    if not BEST:
+        pin = {k: "S" if o["pipe"] is not None else "A" for k, o in enumerate(ops) if len(o["alts"]) > 1 and o["alts"].get("A", [PIN])[0] < PIN}
+        BEST.append(improve(ops, others, *listing(ops, 0, pin)))
     seq, eng = BEST[0][:2]
     for o, e in zip(ops, eng):
         o["eng"] = e
@@ -783,7 +1102,7 @@ def plan(T, topo, core):
     ops = build(T, topo, core, FAC, GA, SC)
     for o in ops:
         o["lat"] += 1.5 if o["remote"] else 0.5 if o["pipe"] is not None else 0.0
-    return ops, schedule(ops, others)
+    return ops, schedule2(ops, others)
 
 
 def rank_program(g, core, T, topo):

from concourse.bass import DstId, RemoteDMATransfer
from concourse.mybir import AluOpType as OP, ActivationFunctionType as AF

H, H0, L, CAP, STEPS = 4096, 3072, 1024, 64, 3
ARR, LB = 8, 640
OLD = LB + 2 * L
WW = OLD + L
ZC, ZB, ZA = 256, 1280, 3328
BIG, TOP, STEEP = 8192.0, 196608.0, 2.0 ** 53
COPY, TWICE, HALF = [False, False, False], [0, 1, 0], True
LAG = [[], []]
EARLYA = 0
FILL = [0, 1, 2]
HALVE = 1
FIRST = EARLYG = True
ONCE = 2.0
MERGE = [False, False]
HALFA = [True, True, True]
SPAN, SWEEPS = 140, 30
UNIT = 2.0 ** -18
SW = 72
F, B, I, U, HF = "float32", "bfloat16", "int32", "uint16", "float16"
SIZE = {F: 4, B: 2, I: 4, U: 2, HF: 2}
POOL = {F: ("pf", 4200), B: ("pb", 8000), I: ("pi", 400), U: ("pu", 760), HF: ("ph", 4000)}
SCRATCH = {
    "kp": ("sbuf", [128, H + 16], B), "dm": ("sbuf", [128, H + 16], B), "w0": ("sbuf", [128, WW], B), "ex": ("sbuf", [128, H], I),
    "sg": ("sbuf", [128, L], F), "xs": ("sbuf", [128, L], F), "cs": ("sbuf", [128, L + 8], F), "mp": ("sbuf", [128, L], B),
    "wn": ("sbuf", [128, 6 * WW + 8], F), "zz": ("sbuf", [128, ZA + 2 * L + 8], F),
    "kk": ("sbuf", [128, L], F), "c1": ("sbuf", [128, L], F), "a1": ("sbuf", [128, L], F),
    "mc": ("sbuf", [128, L], B), "eg": ("sbuf", [128, L], HF),
    "g2": ("sbuf", [128, L], HF), "cb": ("sbuf", [128, L], B), "c0": ("sbuf", [128, L], B),
}
for _d, (_n, _w) in POOL.items():
    SCRATCH[_n] = ("sbuf", [128, _w], _d)
for _n in ("qr0", "qr1", "qa", "qb", "qc", "qd", "qe", "qm"):
    SCRATCH[_n] = ("psum", [128, 512], F)
SEMAPHORES = ["eV", "eA", "eP", "eG"] + ["d%d" % k for k in range(70)] + ["rv0", "rv1", "rd0", "rd1", "rc0", "rc1", "ra0", "ra1"]

CY, FAC, GA, SC, PEC, HOP, BIAS = 0.00083, 1.1, 1.45, 3.5, 0.00042, 0.14, 0.3
CASES = [(1.0, 1.56, 3.8, 0.15, 0.13, 1.0, 0.3, 0.8, 1.0, 1.2, 0.9), (1.05, 1.2, 2.4, 0.2, 0.16, 2.0, 0.8, 0.8, 1.2, 1.4, 1.2, 1.4),
         (1.35, 1.8, 4.8, 0.15, 0.13, 1.5, 0.5, 1.15, 1.0, 1.2, 1.0), (1.2, 1.4, 3.2, 0.2, 0.16, 4.0, 1.5, 0.95, 1.2, 1.4, 1.1)]
PIECES, LAST, TRIES, CLIMB, PIN, HEAT, SEED, MEAN, ANY, FAR, EARLY, LAM = 2, 2, 6, 330000, 1.5, 0.7, 7, 0.5, 2, 4, 0.1, 0.3
SA = [2, 1, 1]
KG = 2
KORD = [[(1,), (0,), (2, 3)], [(0,), (1,), (2, 3)], [(1,), (2, 3), (0,)]]
KS = [32, 32, 32]
EPS, MID = 5e-5, 1600.0
BETA = EPS / 4 * (1 - (1024 * EPS) ** 2 / 16)
JO, LO = 1152.0, 1280.0


def build(T, topo, core, FAC, GA, SC, GI=1.0, AC=1.0, PF=1.0, BW=1.0):
    ops, hist, lay, top, nsem, firstg = [], {}, {}, {}, [0], []

    def V(name, a=0, n=None, p=None, step=1):
        t = T[name]
        n = t.shape[1] - a if n is None else n
        cs = slice(a, a + n) if step == 1 else slice(a, a + n, step)
        pm = sum(1 << j for j in range(128)[slice(None) if p is None else p])
        return (name, a, n, t[(slice(None) if p is None else p), cs], pm, step, (n + step - 1) // step)

    def sub(v, a, n, p=None):
        return V(v[0], v[1] + a * v[5], (n - 1) * v[5] + 1, p, v[5])

    def every(v, a, step, n):
        return V(v[0], v[1] + a, (n - 1) * step + 1, None, step)

    def S(name, dt=F, n=64):
        if name not in lay:
            w = (n + 15) // 16 * 16 if n > 1 else 8
            o = top.get(dt, 0)
            o = (o + 15) // 16 * 16 if n > 1 else o
            top[dt] = o + w
            assert top[dt] <= POOL[dt][1], (dt, top[dt])
            lay[name] = V(POOL[dt][0], o, n)
        return lay[name]

    def C(name):
        return S(name, F, 1)

    def psum(v):
        return SCRATCH.get(v[0], ("dram",))[0] == "psum"

    def meet(v, u):
        if not (v[1] < u[1] + u[2] and u[1] < v[1] + v[2] and v[4] & u[4]):
            return False
        if v[5] > 64 or u[5] > 64:
            a, b = (v, u) if v[5] > 64 else (u, v)
            return any(b[1] <= c < b[1] + b[2] for c in range(a[1], a[1] + a[2], a[5]))
        return not (v[5] == u[5] and (v[1] - u[1]) % v[5])

    def add(alts, rd, wr, lat=0.0, sem=None, after=()):
        k = len(ops)
        deps = {}
        use = [(x, False) for x in rd if x[0] in SCRATCH] + [(x, True) for x in wr if x[0] in SCRATCH]
        pe = "P" in alts
        for v, w in use:
            ps = psum(v)
            for u, w2, k2 in hist.get(v[0], ()):
                if (w or w2) and (meet(v, u) or (ps and (pe or "P" in ops[k2]["alts"]))):
                    deps[k2] = True
                elif ps:
                    deps.setdefault(k2, False)
        for v, w in use:
            hs = hist.setdefault(v[0], [])
            if w and psum(v) and pe:
                hs[:] = [e for e in hs if e[2] == k]
            elif w:
                hs[:] = [e for e in hs if not (v[1] <= e[0][1] and e[0][1] + e[0][2] <= v[1] + v[2] and e[0][4] & ~v[4] == 0
                                               and (v[5] == 1 or (v[5] == e[0][5] and (v[1] - e[0][1]) % v[5] == 0)))]
            hs.append((v, w, k))
        ops.append({"alts": alts, "deps": deps, "lat": lat, "sem": sem, "after": list(after),
                    "nm": ([n for n, x in lay.items() if wr and meet(x, wr[0]) and x[0] == wr[0][0]] + [x[0] for x in wr] + ["-"])[0]})
        return k

    def isv(x):
        return isinstance(x, tuple)

    def ap(x):
        return x[3] if isv(x) else x

    def tv(n, c=1.0):
        return (0.04 + max(64.0, n * c) * CY) * FAC

    def two(*vs):
        return all(SIZE[SCRATCH[v[0]][2]] == 2 for v in vs)

    def tsv(o, x, s1, op0, s2=None, op1=None, off=None):
        xi = x[3] if off is None else x[3].indirect(off[3])
        a = (o[3], xi, ap(s1), ap(s2), op0) + (() if op1 is None else (op1,))
        return (tv(o[6], GA if off else 0.5 if two(o, x) else 1), lambda q: q.tensor_scalar(*a))

    def ts(o, x, s1, op0, s2=None, op1=None):
        add({"V": tsv(o, x, s1, op0, s2, op1)}, [x] + [s for s in (s1, s2) if isv(s)], [o])
        return o

    def tt(o, x, y, op):
        add({"V": (tv(o[6], 1 if psum(x) or psum(y) else 2), lambda q: q.tensor_tensor(o[3], x[3], y[3], op))}, [x, y], [o])
        return o

    def act(o, x, fn, scale=1.0, bias=0.0, acc=None, off=None, alt=None, extra=0.0):
        xi = x[3] if off is None else x[3].indirect(off[3])
        kw = {} if acc is None else {"accum_out": acc[3]}
        if not (fn == AF.Copy or (not isv(bias) and bias == 0.0)):
            kw["bias"] = ap(bias)
        if isv(scale) or scale != 1.0:
            kw["scale"] = ap(scale)
        alts = {"A": (tv(o[6], GA if off else 1) + 0.03 + extra, lambda q: q.activation(o[3], xi, fn, **kw))}
        if alt:
            alts["V"] = alt
        add(alts, [x] + [s for s in (scale, bias, off) if isv(s)], [o] + ([acc] if acc else []))
        return o

    def aff(o, x, mul, plus, off=None):
        return act(o, x, AF.Identity, mul, plus, off=off, alt=tsv(o, x, mul, OP.mult, plus, OP.add, off))

    def to16(o, x, mul=1.0, plus=0.0):
        return act(o, x, AF.Relu, mul, plus, alt=tsv(o, x, mul, OP.mult, plus, OP.add))

    def over(o, x, v):
        return act(o, x, AF.Sigmoid, STEEP, 100.0 - v * STEEP, alt=tsv(o, x, v, OP.is_ge))

    def cp(o, x, both=False):
        v = (tv(o[6], 0.5 if two(o, x) else 1), lambda q: q.tensor_copy(o[3], x[3]))
        if both:
            return act(o, x, AF.Copy, alt=v)
        add({"V": v}, [x], [o])
        return o

    def gat(o, win, off):
        return act(o, win, AF.Copy, off=off, alt=(tv(o[6], GA), lambda q: q.tensor_copy(o[3], win[3].indirect(off[3]))))

    def gtt(o, win, off, y, op):
        add({"V": (tv(o[6], GA), lambda q: q.tensor_tensor(o[3], win[3].indirect(off[3]), y[3], op))}, [win, off, y], [o])
        return o

    def scat(win, off, x, silu=None):
        if silu:
            add({"A": (tv(x[6], SC), lambda q: q.activation(win[3].indirect(off[3]), x[3], AF.Sigmoid))}, [off, x], [win])
        else:
            add({"V": (tv(x[6], SC), lambda q: q.tensor_copy(win[3].indirect(off[3]), x[3]))}, [off, x], [win])

    def iog(o, pat, base, cm):
        kw = {} if SCRATCH[o[0]][2] == I else {"allow_small_or_imprecise_dtypes": True}
        return (0.13 + 2 * o[6] * CY * FAC, lambda q: q.iota(o[3], pat, base, cm, **kw))

    def iota(o, pat, base=0, cm=0):
        add({"G": iog(o, pat, base, cm)}, [], [o])
        return o

    def mset(o, c):
        alts = {"V": (tv(o[6], 0.5 if two(o) else 1), lambda q: q.memset(o[3], c))}
        if SCRATCH[o[0]][2] != HF and o[5] == 1 and c == int(c):
            alts["G"] = iog(o, [[0, o[6]]], int(c), 0)
        add(alts, [], [o])
        return o

    def scan(o, d0, d1, op1=OP.add):
        add({"V": (tv(o[6], 0.5 if two(o, d0, d1) else 1), lambda q: q.tensor_tensor_scan(o[3], d0[3], d1[3], 0.0, OP.mult, op1))}, [d0, d1], [o])
        return o

    def pick(o, x, pat, base, op=OP.is_equal):
        add({"G": (0.17 + 2 * o[6] * CY * FAC, lambda q: q.affine_select(o[3], x[3], pat, op, 0.0, base, 1))}, [x], [o])
        return o

    def mms(lst):
        def emit(q):
            r = None
            for o, l, x, s0, s1 in lst:
                r = q.matmul(o[3], l[3], x[3], s0, s1)
            return r
        add({"P": (0.05 + sum(max(64, m[0][6]) * PEC * PF * FAC * (SIZE[SCRATCH[m[1][0]][2]] // 2) ** 2 + 0.01 for m in lst), emit)}, [v for m in lst for v in m[1:3]], [m[0] for m in lst])

    def acc(o, terms, first=True, last=True):
        return [(o, l, x, first and j == 0, last and j == len(terms) - 1) for j, (l, x) in enumerate(terms)]

    def wrap(o, bm, x, n, first=True, last=True):
        mms([(o, sub(bm, 15 - i, 128), every(x, i, 16, n), first and i == 0, last and i == 15) for i in range(16)])
        return o

    def dma(eng, o, x, kb, acc=False):
        s = "d%d" % nsem[0]
        nsem[0] += 1
        kb *= (AC if acc else 1.0) * BW
        kw = {"accum_op": OP.add, "max_dma_last_dim": 8192} if acc else {}
        add({e: (GI + (0.0 if firstg else ONCE * GI) if e == "G" else 0.1, lambda q: q.dma_start(ap(o), ap(x), **kw)) for e in ("G" if eng == "G" else "SA")},
            [v for v in (x, o if acc else None) if isv(v)], [o] if isv(o) else [], lat=1.6 + kb / 600.0, sem=(s, 16), after=firstg if eng == "G" else ())
        if eng == "G" and not firstg:
            firstg.append(len(ops) - 1)
        ops[-1]["pipe"] = kb / 600.0

    def send(items, rsem, land):
        s = "d%d" % nsem[0]
        nsem[0] += 1
        trs, tot = [], 0
        for j, (src, dst, to) in enumerate(items):
            en = topo.engines(core, to)
            w = len(en) // len(items) // (HALVE if rsem == "rc0" else 1)
            m = sum(1 << e for e in en[j * w:(j + 1) * w])
            rid, pid, _ = topo.addr(to)
            trs.append(RemoteDMATransfer(dst_ids=[DstId(rid=rid, pnc=pid)], dma_engine_mask=m, remote_sem=T.sem[rsem], src=src[3], dst=dst[3]))
            tot += w
        k = add({"G": (GI, lambda q: q.remote_dma_fused(trs, local_sem=T.sem[s]))}, [i[0] for i in items], [], lat=1.5 + (2.0 * AC if rsem == "rc0" else 0.0), sem=(s, tot))
        ops[k]["remote"] = True
        add({}, [], land, lat=0.3, sem=(rsem, tot), after=[k])

    rank, n = T.rank_of(core), len(T.cores)
    to1, to2 = T.cores[(rank + 1) % n], T.cores[(rank + 2) % n]
    kp, dm, sg, ex, zz, mc = [V(x) for x in ("kp", "dm", "sg", "ex", "zz", "mc")]
    kk, c1, a1, eg, g2, cb, c0, w0, xs = [V(x) for x in ("kk", "c1", "a1", "eg", "g2", "cb", "c0", "w0", "xs")]
    nl, ab, mp, cs, kq_ = mc, sub(w0, OLD, L), V("mp"), V("cs"), V("kp", 0, H0 + 16)
    wc, wa = [V("wn", 2 * t * WW, WW + 8) for t in range(3)], [V("wn", (2 * t + 1) * WW, WW + 8) for t in range(3)]
    qr = [V("qr0"), V("qr1")]
    HV = [(0, 512), (512, 512)]
    PV = [(j * L // PIECES, L // PIECES) for j in range(PIECES)]
    mul, plus, minus = OP.mult, OP.add, OP.subtract

    mset(sub(ex, 0, L), 0)
    cp(sub(ex, L, L), sub(ex, 0, L), True)
    mset(sub(ex, 2 * L, L), 0)
    p4 = S("p4", I)
    dma("S", ab, T.amp[:], 256)
    dma("S", cb, T.cro[:], 256)
    for j in range(4):
        dma("S", sub(p4, 16 * j, 16), T.place[j % 2::2, 512 * (j // 2):512 * (j // 2) + 512], 30)
    for a in (0, 2 * L, L):
        dma("S", V("ex", a, L, slice(0, 128, 16)), T.lf[:, a:a + L], 100)
        dma("S", V("ex", a, L, slice(8, 128, 16)), T.rt[:, a:a + L], 100)
    dma("S", sub(kq_, 0, H0), T.kap[:, 0:H0], 750)
    ops[-1]["after"] += [len(ops) - 3, len(ops) - 2]
    for j, o in enumerate(ops):
        o["first"] = 1000.0 - j
    k = len(ops) - 1
    for j in range(2):
        dma("G" if j and EARLYG else "S", sub(w0, LB + j * L, L), T.amp[:], 256)
        ops[-1]["after"].append(k - (6 if j and EARLYG else 0))
    dma("S", sub(dm, 0, H), T.dam[:], 1000)
    ops[-1]["after"].append(k)
    mset(sub(kq_, H0, 1), 0.5)
    mset(sub(cs, L, 1), -8.0)
    mset(sub(dm, H, 1), 40.0)
    mset(sub(kp, H, 1), 0.0)
    mset(sub(w0, 0, 1), 0.0)

    pi = iota(S("pi", I, 1), [[0, 1]], 0, 1)
    pc = iota(C("pc"), [[0, 1]], 0, 1)
    io = iota(S("io", F, 272), [[1, 272]])
    qg = iota(S("qg", F, 128), [[16, 8], [0, 16]])
    l16 = iota(S("l16"), [[16, 64]])
    iota(sub(ex, H0, L), [[1, L]], H0)
    mset(V("wn", 0, 6 * WW + 1, None, 2 * WW), -8.0)
    mset(V("wn", WW, 4 * WW + 1, None, 2 * WW), 0.0)
    all1 = mset(S("all1", B, 512), 1.0)
    rs = act(S("rs", B, 3 * SW), sub(io, 0, 3 * SW), AF.Sigmoid, 1.0, 40.0, extra=1.3)
    mset(every(rs, SW, SW, 2), 0.0)
    one64, one1 = sub(all1, 0, 64), sub(all1, 0, 1)
    nil = S("nil", B, 4 * SW + 128)
    mset(sub(nil, 0, 4 * SW), 0.0)
    seg = sub(nil, 0, 3 * SW)
    dis, cdc = sub(nil, 3 * SW, 65), sub(nil, 4 * SW, 128)
    mset(sub(cdc, 0, 64), -2048.0 - LO - 32 * JO)
    mset(sub(cdc, 64, 64), LB - 1024.0)
    qb_ = S("qbm", B, 144)
    mset(sub(qb_, 0, 3), 0.0)
    zeros = mset(S("zeros", HF, 384), 0.0)
    kd0, kq0, kt0 = [sub(zeros, 128 * j, 128) for j in range(3)]
    ici = ts(S("ici", I, 1), pi, 15, OP.bitwise_and)
    ic = cp(C("ic"), ici)
    g16 = aff(C("g16"), ic, -1.0, pc)
    lid = aff(S("lid"), l16, 1.0, ic)
    nlid = aff(S("nlid"), lid, -1.0, 0.0)
    lidh = cp(S("lidh", HF), lid, True)
    jh = aff(S("jh", F, 4), sub(lid, 0, 4), 1.0, 0.5)
    i128, i64 = sub(io, 0, 128), sub(io, 0, 64)
    b1 = ts(S("b1", B, 272), io, -31.0, plus, g16, OP.is_equal)

    def sel(name, w):
        return aff(S(name, B, 144), sub(b1, 16, 144), w, 0.0)
    e16 = ts(S("e16", F, 16), sub(io, 0, 16), ic, OP.is_equal)
    bim, bx0, bx8 = [sel("bs%d" % j, w) for j, w in enumerate((ic, sub(e16, 0, 1), sub(e16, 8, 1)))]
    bw = sub(b1, 16, 144)
    ones = ts(S("ones", B, 128), qg, g16, OP.is_equal)
    tri = pick(S("tri", B, 128), aff(S("tri0", B, 128), ones, -1.0, 0.0), [[-1, 128]], 0, OP.is_ge)
    qn = S("qn", F, 128)
    iota(sub(qn, 0, 16), [[0, 16]], 112)
    iota(sub(qn, 16, 112), [[16, 7], [0, 16]])
    osh = ts(S("osh", F, 128), qn, g16, OP.is_equal, 0.5, mul)
    onh = aff(S("onh", F, 128), ones, 0.5, 0.0)
    row0 = ts(S("row0", B, 128), ones, sub(e16, 0, 1), mul, -1.0, mul)
    i12 = pick(S("i12", B, 152), sub(all1, 0, 152), [[-1, 152]], 12)
    ip = sub(i12, 12, 128)
    im, kp1, km1, bp, bm, hp = [aff(S("wt%d" % j, B, 128), ip, w, 0.0) for j, w in enumerate((-1.0, 1024.0, -1024.0, BIG, -BIG, 0.5))]


    def late(name, w, dt=B):
        iota(S(name, dt, 128), [[0, 128]], w)
        ops[-1]["after"] += soon
        return pick(S(name), S(name), [[-1, 128]], 0)
    mmq = pick(S("mmq", B, 512), all1, [[-1, 4], [-16, 8], [-4, 16]], 0)
    soon = firstg + [len(ops) - 1]
    f8i, m2, k4, whole = late("f8i", 8, F), late("m2", -2), late("k4", -4096), late("whole", int(8 / UNIT))
    kp2, km2, km3 = late("kp2", 2048), late("km2", -2048), late("km3", -3072)
    e4 = ts(S("e4", F, 4), sub(io, 0, 4), cp(C("q4"), ts(S("q4i", I, 1), ici, 2, OP.arith_shift_right)), OP.is_equal)
    mu = [aff(S("mu%d" % u, B, 152), i12, sub(e4, u, 1), 0.0) for u in range(4)]
    muk = [aff(S("muk%d" % u, B, 152), mu[u], 1024.0, 0.0) for u in range(4)]
    mu32 = aff(S("mu32", B, 152), mu[2], 32.0, 0.0)
    p32, m32 = [aff(S("w32%d" % j, B, 128), ip, w, 0.0) for j, w in enumerate((32.0, -32.0))]
    kilo = mset(S("kilo", B), 1024.0)
    lidb, lidc = aff(S("lidb"), lid, BIG, 0.0), aff(S("lidc"), lid, 1.0, -511.5)
    step = S("step", F, 128)
    iota(sub(step, 0, 16), [[1, 16]], 112)
    iota(sub(step, 16, 112), [[1, 112]])
    for o in ops[-2:]:
        o["after"] += soon
    ts(step, step, pc, OP.is_equal)
    ntop, cfar = mset(S("top", B), -TOP), mset(S("cfar", B), LB + 2048.0)
    e1 = sub(e16, 1, 1)
    inb, inx, outb = [aff(C("cb%d" % j), e1, w * MID, b - w * MID) for j, (w, b) in enumerate(((BETA, 0.5), (EPS, 0.0), (-1.0, -0.5 / BETA)))]
    pick(sub(qb_, 3, 128), sub(all1, 0, 128), [[-16, 8], [-1, 4], [1000, 4]], 0)
    rt_ = S("rt", I, 128)
    c84 = mset(S("c84", B, 64), -1984.0)
    idq = ts(S("idq", HF, 256), sub(io, 0, 256), aff(C("id0"), sub(e4, 1, 1), 4.0, 0.0), mul, ts(C("id1"), ic, -1028.0, plus, sub(e4, 1, 1), mul), plus)
    xf = S("xf", HF, 192)
    own = aff(sub(xf, 128, 64), lid, 1.0, LB - 1024.0)
    cj = [mset(S("cj%d" % t, B), 1792.0 + BIG + 128 * (1 - t)) for t in range(2)]
    kc = S("kc", B, 3)
    for j, w in enumerate((-2048.0, -1536.0, 448.0)):
        mset(sub(kc, j, 1), w)

    pt = S("pt")
    pf = cp(S("pf0"), p4)
    add({"V": (tv(64), lambda q: q.transpose(pt[3], pf[3]))}, [pf], [pt])
    so = S("so", U, 192)
    hoff, s1, s2 = [sub(so, 64 * j, 64) for j in range(3)]
    to16(hoff, pt)
    hk = ts(S("hkk", U), pt, float(H0), OP.min)
    rf = S("rf", HF, 192)
    rfo, fr, rest = [sub(rf, 64 * j, 64) for j in range(3)]
    ts(rest, pt, float(H0), OP.is_ge, -1.0, mul)
    for j, (a, w) in enumerate(HV):
        ts(sub(nl, a, w), sub(ab, a, w), 0.0, OP.is_equal)
        mms(acc(qr[j], [(km1, sub(nl, a, w)), (ip, sub(cb, a, w))]))
        if FIRST:
            over(sub(mp, a, w), qr[j], 0.0)
        aff(sub(c0, a, w), qr[j], UNIT, 0.0)
        if not FIRST:
            over(sub(mp, a, w), sub(c0, a, w), 0.0)
    n1 = aff(C("n1"), e1, ARR - LB - 1024.0 - JO - 32, JO + 32)
    svc = ts(S("svc", HF, 128), i128, e1, mul, aff(C("n3"), sub(e16, 3, 1), LO - 2048.0 - JO - 32, n1), plus)
    mc_, nfc, nfa = [V("qm", j, 1) for j in (0, 8, 9)]
    n0a, n0b = V("qc", 384, 1), V("qc", 385, 1)
    de, do, sf = [sub(seg, SW * j, SW) for j in range(3)]
    scs = S("scs", B, 3 * SW)
    ce, co, cf = [sub(scs, SW * j, SW) for j in range(3)]
    pre = lid
    mark, held = {}, []

    def leave(t, j, win, sd):
        sh = S("sh%d%d" % (t, j))
        if j:
            dma("S", sub(sh, 0, 64, slice(16, 128)), sub(sd, 64, 64, slice(0, 112)), 32)
            dma("S", sub(sh, 0, 64, slice(0, 16)), sub(sd, 64, 64, slice(112, 128)), 32)
        else:
            mms([(V("qd", 416, 64), step, sub(sd, 64, 64), True, True)])
            cp(sh, V("qd", 416, 64), True)
        held.append(([(sub(sd, 0, 64), sub(win, ARR, 64), to1), (sh, sub(win, ARR + 64, 64), to2)], sub(win, ARR, 128)))
        if j or not MERGE[t]:
            send([x for h in held for x in h[0]], "%s%d" % (("rd", "ra")[j], t), [h[1] for h in held])
            held.clear()

    for t in range(STEPS):
        cw, aw, cn, an = wc[t], wa[t], wc[(t + 1) % 3], wa[(t + 1) % 3]
        c, A = (c0, ab) if t == 0 else (sub(cs, 0, L), sub(aw, OLD, L))
        ws, ks = ZC - 128 * t, KS[t]
        hl, u = V("qa", 0, 64), V("qb", 0, 64)
        wrap(hl, bw, nl, 64)
        hs = aff(S("hs", HF), hl, 0.5 if t else -0.5, 0.0 if t else 8.0)
        mms(acc(u, [(kp1, rest)] + ([(km1, fr)] if t else []), last=False))
        wrap(u, bw, mp, 64, False, False)
        mms(acc(u, [(im, hs)], first=False))
        if t == 0:
            ts(sub(sf, 0, 64), hl, 16.0, OP.is_equal)
            cp(fr, sub(sf, 0, 64), True)
            scan(cf, sub(rs, 2 * SW, SW), sf)
            pf_ = V("qd", 0, 64)
            mms(acc(pf_, [(tri, sub(sf, 0, 64)), (ones, sub(cf, 0, 64)), (km1, sub(sf, 0, 64)), (km1, sub(sf, 0, 64))]))
            mms(acc(nfc, [(ones, sub(cf, 64, 1)), (ip, sub(kc, 0, 1))]) + (acc(nfa, [(ones, sub(cf, ks - 1, 1)), (ip, sub(kc, 0, 1))]) if ks else []))
            cp(rfo, pf_, True)
        for a, w in PV:
            aff(sub(eg, a, w), ex, 1.0, -2048.0, sub(hoff, a // 16, w // 16))
        wrap(V("qc", 0, 64), bx0, eg, 64)
        wrap(V("qc", 64, 64), bx8, eg, 64)
        jf = aff(S("jf", HF, 128), V("qc", 0, 128), 1.0 / 32, JO + 64 - 15.5 / 32)
        cp(sub(xf, 0, 128), V("qc", 0, 128), True)
        jl, jr, xl, xr, off = sub(jf, 0, 64), sub(jf, 64, 64), sub(xf, 0, 64), sub(xf, 64, 64), sub(cdc, 0, 64)
        pj, pl = V("qc", 128, 128), V("qc", 256, 128)
        mms(acc(every(pj, 0, 2, 64), [(ip, jr), (im, jl)]) + acc(every(pj, 1, 2, 64), [(ip, jl)])
            + acc(every(pl, 0, 2, 64), [(ip, xr), (im, xl), (m32, jr), (p32, jl)]) + acc(every(pl, 1, 2, 64), [(ip, xl), (m32, jl), (im, off)]))
        unit = UNIT / 2 ** (t + 1)
        for j in range(2):
            aff(sub(cw, LB + j * L, L), mp, (6.0 - unit, -6.0)[j], (-6.0, unit)[j])
        for a, w in (PV if HALF else [(0, L)]):
            gtt(sub(cw, OLD + a, w), kq_, sub(hk, a // 16, w // 16), sub(c, a, w), mul)
        if t == 0:
            aw = w0
        if t == STEPS - 1:
            dma("S", sub(kp, H0, L), T.kap[:, H0:H], 256)
        for j in range(2):
            if FILL[t] == 2:
                aff(sub(aw, LB + j * L, L), mp, (6.0, -6.0)[j], (-6.0, 0.0)[j])
            elif FILL[t]:
                dma("S", sub(aw, LB + j * L, L), sub(cw, LB + j * L, L), 512)
            dma("G", sub(cw, LB + j * L, L), sub(cw, OLD, L), 700, True)

        def sections():
            for j in range(2 if t else 0):
                dma("G" if FILL[t] else "S", sub(aw, LB + j * L, L), A, 700 if FILL[t] else 512, FILL[t] > 0)
            for j in range(0 if FILL[t] else SA[t]):
                w = 2 * L // SA[t]
                dma("G", sub(aw, LB + j * w, w), sub(cw, LB + j * w, w), (1400 if t else 1000) // SA[t], True)
        qe = V("qe", 0, 128)
        dj, jx, qp, qj, qz = every(qe, 0, 2, 64), every(qe, 1, 2, 64), V("qe", 128, 64), V("qe", 192, 64), V("qe", 256, 64)
        mms(acc(qp, [(im, rfo), (km3, fr)]) + acc(qz, [(kp2, fr)]) if t else acc(qp, [(im, rfo), (km1, fr), (km1, fr), (km1, fr)]))
        p0 = tt(S("p0"), qp, nlid, OP.min)
        mms(acc(dj, [(ip, jl), (im, jr)]))
        kq1 = S("kq1", HF, 128)
        lw, capv, par = every(kd0, 1, 2, 64), every(kq0, 1, 2, 64), every(kq1, 0, 2, 64)
        if t == 0:
            key = tt(S("key", HF), ts(S("cap0", HF), dj, 0.0, OP.not_equal), fr, OP.is_gt)
        else:
            ts(capv, dj, 0.0, OP.is_equal, 2047.0, plus)
            tt(jx, qz, jr, OP.max)
            keyl = tt(S("keyl", HF), qz, capv, OP.max) if TWICE[t] else None
            cnt = sub(S("cnt", F, 16), 8 * (t - 1), 8)
            mms(acc(mc_, [(kp1, one1), (onh, sub(cnt, 0, 1)), (osh, sub(cnt, 4, 1))]))
            isa = ts(S("isa", HF), rfo, 2048.0, plus, mc_, OP.is_lt)
        au = act(S("au"), u, AF.Abs)
        act(lw, u, AF.Sigmoid, 200.0, 50.0, alt=tsv(lw, u, 0.0, OP.is_ge))
        tt(sub(dis, 0, 64), au, hs, OP.is_lt)
        mark["dis"] = len(ops) - 1
        if t:
            amps(*later, [mark[x] for x in LAG[t - 1]])
        sections()
        scd = scan(S("scd", B, 65), sub(rs, 0, 65), dis)
        rd, ndc, nda = V("qa", 0, 64), V("qa", 64, 1), V("qa", 72, 1)
        mms(acc(V("qa", 0, 65), [(tri, dis)] + ([(km2, dis)] if t else [(km1, dis)] * 2) + [(ones, scd)], last=False) + acc(ndc, [(ip, sub(kc, 0, 1))], first=False)
            + (acc(nda, [(ones, sub(scd, ks - 1, 1)), (ip, sub(kc, 0, 1))]) if ks else []))

        def cmp(o, x, sign, y, op):
            return ts(o, x, y, op) if t == 0 else ts(o, x, mc_, sign, y, op)
        if t:
            scan(kq1, kd0, qe)
        cmp(par, rd, plus, nfc, OP.is_lt)
        jo, lo = [every(scan(S(nm, HF, 128), kd0, x), 1, 2, 64) for nm, x in (("jo", pj), ("lo", pl))]
        if t:
            key = every(scan(S("kq2", HF, 128), kq0, kq1, OP.max), 1, 2, 64)
            mms([(V("qc", 384, 2), ip, sub(kc, 1, 2), True, False), (n0a, onh, sub(cnt, 0, 1), False, False), (n0b, onh, sub(cnt, 0, 1), False, True)])
            aj0 = ts(S("aj0", HF), rfo, n0a, OP.is_ge, n0b, mul)
            mms(acc(qj, [(ip, cj[t - 1]), (ip, rfo), (im, aj0), (bm, isa)]))
            pre = tt(S("pre"), qj, tw, OP.min)
        end = t == STEPS - 1
        fb = V("qd", 0, 128)
        fq = [sub(fb, 64 * j, 64) for j in range(2)]
        mms([(fb, ip, sub(xf, 64, 128), True, False)]
            + [(fq[j], l, x, False, False) for j, l, x in ((0, ip, xl), (0, im, off), (0, bm, fr), (1, bm, fr), (1, km1, rest), (1, km1, lw), (0, m32, jo))]
            + [(fq[0], im, lo, False, True)])
        fc = cp(S("fc", HF, 128), fb, True)
        qw = V("qr1", 0, 256)
        code = [(mu, key), (muk, lw), (mu, jo), (mu, lo)]

        def ahead(f, m, x, last=False):
            return [(every(qw, u, 4, 64), sub(m[u], 12 - 4 * (f - u), 128), x, False, last and u == 3) for u in range(4)]
        def rows(j, x):
            mms([(every(qr[j], r, 4, 128), sub(mmq, 128 * r, 128), sub(x, 128 * j, 128), True, True) for r in range(4)])
        split = TWICE[t]
        if split:
            code[0] = (mu, keyl)
        mms([(qw, ip, idq, True, False)] + (ahead(0, muk, one64) if t == 0 else [] if split else ahead(1, muk, rest)))
        kord = KORD[1 if split else 2 if t else 0]
        for fs in kord:
            mms([m for f in fs for m in ahead(f, code[f][0], code[f][1], fs is kord[-1] and f == fs[-1])])
        wsb = cp(S("wsb", HF, 256), qw, True)
        for j in range(2):
            rows(j, wsb)
            if j == 0:
                aff(sub(xs, 0, 512), qr[j], EPS, inx)
            if j or (t and not split):
                aff(sub(xs if split else zz, (0 if split else ZC) + 512 * j, 512), qr[j], BETA, inb)
        posf = tt(S("posf"), rd, p0, OP.min)
        pos = to16(S("pos", U), posf, 1.0, 2048.0)
        scat(sub(zz, ZA, 2 * L + 8), sub(pos, 0, ks), sub(xs, 0, 16 * ks), True)
        scat(sub(zz, ZB, 2 * L), sub(pos, ks, 64 - ks), sub(xs, 512, 512) if split else sub(zz, ZC + 16 * ks, L - 16 * ks))
        if split:
            qw = V("qd", 256, 256)
            mms([(qw, ip, idq, True, False)] + ahead(1, muk, rest) + ahead(1, muk, lw))
            mms(ahead(0, mu, key, True))
            wsb = cp(S("wsb2", HF, 256), qw, True)
            for j in range(2):
                rows(j, wsb)
                aff(sub(zz, ZC + 512 * j, 512), qr[j], BETA, inb)
        qv = aff(S("qv", HF), posf, -1.0, 0.0) if t == 0 else ts(S("qv", HF), posf, mc_, plus, -1.0, mul)
        js = [cmp(S("j1", HF), rd, plus, nfa, OP.is_lt), cmp(S("j2", HF), rfo, minus, nda, OP.is_lt)] if ks else []
        nba = cmp(S("nba", HF), rfo, minus, ndc, OP.is_ge)
        pp = V("qb", 0, 64)
        mms(acc(pp, [(ip, qv), (bp, par), (bm, nba)] + ([(kp2, x) for x in js] + [(bm, isa)] if t else [(kp1, x) for x in js + js])))
        if t:
            idx = to16(S("idx", U), tt(S("idf"), pp, pre, OP.max), 1.0, float(ZC - ws))
        else:
            idx = ts(S("idx", U), pp, L - 1.0, OP.max)
        for a, w in PV:
            aff(sub(g2, a, w), sub(zz, ws, ZA + 2 * L + 8 - ws), 1.0 / BETA, outb, sub(idx, a // 16, w // 16))
        still, o2 = V("qe", 320, 64), V("qe", 384, 64)
        mms(([] if end and EARLYA else acc(still, [(k4, rest), (k4, fr), (m2, kilo)] + ([(bp, isa)] if t else []))) + acc(o2, [(bp, one64), (bm, fr), (bm, nba)])
            + acc(qp, [(ip, own), (kp1, one64), (kp1, lw), (bp, par), (bm, one64)]))
        mine = cp(S("mine"), qp, True)
        q4 = V("qr0", 0, 256)
        mms(acc(q4, [(sub(qb_, 3 - r, 128), every(g2, r, 4, 256)) for r in range(4)]))
        qsb = cp(S("qsb", HF, 256), q4, True)

        def back(m, f):
            return [(sub(m, 12 - 4 * (u - f), 128), every(qsb, u, 4, 64)) for u in range(4)]
        pk, pr, r1 = V("qa", 0, 64), V("qb", 0, 64), V("qb", 64, 64)
        end = t == STEPS - 1
        mq = [V("qc", 0, 64), V("qc", 64, 64)]
        mms([(V("qc", 0, 128), ip, cdc, True, False)] + [(mq[j], bm, nba, False, False) for j in (0, 1, 1)])
        mms(acc(pk, [(ip, key), (bp, nba), (bm, par)] if t == 0 else [(im, key), (bp, fr), (bp, nba), (bp, isa)], last=False))
        mms(acc(pr, [(im, lidh), (kp1, one64), (im, ntop)], last=False))
        far = V("qd", 0, 64)
        mms(acc(far, [(bm, par), (m2, ntop), (ip, cfar)], last=False))
        mms(acc(mq[0], back(mu32, 2) + back(mu[3], 3), False, False) + acc(mq[1], back(mu[1], 1), False))
        mms(acc(pr, back(mu[1], 1), first=False))
        mms(acc(pk, back(mu[0], 0), first=False))
        tt(rt_, V("qc", 0, 128), fc, OP.max)
        side = tt(S("side", B), pr, lidc, plus)
        pd = tt(S("pd", I), pr, side, minus)
        mms(acc(far, back(mu[1], 1) + [(m2, side)], first=False))
        f8 = V("qm", 64, 64)
        ts(f8, pk, 1024.5, OP.is_lt, BIG, mul) if t == 0 else ts(f8, pk, BIG, OP.is_equal, BIG, mul)
        eb = tt(S("eb"), f8, pd, mul)
        upn = tt(V("qm", 128, 64), eb, o2, OP.min)
        h = sub(rt_, 0, 64)
        hsg = S("hsg", U)
        if end:
            to16(s1, sub(rt_, 64, 64), 1.0, 2048.0)
            s1c = to16(S("s1c", U), tt(S("s1f"), upn, sub(rt_, 64, 64), plus), 1.0, 2048.0)
            ts(hoff, tt(S("hk"), h, upn, minus), 2048.0, OP.min, 2048.0, plus)
        else:
            to16(sub(so, 0, 128), rt_, 1.0, 2048.0)
            ts(hk, h, 2048.0, plus, float(H0), OP.min)
        to16(s2, tt(S("s2f"), eb, tt(V("qm", 320, 64), far, mine, OP.max), OP.min))
        if not (end and EARLYA):
            to16(hsg, tt(S("hsf"), still, h, OP.max), 1.0, 2048.0)
            mate = to16(S("mate", U), tt(S("matef"), eb, lidb, plus), 1.0 / BIG)
        c, A = sub(cs, 0, L), sub(an, OLD, L)
        cwin, awin = sub(cw, 0, WW), sub(aw, 0, WW)
        for a, w in PV:
            gat(sub(c1, a, w), cwin, sub(s1c if end else s1, a // 16, w // 16))

        def amps(t, A, awin, an, mate, behind):
            cut = PV if HALFA[t] else [(0, L)]
            for a, w in cut:
                act(sub(sg, a, w), dm, AF.Sigmoid, off=sub(hsg, a // 16, w // 16))
                ops[-1]["after"] += behind
                gtt(sub(a1, a, w), awin, sub(s1, a // 16, w // 16), sub(sg, a, w), mul)
                if COPY[t]:
                    dma("S", sub(kk, a, w), sub(a1, a, w), w // 2)
                else:
                    act(sub(kk, a, w), sub(a1, a, w), AF.Relu, alt=tsv(sub(kk, a, w), sub(a1, a, w), 0.0, OP.max))
            for a, w in cut:
                gtt(sub(A, a, w), a1, sub(mate, a // 16, w // 16), sub(kk, a, w), OP.max)
            if t < STEPS - 1:
                leave(t, 1, an, gat(S("sa%d" % t, F, 128), sub(an, OLD, L + 8), S("lno")))
        if not end:
            later = (t, A, awin, an, mate)
        elif not EARLYA:
            amps(t, A, awin, an, mate, [])
        for a, w in PV:
            o = (a // 16, w // 16)
            gtt(sub(c, a, w), cwin, sub(s2, *o), sub(c1, a, w), OP.max)
            if not end:
                over(sub(nl, a, w), sub(c, a, w), -4 * UNIT)
                over(sub(mp, a, w), sub(c, a, w), 0.0)
                mark["mp"] = len(ops) - 1
                continue
            if EARLYA:
                act(sub(a1, a, w), awin, AF.Relu, off=sub(s1, *o), alt=tsv(sub(a1, a, w), awin, 0.0, OP.max, off=sub(s1, *o)))
                gtt(sub(A, a, w), awin, sub(s2, *o), sub(a1, a, w), OP.max)
            y = sub(sg, a, w)
            if a // w < KG:
                kq = V(("qd", "qc")[a // w % 2], 0, w)
                mms(acc(kq, [(ip, gat(sub(c0, a, w), kp, sub(hoff, *o)))]))
                tt(y, sub(A, a, w), kq, mul)
            else:
                gtt(y, kp, sub(hoff, *o), sub(A, a, w), mul)
            lv = V("qr%d" % (a // w % 2), 0, w)
            on = over(sub(mp, a, w), sub(c, a, w), -4 * UNIT)
            mms(acc(lv, [(whole, on)]))
            dma("S", T.ya[:, a:a + w], y, w // 2)
            dma("S", T.yc[:, a:a + w], tt(sub(xs, a, w), sub(c, a, w), lv, mul), w // 2)
        if end:
            break
        bound, stays = BIG + 200.0 if t else BIG / 2, S("stays", HF)
        act(stays, pk, AF.Sigmoid, -1.0, bound, alt=tsv(stays, pk, bound, OP.is_lt))
        tw = tt(S("tw"), tt(V("qm", 192, 64), stays, pd, mul), lid, plus)
        z = tt(S("z"), upn, ts(S("y", I), h, 3073, OP.bitwise_and), plus)
        ts(sub(de, 0, 64), z, 1024.0, OP.is_equal)
        ts(sub(do, 0, 64), z, 1025.0, OP.is_equal)
        act(sub(sf, 0, 64), upn, AF.Sigmoid, -1.0, -100.0, alt=tsv(sub(sf, 0, 64), upn, 0.0, OP.is_lt))
        scan(scs, rs, seg)
        d64 = [sub(x, 0, 64) for x in (de, do, sf, ce, co, cf)]
        rank_ = [(tri, d64[0]), (tri, d64[1]), (ones, d64[3]), (ones, d64[4])]
        xe, xo_ = V("qb", 0, 64), V("qb", 64, 64)
        mms([(xe, bm, d64[0], True, False), (xo_, bm, d64[1], False, False)] + [(x, tri, y, False, False) for x in (xe, xo_) for y in d64[:2]])
        mms([(x, ones, y, False, x is xo_ and y is d64[4]) for x in (xe, xo_) for y in d64[3:5]])
        sc_, cnt = S("sc%d" % t, F, 16), S("cnt", F, 16)
        le, lo_ = [act(S("le%d" % j, HF), x, AF.Sign, -1.0, CAP - 0.5 - BIG, acc=sub(sc_, 4 * j, 1)) for j, x in enumerate((xe, xo_))]
        send([(sub(sc_, 0, 1), sub(cnt, 8 * t, 1), to1), (sub(sc_, 4, 1), sub(cnt, 8 * t + 4, 1), to2)], "rc%d" % t, [sub(cnt, 8 * t, 8)])
        rk = V("qa", 0, 65)
        mms(acc(rk, [(tri, sub(de, 0, 65)), (tri, sub(do, 0, 65)), (ones, sub(ce, 0, 65)), (ones, sub(co, 0, 65))]))
        r64 = act(S("r64", HF, 65), rk, AF.Relu, -1.0, float(CAP))
        be, cq = V("qd", 0, 2 * SW), V("qr1", 0, 2 * SW)
        mms(acc(be, [(ones, sub(scs, 0, 2 * SW))]))
        mms(acc(sub(cq, 0, SW), [(tri, de), (ones, ce), (bm, de)]) + acc(sub(cq, SW, SW), [(tri, do), (ones, co), (bm, do)]))
        qf = [V("qr0", 64 * j, 64) for j in range(3)]
        mms(acc(qf[0], [(tri, d64[2]), (ones, d64[5]), (ip, c84), (km2, d64[2]), (im, sub(r64, 0, 64)), (km1, le), (km1, lo_)])
            + acc(qf[1], [(ip, d64[2]), (ip, one64), (hp, le), (hp, lo_)])
            + acc(qf[2], [(ip, one64), (hp, le), (hp, lo_), (im, d64[0]), (im, d64[1])]))
        cp(rf, V("qr0", 0, 192), True)
        k2 = KS[t + 1]
        mms(acc(nfc, [(ones, sub(cf, 64, 1)), (ip, sub(c84, 0, 1)), (im, sub(r64, 64, 1))])
            + (acc(nfa, [(ones, sub(cf, k2 - 1, 1)), (ip, sub(c84, 0, 1)), (row0, sub(r64, k2, 1))]) if k2 else []))
        w2 = aff(S("w2", F, 2 * SW), cq, 1.0, BIG)
        kbs = S("kbs", F, 8)
        for j in range(8):
            act(S("jk%d" % j, B), V("qd", SW * (j // 4), 64), AF.Sign, -1.0, sub(jh, j % 4, 1), acc=sub(kbs, j, 1))
        ko = to16(S("ko", U, 8), kbs, 0.5, 32.0)
        msk = S("msk", B, 128)
        for j in range(2):
            gtt(sub(msk, 64 * j, 64), sub(w2, SW * j, SW), sub(ko, 4 * j, 4), i64, OP.is_equal)
        ql = V("qd", 400, 8)
        mms([(ql, f8i, kbs, True, False)])
        wrap(ql, bim, msk, 8, first=False)
        lno = to16(S("lno", U, 8), ql, 1.0, 512.0)
        hvm = gtt(S("hvm", HF, 128), sub(rt_, 0, SW), ko, msk, mul)
        vr = V("qd", 256, 128)
        mms([(vr, ip, svc, True, False)] + acc(sub(vr, 0, 64), [(sub(b1, 28, 128), sub(hvm, 0, 64))], False, False)
            + acc(sub(vr, 64, 64), [(sub(b1, a, 128), sub(hvm, 64, 64)) for a in (12, 140)], False))
        sv = aff(S("sv%d" % (t + 1), F, 128), vr, BETA, inb)
        av = ws - 128
        send([(sub(sv, 0, 64), sub(zz, av, 64), to1), (sub(sv, 64, 64), sub(zz, av + 64, 64), to2)], "rv%d" % t, [sub(zz, av, 128)])
        leave(t, 0, cn, aff(S("sd%d" % t, F, 128), cs, 0.5, 0.0, lno))
    up = []
    for o in ops:
        for d in [d for d, hard in o["deps"].items() if not hard and len(o["alts"]) == 1 and list(ops[d]["alts"]) == list(o["alts"])]:
            del o["deps"][d]
        near = list(o["deps"]) + o["after"]
        far = 0
        for d in near:
            far |= up[d]
        o["all"] = [d for d in near if not far >> d & 1]
        up.append(far | sum(1 << d for d in set(near) if not far >> d & 1))
        o.setdefault("remote", False)
        o.setdefault("pipe", 0.1 if o["remote"] else None)
    return ops


BEST = []


def schedule(ops, others):
    n = len(ops)
    deps = [o["all"] for o in ops]
    pipe = [o["pipe"] for o in ops]
    pipes = [[o["pipe"] for o in oth] for oth in others]
    cost = [[dict([(None, 0.0)] + [(e, a[0]) for e, a in o["alts"].items()]) for o in oth] for oth in others]
    late = [[o["lat"] + (0.0 if o["pipe"] is None else w[5] if o["remote"] else w[6]) for o in oth] for oth, w in zip(others, CASES)]

    succ = [[s for s in range(n) if k in deps[s]] for k in range(n)]
    flex = [k for k, o in enumerate(ops) if len(o["alts"]) > 1 and "V" in o["alts"]]

    QS = list("VAPGS") + ["pipe", None]

    def length(seq, eng, i=0, old=None, room=1e9, j=10 ** 9, touched=()):
        before = {}
        for k in seq[:i]:
            before[eng[k]] = k
            if pipes[0][k] is not None:
                before["pipe"] = k
        new, total, way = [], 0.0, []
        for c, w in enumerate(CASES):
            fin, why, end, pend = [x[:] for x in old[c][:4]] if old else ([0.0] * n, [None] * n, [0.0] * n, [0.0] * n)
            last, hop, own, co, la, pipe = dict(before), w[3], w[4], cost[c], late[c], pipes[c]
            moved, stale = dict.fromkeys(QS, True), set(touched)
            for at, k in enumerate(seq[i:], i):
                e = eng[k]
                p = pipe[k]
                if at > j and not moved[e] and k not in stale and (p is None or not moved["pipe"]):
                    last[e] = k
                    if p is not None:
                        last["pipe"] = k
                    continue
                y = last.get(e) if e else None
                t = 0.0 if y is None else end[y]
                for d in deps[k]:
                    u = fin[d] + (own if eng[d] == e else hop)
                    if u > t:
                        t = u
                        y = d
                t += co[k][e]
                moved[e] = at <= j or t != end[k]
                end[k] = t
                last[e] = k
                if p is not None:
                    d = last.get("pipe")
                    if d is not None and pend[d] > t:
                        t = pend[d]
                        y = d
                    moved["pipe"] = at <= j or t + p != pend[k]
                    pend[k] = t + p
                    last["pipe"] = k
                t += la[k]
                if t != fin[k]:
                    fin[k] = t
                    stale.update(succ[k])
                why[k] = y
            m = max(fin)
            part = (m + MEAN * sum(fin) / n) / w[7]
            total += part
            if old:
                room -= part - old[c][4]
                if room < -EARLY * (len(CASES) - 1 - c) - 1.0 * (c == len(CASES) - 1):
                    return 1e9, None, None
            k = fin.index(m)
            while why[k] is not None:
                if why[k] not in deps[k]:
                    way.append((why[k], k))
                k = why[k]
            new.append((fin, why, end, pend, part))
        return total / len(CASES) + LAM * sum(cost[0][k]["V"] for k in flex if eng[k] == "V"), way, new
    if not BEST:
        pin = {k: "S" if pipe[k] is not None else "A" for k, o in enumerate(ops) if len(o["alts"]) > 1 and o["alts"].get("A", [PIN])[0] < PIN}
        seq, eng = min((listing(ops, s, pin) for s in range(TRIES)), key=lambda r: length(*r)[0])
        now, way, old = length(seq, eng)
        best, keep = now, (seq, eng, old)
        x = SEED
        for it in range(CLIMB):
            x = (x * 1103515245 + 12345) % 2 ** 31
            a, b = way[(x >> 8) % len(way)]
            if (x >> 23) % 8 < ANY:
                k = (x >> 8) % n
                y = old[(x >> 5) % len(CASES)][1][k]
                if y is None or y in deps[k]:
                    continue
                a, b = y, k
            u = (x >> 20) % 8
            s2, e2 = seq, eng
            if (x >> 26) % 8 < FAR:
                k = (a, b, (x >> 6) % n)[(x >> 4) % 3]
                j = seq.index(k)
                s2 = seq[:j] + seq[j + 1:]
                lo = max([s2.index(d) + 1 for d in deps[k]] or [0])
                hi = min([s2.index(d) for d in succ[k]] or [n - 1])
                x = (x * 1103515245 + 12345) % 2 ** 31
                i = lo + (x >> 8) % (hi - lo + 1)
                s2.insert(i, k)
                i, j = min(i, j), max(i, j)
                if len(ops[k]["alts"]) > 1 and (x >> 5) % 3 == 0:
                    e2 = list(eng)
                    e2[k] = [e for e in ops[k]["alts"] if e != eng[k]][0]
            elif u < 2:
                k = a if u else b
                if len(ops[k]["alts"]) < 2:
                    continue
                e2 = list(eng)
                e2[k] = [e for e in ops[k]["alts"] if e != eng[k]][0]
                i = j = seq.index(k)
            else:
                i, j = seq.index(a), seq.index(b)
                if u == 7:
                    i = max(0, i - 1 - (x >> 4) % 12)
                elif u == 6:
                    j = min(len(seq) - 1, j + 1 + (x >> 4) % 12)
                part = seq[i:j + 1]
                if u % 2:
                    need = set(deps[b])
                    go = {b}
                    for k in part[::-1]:
                        if k in need:
                            go.add(k)
                            need.update(deps[k])
                    if a in go:
                        continue
                    part = [k for k in part if k in go] + [k for k in part if k not in go]
                else:
                    go = {a}
                    for k in part:
                        if not go.isdisjoint(deps[k]):
                            go.add(k)
                    if b in go:
                        continue
                    part = [k for k in part if k not in go] + [k for k in part if k in go]
                s2 = seq[:i] + part + seq[j + 1:]
            x = (x * 1103515245 + 12345) % 2 ** 31
            room = HEAT * (1 - it / CLIMB) * (x / 2.0 ** 31) ** 3
            m, w2, new = length(s2, e2, i, old, len(CASES) * room + (LAM if e2 is not eng else 0.0), j, succ[k] if e2 is not eng else ())
            if m <= now + room:
                now, seq, eng, way, old = m, s2, e2, w2, new
                if m < best:
                    best, keep = m, (seq, eng, old)
        BEST.append(keep + (best,))
    seq, eng = BEST[0][:2]
    for o, e in zip(ops, eng):
        o["eng"] = e
    return {e: [k for k in seq if eng[k] == e] for e in "VAPGS"}


def improve(ops, others, seq, eng):
    n = len(ops)
    deps = [o["all"] for o in ops]
    succ = [[] for _ in range(n)]
    for k in range(n):
        for d in deps[k]:
            succ[d].append(k)
    pipes = [[o["pipe"] for o in oth] for oth in others]
    cost = [[dict([(None, 0.0)] + [(e, a[0]) for e, a in o["alts"].items()]) for o in oth] for oth in others]
    late = [[o["lat"] + (0.0 if o["pipe"] is None else w[5] if o["remote"] else w[6]) for o in oth] for oth, w in zip(others, CASES)]
    other = [dict(zip(o["alts"], list(o["alts"])[::-1])) if len(o["alts"]) > 1 else None for o in ops]
    fee = [LAM * cost[0][k]["V"] if other[k] and "V" in other[k] else 0.0 for k in range(n)]
    QS = list("VAPGS") + ["pipe"]

    def rest(seq, eng, old, a, b):
        behind, res = set(seq[b:]), []
        for c, w in enumerate(CASES):
            hop, own, co, la, pipe = w[3], w[4], cost[c], late[c], pipes[c]
            q, nxt = [0.0] * n, dict.fromkeys(QS + [None], 0.0)
            for k in reversed(seq[b:]):
                e = eng[k]
                t = la[k] + max([q[s] + (own if eng[s] == e else hop) for s in succ[k]] or [0.0])
                if pipe[k] is not None:
                    t = nxt["pipe"] = max(t, pipe[k] + nxt["pipe"])
                q[k] = co[k][e] + (max(t, nxt[e]) if e else t)
                nxt[e] = q[k]

            def out(k, e):
                return max([q[s] + (own if eng[s] == e else hop) for s in succ[k] if s in behind] or [0.0])
            outs = [(k, dict((e, out(k, e)) for e in co[k])) for k in seq[a:b] if not succ[k] or not behind.isdisjoint(succ[k])]
            res.append((outs, nxt, max([old[c][0][k] + out(k, eng[k]) for k in seq[:a]] or [0.0])))
        return res

    def length(seq, eng, i, b, old, far, room=1e9):
        before = dict.fromkeys(QS + [None], n)
        for k in seq[:i]:
            before[eng[k]] = k
            if pipes[0][k] is not None:
                before["pipe"] = k
        new, total, way, part = [], 0.0, [], seq[i:b]
        for c, w in enumerate(CASES):
            fin, why, end, pend = [x[:] for x in old[c][:4]]
            last, hop, own, co, la, pipe = dict(before), w[3], w[4], cost[c], late[c], pipes[c]
            for k in part:
                e = eng[k]
                y = last[e] if e else n
                t = end[y]
                for d in deps[k]:
                    u = fin[d] + (own if eng[d] == e else hop)
                    if u > t:
                        t = u
                        y = d
                t += co[k][e]
                end[k] = t
                last[e] = k
                p = pipe[k]
                if p is not None:
                    d = last["pipe"]
                    if pend[d] > t:
                        t = pend[d]
                        y = d
                    pend[k] = t + p
                    last["pipe"] = k
                fin[k] = t + la[k]
                why[k] = y
            outs, nxt, m = far[c]
            y = n
            for k, o in outs:
                t = fin[k] + o[eng[k]]
                if t > m:
                    m, y = t, k
            for e in QS:
                k = last[e]
                t = (pend if e == "pipe" else end)[k] + nxt[e]
                if t > m:
                    m, y = t, k
            v = (m + MEAN * sum(fin) / n) / w[7]
            total += v
            room -= v - old[c][4]
            if room < -EARLY * (len(CASES) - 1 - c) - 1e-9:
                return 1e9, None, None
            while y < n:
                if why[y] < n and why[y] not in deps[y]:
                    way.append((why[y], y))
                y = why[y]
            new.append((fin, why, end, pend, v, m))
        return total / len(CASES), way, new
    none = [([], dict.fromkeys(QS, 0.0), 0.0)] * len(CASES)
    zero = [([0.0] * (n + 1), [n] * (n + 1), [0.0] * (n + 1), [0.0] * (n + 1), 1e9)] * len(CASES)
    starts = [a for _ in range(SWEEPS) for a in list(range(0, n - SPAN, SPAN // 2)) + [n - SPAN]]
    x, keep = SEED, None
    for turn, a0 in enumerate(starts):
        b0 = a0 + SPAN
        old = length(seq, eng, 0, n, zero, none)[2]
        now = sum((max(o[0]) + MEAN * sum(o[0]) / n) / w[7] for o, w in zip(old, CASES)) / len(CASES) + sum(f for f, e in zip(fee, eng) if e == "V")
        if keep is None or now < keep[3]:
            keep = (seq, eng, old, now)
        order = sorted(range(n), key=lambda j: (old[0][2][seq[j]] - cost[0][seq[j]][eng[seq[j]]], j))
        if turn % (len(starts) // SWEEPS) == 0:
            s2 = [seq[j] for j in order]
            o2 = length(s2, eng, 0, n, zero, none)[2]
            if sum(max(o[0]) for o in o2) <= sum(max(o[0]) for o in old) + 0.2:
                seq, old = s2, o2
        far = rest(seq, eng, old, a0, b0)
        now, way, old = length(seq, eng, a0, b0, old, far)
        inside = set(seq[a0:b0])
        way = [p for p in way if p[0] in inside]
        for it in range(CLIMB // len(starts)):
            x = (x * 1103515245 + 12345) % 2 ** 31
            if (x >> 23) % 8 < ANY or not way:
                b = seq[a0 + (x >> 8) % SPAN]
                a = old[(x >> 5) % len(CASES)][1][b]
                if a not in inside or a in deps[b]:
                    continue
            else:
                a, b = way[(x >> 8) % len(way)]
            u = (x >> 20) % 8
            s2, e2, flip = seq, eng, None
            if (x >> 26) % 8 < FAR:
                k = (a, b, seq[a0 + (x >> 6) % SPAN])[(x >> 4) % 3]
                j = seq.index(k, a0)
                s2 = seq[:j] + seq[j + 1:]
                lo = max([s2.index(d, a0) + 1 for d in deps[k] if d in inside] or [a0])
                hi = min([s2.index(d, a0) for d in succ[k] if d in inside] or [b0 - 1])
                x = (x * 1103515245 + 12345) % 2 ** 31
                i = lo + (x >> 8) % (hi - lo + 1)
                s2.insert(i, k)
                i = min(i, j)
                if other[k] and (x >> 5) % 3 == 0:
                    flip = k
            elif u < 2:
                flip = a if u else b
                if not other[flip]:
                    continue
                i = seq.index(flip, a0)
            else:
                i, j = seq.index(a, a0), seq.index(b, a0)
                if u == 7:
                    i = max(a0, i - 1 - (x >> 4) % 12)
                elif u == 6:
                    j = min(b0 - 1, j + 1 + (x >> 4) % 12)
                part = seq[i:j + 1]
                if u % 2:
                    need = set(deps[b])
                    go = {b}
                    for k in part[::-1]:
                        if k in need:
                            go.add(k)
                            need.update(deps[k])
                    if a in go:
                        continue
                    part = [k for k in part if k in go] + [k for k in part if k not in go]
                else:
                    go = {a}
                    for k in part:
                        if not go.isdisjoint(deps[k]):
                            go.add(k)
                    if b in go:
                        continue
                    part = [k for k in part if k not in go] + [k for k in part if k in go]
                s2 = seq[:i] + part + seq[j + 1:]
            extra = 0.0
            if flip is not None:
                e2 = list(eng)
                e2[flip] = other[flip][eng[flip]]
                extra = fee[flip] if e2[flip] == "V" else -fee[flip]
            x = (x * 1103515245 + 12345) % 2 ** 31
            room = HEAT * (1 - (turn + 1.0) / len(starts)) * (x / 2.0 ** 31) ** 3 - extra
            m, w2, new = length(s2, e2, i, b0, old, far, len(CASES) * room)
            if m <= now + room:
                now, seq, eng, old = m, s2, e2, new
                way = [p for p in w2 if p[0] in inside]
    old = length(seq, eng, 0, n, zero, none)[2]
    now = sum((max(o[0]) + MEAN * sum(o[0]) / n) / w[7] for o, w in zip(old, CASES)) / len(CASES) + sum(f for f, e in zip(fee, eng) if e == "V")
    return keep if keep[3] < now else (seq, eng, old, now)


def schedule2(ops, others):
    if not BEST:
        pin = {k: "S" if o["pipe"] is not None else "A" for k, o in enumerate(ops) if len(o["alts"]) > 1 and o["alts"].get("A", [PIN])[0] < PIN}
        BEST.append(improve(ops, others, *listing(ops, 0, pin)))
    seq, eng = BEST[0][:2]
    for o, e in zip(ops, eng):
        o["eng"] = e
    return {e: [k for k in seq if eng[k] == e] for e in "VAPGS"}


def listing(ops, seed, pin):
    n = len(ops)
    x = [seed * 7919 + 1]

    def rnd():
        x[0] = (x[0] * 1103515245 + 12345) % 2 ** 31
        return x[0] / 2.0 ** 31
    bias = BIAS * (0.5 + 2 * rnd())
    noise = 0.6 * rnd()
    look, gap = 0.6 * rnd(), 0.5 + 3 * rnd()
    succ = [[] for _ in range(n)]
    for k, o in enumerate(ops):
        for d in o["all"]:
            succ[d].append(k)
    pr = [0.0] * n
    for k in range(n - 1, -1, -1):
        o = ops[k]
        pr[k] = min([a[0] for a in o["alts"].values()] or [0.0]) * (1 + noise * (rnd() - 0.5)) + o["lat"] + HOP + max([pr[s] for s in succ[k]] or [0.0])
    pr = [o.get("first", pr[k]) for k, o in enumerate(ops)]
    engs = [[pin[k]] if k in pin else list(o["alts"]) for k, o in enumerate(ops)]
    left = [len(o["all"]) for o in ops]
    ready, seq, eng = [0.0] * n, [], [None] * n
    free = {e: 0.0 for e in list("VAPGS") + ["pipe"]}
    cand = [k for k in range(n) if left[k] == 0]

    def done(k, t):
        seq.append(k)
        cand.remove(k)
        for s in succ[k]:
            ready[s] = max(ready[s], t + HOP)
            left[s] -= 1
            if left[s] == 0:
                cand.append(s)
    while cand:
        z = [k for k in cand if not ops[k]["alts"]]
        if z:
            done(z[0], ready[z[0]] + ops[z[0]]["lat"])
            continue
        t, e = min((max(free[e], ready[k]), e) for k in cand for e in engs[k])
        mine = [k for k in cand if e in engs[k] and ready[k] <= t + 0.05]
        k = max(mine, key=lambda j: pr[j])
        soon = [j for j in cand if e in engs[j] and ready[j] <= t + look * ops[k]["alts"][e][0] and pr[j] > pr[k] + gap]
        if soon:
            k = max(soon, key=lambda j: pr[j])
        e = min(engs[k], key=lambda x: max(free[x], ready[k]) + ops[k]["alts"][x][0] * (1 + bias if x == "V" else 1) + (bias if x == "V" else 0.0))
        t = max(free[e], ready[k])
        free[e] = t + ops[k]["alts"][e][0]
        eng[k] = e
        t = free[e]
        if ops[k]["pipe"] is not None:
            t = max(t, free["pipe"])
            free["pipe"] = t + ops[k]["pipe"]
        done(k, t + ops[k]["lat"])
    return seq, eng


def plan(T, topo, core):
    others = [] if BEST else [build(T, topo, core, *(w[:3] + w[8:])) for w in CASES]
    ops = build(T, topo, core, FAC, GA, SC)
    for o in ops:
        o["lat"] += 1.5 if o["remote"] else 0.5 if o["pipe"] is not None else 0.0
    return ops, schedule2(ops, others)


def rank_program(g, core, T, topo):
    if T.rank_of(core) is None:
        return
    ops, order = plan(T, topo, core)
    qs = {"V": g.vector, "A": g.scalar, "P": g.tensor, "G": g, "S": g.sync}
    known, done = dict((e, 0) for e in order), {}
    for k in BEST[0][0]:
        o = ops[k]
        e = o["eng"]
        o["wait"] = []
        if e is None:
            done[k] = 1 << k
            continue
        for d in sorted(o["deps"], reverse=True, key=BEST[0][0].index):
            if (o["deps"][d] or ops[d]["eng"] != e) and not known[e] >> d & 1:
                o["wait"].append(d)
                known[e] |= done[d]
        done[k] = known[e] | 1 << k
        if o["sem"] is None:
            done[k] |= done.get(e, 0)
            done[e] = done[k]
    needed = set(d for o in ops for d in o["wait"])
    cnt = {}
    for e in order:
        for k in order[e]:
            if ops[k]["sem"] is None and k in needed:
                cnt[e] = cnt.get(e, 0) + 1
                ops[k]["sem"], ops[k]["one"] = ("e" + e, cnt[e]), True
    top = {}
    for e in order:
        seen = {}
        for k in order[e]:
            o = ops[k]
            want = {}
            for d in o["wait"]:
                s, v = ops[d]["sem"]
                want[s] = max(want.get(s, 0), v)
            for s, v in sorted(want.items()):
                if seen.get(s, 0) < v:
                    qs[e].wait_ge(T.sem[s], v)
                    seen[s] = v
                    top[s] = max(top.get(s, 0), v)
            r = o["alts"][e][1](qs[e])
            if o.get("one"):
                r.then_inc(T.sem[o["sem"][0]], 1)
            elif o["sem"] is not None and not o["remote"]:
                r.then_inc(T.sem[o["sem"][0]], o["sem"][1])
    for o in ops:
        if o["sem"] is not None and not o.get("one") and top.get(o["sem"][0], 0) < o["sem"][1]:
            g.sync.wait_ge(T.sem[o["sem"][0]], o["sem"][1])
